import numpy as np
import ml_dtypes


def mxq(x, axis, fmt="e4m3"):
    dtype, down = {"e4m3": (ml_dtypes.float8_e4m3fn, 7), "e5m2": (ml_dtypes.float8_e5m2, 14)}[fmt]
    v = np.moveaxis(np.asarray(x, np.float32).astype(ml_dtypes.bfloat16).astype(np.float64), axis, -1)
    blocks = v.reshape(v.shape[:-1] + (-1, 32))
    amax = np.abs(blocks).max(-1, keepdims=True)
    byte = np.maximum(np.where(amax > 0, np.frexp(amax)[1] - 1 + 127, 0) - down, 1)
    scale = np.exp2(byte - 127.0)
    codes = (blocks / scale).astype(np.float32).astype(dtype).astype(np.float64)
    return np.moveaxis((codes * scale).reshape(v.shape), -1, axis)


WIDE = False


def mx_kscale(k):
    if not WIDE:
        return np.ones(k)
    levels = np.array([18, -18])
    if k % 512:
        return np.exp2(np.random.permutation(np.resize(levels, k // 32))).repeat(32)
    a = np.empty((k // 512, 16))
    for p in range(k // 512):
        a[p, :8] = np.random.permutation(np.resize(levels, 8))
        for g in range(8):
            far = levels[np.abs(levels - a[p, g]) >= 10]
            a[p, g + 8] = far[np.random.randint(len(far))]
    return np.exp2(a.ravel()).repeat(32)


def f64(x):
    return np.asarray(x).astype(np.float64)


def striped(idx):
    return np.tile(np.asarray(idx).reshape(-1, 16).T, (8, 1)).astype(np.uint16)


def unstriped(offs):
    return offs[:16].T.reshape(-1).astype(np.int64)


B, N, T, D, DV = 2, 512, 2048, 512, 512


def setup_inputs():
    n = np.random.standard_normal
    idx = np.random.permutation(T)[:B * N]
    u = np.ones(T)
    u[idx] = mx_kscale(B * N)
    v = mx_kscale(DV)[:, None]
    coarse = lambda x: x.astype(np.float32).astype(ml_dtypes.bfloat16).astype(np.float64)
    r = np.random.randint(8, 33, T) / 16.0 * u
    return {
        "xT": (n((D, T)) / np.sqrt(N) / u).astype(np.float32),
        "dyT": (coarse(n((DV, T))) * v).astype(np.float32),
        "hT": (np.random.randint(1, 32, (DV, T)) / 32.0).astype(np.float32),
        "ts": np.tile(r, (128, 1)).astype(np.float32),
        "wm": (n((B, DV, D)) / np.sqrt(DV) / v).astype(np.float32),
        "offs": striped(idx),
    }


def reference(xT, dyT, hT, ts, wm, offs):
    idx = unstriped(offs)
    pick = lambda x: x[:, idx].reshape(x.shape[0], B, N).transpose(1, 0, 2)
    h = pick(f64(hT))
    dz = pick(f64(ts))[:, :1, :] * pick(f64(dyT)) * h * (1.0 - h)
    gw = mxq(pick(f64(xT)), 2, "e4m3") @ mxq(dz, 2, "e5m2").transpose(0, 2, 1)
    dx = mxq(f64(wm), 1, "e4m3").transpose(0, 2, 1) @ mxq(dz, 1, "e5m2")
    gx = np.zeros((D, T))
    gx[:, idx] = dx.transpose(1, 0, 2).reshape(D, B * N)
    return gw, gx

@@ -1,0 +1,284 @@
+from contextlib import ExitStack
+
+import concourse.mybir as mybir
+from concourse.masks import make_identity
+
+B, N, T, D, DV = 2, 512, 2048, 512, 512
+FLOPS = 2 * 2 * B * N * D * DV
+
+F32 = mybir.dt.float32
+BF16 = mybir.dt.bfloat16
+U32 = mybir.dt.uint32
+U16 = mybir.dt.uint16
+U8 = mybir.dt.uint8
+E4M3 = mybir.dt.float8_e4m3fn_x4
+E5M2 = mybir.dt.float8_e5m2_x4
+MULT = mybir.AluOpType.mult
+ADD = mybir.AluOpType.add
+COPY = mybir.ActivationFunctionType.Copy
+IDENTITY = mybir.ActivationFunctionType.Identity
+
+P = 128
+PACK = 4
+LIST_COLS = N // 16
+TS_ROW = 96
+
+
+def tile_attend_gex_sig_wx_kernel(tc, xT, dyT, hT, ts, wm, offs, out_0, out_1):
+    nc = tc.nc
+    with ExitStack() as ctx:
+        lists = ctx.enter_context(tc.tile_pool(name="lists", bufs=1))
+        keep = ctx.enter_context(tc.tile_pool(name="keep", bufs=1))
+        ring = ctx.enter_context(tc.tile_pool(name="ring", bufs=2))
+        psum = ctx.enter_context(tc.psum_pool(name="psum", bufs=2))
+
+        offsets = lists.tile([P, B * LIST_COLS], U16, name="offsets")
+        nc.sync.dma_start(offsets[:], offs)
+
+        def expert_list(b):
+            return offsets[:, b * LIST_COLS : (b + 1) * LIST_COLS]
+
+        ts_pool = keep.tile([P, T], F32, name="ts_pool", tag="ts_then_wm")
+        nc.sync.dma_start(ts_pool[TS_ROW:, :], ts[TS_ROW:, :])
+        nc.vector.memset(ts_pool[:TS_ROW, :], 0.0)
+
+        ident = keep.tile([P, P], F32, name="ident")
+        make_identity(nc, ident[:])
+
+        windows = [keep.tile([P, T], F32, name="window0")]
+        nc.vector.memset(windows[0][:], 0.0)
+
+        def load(rows, shape, name, tag):
+            raw = keep.tile(shape, F32, name=name, tag=tag)
+            nc.sync.dma_start(raw[:], rows)
+            return raw
+
+        h_rows = hT.rearrange("(m j) c -> j m c", j=PACK)
+        dy_rows = dyT.rearrange("(m j) c -> j m c", j=PACK)
+        wm_rows = [wm[b].rearrange("(m j) d -> m j d", j=PACK) for b in range(B)]
+        x_rows = xT.rearrange("(k m) c -> k m c", m=P)
+        h_pool = [load(h_rows[j], [P, T], "h_pool%d" % j, "h%d" % j) for j in range(PACK)]
+        dy_pool = [load(dy_rows[j], [P, T], "dy_pool%d" % j, "dy%d" % j) for j in range(2)]
+        x_pool = [load(x_rows[0], [P, T], "x_pool0", "x0")]
+        dy_pool += [load(dy_rows[j], [P, T], "dy_pool%d" % j, "dy%d" % j) for j in range(2, PACK)]
+
+        def turn(bank, words, b):
+            for t in range(PACK):
+                nc.tensor.transpose(bank[:, t, :], words[:, b * N + t : (b + 1) * N : PACK], ident[:])
+
+        ts_g = keep.tile([P, B * N], F32, name="ts_g")
+        nc.vector.tensor_copy(ts_g[:], ts_pool[:].indirect(offsets[:]))
+        ts_pos = [keep.tile([P, PACK], F32, name="ts_pos%d" % b, tag="pos%d" % b) for b in range(B)]
+        ts_neg = [keep.tile([P, PACK], F32, name="ts_neg%d" % b, tag="neg%d" % b) for b in range(B)]
+        for b in range(B):
+            bank = psum.tile([P, PACK, P], F32, name="ts_bank", tag="early")
+            turn(bank, ts_g, b)
+            nc.scalar.activation(ts_pos[b][:], bank[:, :, TS_ROW], COPY)
+            nc.scalar.activation(ts_neg[b][:], bank[:, :, TS_ROW], COPY, scale=-1.0)
+
+        h_g = [keep.tile([P, B * N], F32, name="h_g%d" % j, align_bytes=64) for j in range(PACK)]
+        rest = {}
+        for j in range(PACK):
+            nc.vector.tensor_copy(h_g[j][:], h_pool[j][:].indirect(offsets[:]))
+            for b in range(B):
+                bank = psum.tile([P, PACK, P], F32, name="h_bank", tag="early")
+                turn(bank, h_g[j], b)
+                rest[b, j] = keep.tile([P, PACK, P], F32, name="rest%d_%d" % (b, j), tag="rest%d_%d" % (b, j), align_bytes=64)
+                for t in range(PACK):
+                    nc.scalar.activation(
+                        rest[b, j][:, t, :], bank[:, t, :], IDENTITY,
+                        bias=ts_pos[b][:, t : t + 1], scale=ts_neg[b][:, t : t + 1],
+                    )
+
+        for k, tag in ((1, "pos0"), (2, "neg0"), (3, "pos1")):
+            windows.append(keep.tile([P, T], F32, name="window%d" % k, tag=tag))
+            nc.gpsimd.memset(windows[k][:], 0.0)
+
+        wm_raw = [load(wm_rows[0], [P, PACK, D], "wm_raw0", "ts_then_wm")]
+        x_pool.append(load(x_rows[1], [P, T], "x_pool1", "h0"))
+        wm_raw.append(load(wm_rows[1], [P, PACK, D], "wm_raw1", "h1"))
+        x_pool.append(load(x_rows[2], [P, T], "x_pool2", "h2"))
+        x_pool.append(load(x_rows[3], [P, T], "x_pool3", "h3"))
+
+        def mx_tiles(width, name, tag):
+            codes = keep.tile([P, width], U32, name=name + "_codes", tag=tag, align_bytes=64)
+            scales = keep.tile([P, width], U8, name=name + "_scales", align_bytes=64)
+            return codes, scales
+
+        def quantize(src, width, fmt, name, tag):
+            codes, scales = mx_tiles(width, name, tag)
+            nc.vector.quantize_mx(out=codes[:].bitcast(fmt), scales=scales[:], in_=src)
+            return codes, scales
+
+        def product(acc, left, e, right):
+            nc.tensor.matmul_mx(
+                out=acc[:],
+                lhsT=left[0][:, e * P : (e + 1) * P].bitcast(E4M3),
+                lhsT_scale=left[1][:, e * P : (e + 1) * P],
+                rhs=right[0][:].bitcast(E5M2),
+                rhs_scale=right[1][:],
+                start=True,
+                stop=True,
+            )
+
+        dyh_tiles = [keep.tile([P, B * N], F32, name="dyh%d" % i) for i in range(2)]
+        dyh = {(b, j): dyh_tiles[j][:, b * N : (b + 1) * N] for b in range(B) for j in range(2)}
+        dyh[0, 2], dyh[0, 3], dyh[1, 3] = dyh[0, 0], dyh[1, 0], dyh[0, 1]
+        dyh[1, 2] = h_g[3][:, :N]
+
+        def quarter(j, i):
+            return h_g[j][:, i * 2 * P : (i + 1) * 2 * P].bitcast(BF16)
+
+        dz = {(b, j): quarter(j + 1, b) for b in range(B) for j in range(2)}
+        for b in range(B):
+            for j in range(2, PACK):
+                dz[b, j] = quarter(0, 2 * b + j - 2)
+
+        def gather_dy_both(j):
+            nc.vector.tensor_tensor(dyh_tiles[j][:], dy_pool[j][:].indirect(offsets[:]), h_g[j][:], MULT)
+
+        def gather_dy(b, j):
+            nc.vector.tensor_tensor(dyh[b, j], dy_pool[j][:].indirect(expert_list(b)), h_g[j][:, b * N : (b + 1) * N], MULT)
+
+        def make_dz(b, j):
+            bank = psum.tile([P, PACK, P], F32, name="dyh_bank", tag="wide", bufs=PACK)
+            turn(bank, dyh[b, j], 0)
+            nc.vector.tensor_tensor(
+                dz[b, j].rearrange("p (a e t) -> p a t e", e=2, t=PACK),
+                bank[:].rearrange("p t (a e) -> p a t e", e=2),
+                rest[b, j][:].rearrange("p t (a e) -> p a t e", e=2),
+                MULT,
+            )
+
+        def dz_by_slots(b):
+            codes, scales = mx_tiles(DV, "dzs%d" % b, "rest1_%d" % (2 + b))
+            for j in range(PACK):
+                cols = slice(j * P, (j + 1) * P)
+                nc.vector.quantize_mx(out=codes[:, cols].bitcast(E5M2), scales=scales[:, cols], in_=dz[b, j])
+            return codes, scales
+
+        def dz_by_features(b, tag):
+            dz_feat = ring.tile([P, 2, 2 * P, PACK], BF16, name="dz_feat", align_bytes=64)
+            for u in range(2):
+                bank = psum.tile([P, PACK, P], F32, name="feat_bank", tag="late")
+                for j in range(PACK):
+                    nc.tensor.transpose(bank[:, j, :], dz[b, j].bitcast(F32)[:, u::2], ident[:])
+                nc.scalar.copy(
+                    dz_feat[:, u, :, :],
+                    bank[:].rearrange("p j s -> p (j s)").bitcast(BF16).rearrange("p (j q) -> p q j", j=PACK),
+                )
+            return quantize(dz_feat[:].rearrange("p u q j -> p (u q j)"), N, E5M2, "dzf%d" % b, tag)
+
+        def wm_half(b, half):
+            wm_bf = ring.tile([P, 2 * P * PACK], BF16, name="wm_bf", align_bytes=64)
+            dst = wm_bf[:].rearrange("p (a e j) -> p a j e", e=2, j=PACK)
+            src = wm_raw[b][:, :, half * 2 * P : (half + 1) * 2 * P].rearrange("p j (a e) -> p a j e", e=2)
+            if b == 0:
+                nc.scalar.copy(dst, src)
+            else:
+                nc.gpsimd.tensor_scalar(dst, src, 1.0, 0.0, MULT, ADD)
+            return quantize(wm_bf[:], 2 * P, E4M3, "wm%d_%d" % (b, half), "wm%d_%d" % (b, half))
+
+        def dx_block(wm_mx, k, dz_mx, acc, tag):
+            staged = keep.tile([P, N], F32, name="dx_staged", tag=tag, align_bytes=64)
+            product(acc, wm_mx[k // 2], k % 2, dz_mx)
+            nc.scalar.copy(
+                staged[:].rearrange("p (s u e) -> p s u e", u=2, e=2),
+                acc[:].rearrange("p (u s e) -> p s u e", u=2, e=2),
+            )
+            return staged
+
+        def scatter(b, k, staged):
+            nc.vector.tensor_copy(windows[k][:].indirect(expert_list(b)), staged[:])
+            if b == B - 1:
+                nc.sync.dma_start(out_1[k * P : (k + 1) * P, :], windows[k][:])
+
+        x_bf, x_g = {}, {}
+
+        def x_cast(k):
+            x_bf[k] = keep.tile([P, T], BF16, name="x_bf", tag="x_bf%d" % (k % 2), align_bytes=64)
+            nc.scalar.activation(x_bf[k][:], x_pool[k][:], COPY)
+
+        def x_gather(k):
+            x_g[k] = keep.tile([P, 2, B * P, 2], BF16, name="x_g", tag="x_g%d" % k, align_bytes=64)
+            nc.scalar.activation(x_g[k][:].rearrange("p u s e -> p s u e"), x_bf[k][:].indirect(offsets[:]), COPY)
+
+        def x_quantize(pair, b):
+            bank = psum.tile([P, 2, 2, P], F32, name="x_bank", tag="early")
+            for e in range(2):
+                words = x_g[2 * pair + e][:].rearrange("p u s e -> p (u s e)").bitcast(F32)
+                for u in range(2):
+                    first = (u * B + b) * P
+                    nc.tensor.transpose(bank[:, e, u, :], words[:, first : first + P], ident[:])
+            x_slot = ring.tile([P, 2 * P * PACK], BF16, name="x_slot", align_bytes=64)
+            nc.scalar.copy(
+                x_slot[:].bitcast(F32).rearrange("p (e m u) -> p e m u", e=2, u=2),
+                bank[:].rearrange("p e u m -> p e m u"),
+            )
+            return quantize(x_slot[:], 2 * P, E4M3, "x%d_%d" % (pair, b), "x%d_%d" % (pair, b))
+
+        def gw_block(b, k, x_mx, dz_mx):
+            acc = psum.tile([P, DV], F32, name="gw_acc", tag="wide", bufs=PACK)
+            product(acc, x_mx, k % 2, dz_mx)
+            gw = ring.tile([P, DV], F32, name="gw", bufs=PACK)
+            nc.scalar.copy(gw[:].rearrange("p (m j) -> p m j", j=PACK), acc[:].rearrange("p (j m) -> p m j", j=PACK))
+            nc.sync.dma_start(out_0[b, k * P : (k + 1) * P, :], gw[:])
+
+        def late_bank():
+            return psum.tile([P, N], F32, name="dx_acc", tag="late")
+
+        def wide_bank():
+            return psum.tile([P, N], F32, name="dx_acc", tag="wide", bufs=PACK)
+
+        x_cast(0)
+        x_gather(0)
+        gather_dy_both(0)
+        gather_dy_both(1)
+        make_dz(0, 0)
+        make_dz(1, 0)
+        gather_dy(0, 2)
+        make_dz(0, 1)
+        make_dz(1, 1)
+        make_dz(0, 2)
+        gather_dy(0, 3)
+        gather_dy(1, 2)
+        make_dz(0, 3)
+        dzf0 = dz_by_features(0, "dzf0")
+        wm0 = [wm_half(0, half) for half in range(2)]
+        dx0 = [dx_block(wm0, k, dzf0, late_bank(), "dx0_%d" % k) for k in range(PACK)]
+        gather_dy(1, 3)
+        make_dz(1, 2)
+        make_dz(1, 3)
+        dzs = [dz_by_slots(b) for b in range(B)]
+        for k in range(2):
+            scatter(0, k, dx0[k])
+        dzf1 = dz_by_features(1, "dx0_0")
+        wm1 = [wm_half(1, half) for half in range(2)]
+        for k in range(2, PACK):
+            scatter(0, k, dx0[k])
+
+        x_cast(1)
+        x_gather(1)
+        x_cast(2)
+        x_mx = [x_quantize(0, b) for b in range(B)]
+        staged_pair = keep.tile([P, 2, N], F32, name="staged_pair", tag="h2")
+        for k in range(2):
+            acc = wide_bank()
+            product(acc, wm1[0], k, dzf1)
+            nc.scalar.copy(
+                staged_pair[:, k, :].rearrange("p (s u e) -> p s u e", u=2, e=2),
+                acc[:].rearrange("p (u s e) -> p s u e", u=2, e=2),
+            )
+            scatter(1, k, staged_pair[:, k, :])
+        for b in range(B):
+            for k in range(2):
+                gw_block(b, k, x_mx[b], dzs[b])
+        x_gather(2)
+        scatter(1, 2, dx_block(wm1, 2, dzf1, wide_bank(), "x_bf0"))
+        x_cast(3)
+        x_gather(3)
+        x_mx = [x_quantize(1, b) for b in range(B)]
+        scatter(1, 3, dx_block(wm1, 3, dzf1, wide_bank(), "x_g3"))
+        for b in range(B):
+            for k in range(2, PACK):
+                gw_block(b, k, x_mx[b], dzs[b])

@@ -38,18 +38,15 @@ def tile_attend_gex_sig_wx_kernel(tc, xT, dyT, hT, ts, wm, offs, out_0, out_1):
         def expert_list(b):
             return offsets[:, b * LIST_COLS : (b + 1) * LIST_COLS]
 
-        ts_pool = keep.tile([P, T], F32, name="ts_pool", tag="ts_then_wm")
+        ts_pool = keep.tile([P, T], F32, name="ts_pool", tag="ts_then_wm", align_bytes=64)
         nc.sync.dma_start(ts_pool[TS_ROW:, :], ts[TS_ROW:, :])
         nc.vector.memset(ts_pool[:TS_ROW, :], 0.0)
 
         ident = keep.tile([P, P], F32, name="ident")
         make_identity(nc, ident[:])
 
-        windows = [keep.tile([P, T], F32, name="window0")]
-        nc.vector.memset(windows[0][:], 0.0)
-
-        def load(rows, shape, name, tag):
-            raw = keep.tile(shape, F32, name=name, tag=tag)
+        def load(rows, shape, name, tag, align_bytes=None):
+            raw = keep.tile(shape, F32, name=name, tag=tag, align_bytes=align_bytes)
             nc.sync.dma_start(raw[:], rows)
             return raw
 
@@ -90,13 +87,14 @@ def tile_attend_gex_sig_wx_kernel(tc, xT, dyT, hT, ts, wm, offs, out_0, out_1):
                         bias=ts_pos[b][:, t : t + 1], scale=ts_neg[b][:, t : t + 1],
                     )
 
-        for k, tag in ((1, "pos0"), (2, "neg0"), (3, "pos1")):
+        windows = []
+        for k, tag in enumerate(("pos0", "neg0", "pos1", "neg1")):
             windows.append(keep.tile([P, T], F32, name="window%d" % k, tag=tag))
             nc.gpsimd.memset(windows[k][:], 0.0)
 
-        wm_raw = [load(wm_rows[0], [P, PACK, D], "wm_raw0", "ts_then_wm")]
-        x_pool.append(load(x_rows[1], [P, T], "x_pool1", "h0"))
-        wm_raw.append(load(wm_rows[1], [P, PACK, D], "wm_raw1", "h1"))
+        wm_raw = [load(wm_rows[0], [P, PACK, D], "wm_raw0", "ts_then_wm", 64)]
+        wm_raw.append(load(wm_rows[1], [P, PACK, D], "wm_raw1", "h0"))
+        x_pool.append(load(x_rows[1], [P, T], "x_pool1", "h1"))
         x_pool.append(load(x_rows[2], [P, T], "x_pool2", "h2"))
         x_pool.append(load(x_rows[3], [P, T], "x_pool3", "h3"))
 
@@ -130,9 +128,9 @@ def tile_attend_gex_sig_wx_kernel(tc, xT, dyT, hT, ts, wm, offs, out_0, out_1):
             return h_g[j][:, i * 2 * P : (i + 1) * 2 * P].bitcast(BF16)
 
         dz = {(b, j): quarter(j + 1, b) for b in range(B) for j in range(2)}
-        for b in range(B):
-            for j in range(2, PACK):
-                dz[b, j] = quarter(0, 2 * b + j - 2)
+        for j in range(2, PACK):
+            dz[0, j] = keep.tile([P, P * PACK], BF16, name="dz0_%d" % j, tag="dz0_%d" % j, align_bytes=64)[:]
+            dz[1, j] = quarter(0, j)
 
         def gather_dy_both(j):
             nc.vector.tensor_tensor(dyh_tiles[j][:], dy_pool[j][:].indirect(offsets[:]), h_g[j][:], MULT)
@@ -150,15 +148,16 @@ def tile_attend_gex_sig_wx_kernel(tc, xT, dyT, hT, ts, wm, offs, out_0, out_1):
                 MULT,
             )
 
-        def dz_by_slots(b):
-            codes, scales = mx_tiles(DV, "dzs%d" % b, "rest1_%d" % (2 + b))
-            for j in range(PACK):
-                cols = slice(j * P, (j + 1) * P)
-                nc.vector.quantize_mx(out=codes[:, cols].bitcast(E5M2), scales=scales[:, cols], in_=dz[b, j])
-            return codes, scales
+        def dz_by_slots():
+            codes, scales = mx_tiles(B * DV, "dzs", "ts_then_wm")
+            for b in reversed(range(B)):
+                for j in range(PACK):
+                    cols = slice(b * DV + j * P, b * DV + (j + 1) * P)
+                    nc.vector.quantize_mx(out=codes[:, cols].bitcast(E5M2), scales=scales[:, cols], in_=dz[b, j])
+            return [(codes[:, b * DV : (b + 1) * DV], scales[:, b * DV : (b + 1) * DV]) for b in range(B)]
 
         def dz_by_features(b, tag):
-            dz_feat = ring.tile([P, 2, 2 * P, PACK], BF16, name="dz_feat", align_bytes=64)
+            dz_feat = keep.tile([P, 2, 2 * P, PACK], BF16, name="dz_feat", tag=("ts_then_wm", "dz_feat1")[b], align_bytes=64)
             for u in range(2):
                 bank = psum.tile([P, PACK, P], F32, name="feat_bank", tag="late")
                 for j in range(PACK):
@@ -169,35 +168,47 @@ def tile_attend_gex_sig_wx_kernel(tc, xT, dyT, hT, ts, wm, offs, out_0, out_1):
                 )
             return quantize(dz_feat[:].rearrange("p u q j -> p (u q j)"), N, E5M2, "dzf%d" % b, tag)
 
-        def wm_half(b, half):
-            wm_bf = ring.tile([P, 2 * P * PACK], BF16, name="wm_bf", align_bytes=64)
+        def wm_cast(b, half):
+            wm_bf = keep.tile([P, 2 * P * PACK], BF16, name="wm_bf", tag=("wm_bf%d" % half, "dz0_%d" % (2 + half))[b], align_bytes=64)
             dst = wm_bf[:].rearrange("p (a e j) -> p a j e", e=2, j=PACK)
             src = wm_raw[b][:, :, half * 2 * P : (half + 1) * 2 * P].rearrange("p j (a e) -> p a j e", e=2)
             if b == 0:
                 nc.scalar.copy(dst, src)
             else:
                 nc.gpsimd.tensor_scalar(dst, src, 1.0, 0.0, MULT, ADD)
-            return quantize(wm_bf[:], 2 * P, E4M3, "wm%d_%d" % (b, half), "wm%d_%d" % (b, half))
+            return wm_bf
 
-        def dx_block(wm_mx, k, dz_mx, acc, tag):
-            staged = keep.tile([P, N], F32, name="dx_staged", tag=tag, align_bytes=64)
-            product(acc, wm_mx[k // 2], k % 2, dz_mx)
+        def wm_quantize(b, halves, tag):
+            codes, scales = mx_tiles(D, "wm%d" % b, tag)
+            for half in range(2):
+                cols = slice(half * 2 * P, (half + 1) * 2 * P)
+                nc.vector.quantize_mx(out=codes[:, cols].bitcast(E4M3), scales=scales[:, cols], in_=halves[half][:])
+            return codes, scales
+
+        def staging(tag, blocks=1, align_bytes=None):
+            return keep.tile([P, blocks, N], F32, name="dx_staged", tag=tag, align_bytes=align_bytes)
+
+        def dx_block(wm_mx, k, dz_mx, acc, staged):
+            product(acc, wm_mx, k, dz_mx)
             nc.scalar.copy(
-                staged[:].rearrange("p (s u e) -> p s u e", u=2, e=2),
+                staged.rearrange("p (s u e) -> p s u e", u=2, e=2),
                 acc[:].rearrange("p (u s e) -> p s u e", u=2, e=2),
             )
             return staged
 
         def scatter(b, k, staged):
-            nc.vector.tensor_copy(windows[k][:].indirect(expert_list(b)), staged[:])
+            nc.vector.tensor_copy(windows[k][:].indirect(expert_list(b)), staged)
             if b == B - 1:
                 nc.sync.dma_start(out_1[k * P : (k + 1) * P, :], windows[k][:])
 
         x_bf, x_g = {}, {}
 
         def x_cast(k):
-            x_bf[k] = keep.tile([P, T], BF16, name="x_bf", tag="x_bf%d" % (k % 2), align_bytes=64)
-            nc.scalar.activation(x_bf[k][:], x_pool[k][:], COPY)
+            x_bf[k] = keep.tile([P, T], BF16, name="x_bf", tag="x_bf%d" % (k % 2))
+            pieces = 2 if k == 1 else 1
+            for i in range(pieces):
+                cols = slice(i * T // pieces, (i + 1) * T // pieces)
+                nc.scalar.activation(x_bf[k][:, cols], x_pool[k][:, cols], COPY)
 
         def x_gather(k):
             x_g[k] = keep.tile([P, 2, B * P, 2], BF16, name="x_g", tag="x_g%d" % k, align_bytes=64)
@@ -217,12 +228,12 @@ def tile_attend_gex_sig_wx_kernel(tc, xT, dyT, hT, ts, wm, offs, out_0, out_1):
             )
             return quantize(x_slot[:], 2 * P, E4M3, "x%d_%d" % (pair, b), "x%d_%d" % (pair, b))
 
-        def gw_block(b, k, x_mx, dz_mx):
+        def gw_block(b, k, x_mx, dz_mx, queue):
             acc = psum.tile([P, DV], F32, name="gw_acc", tag="wide", bufs=PACK)
             product(acc, x_mx, k % 2, dz_mx)
-            gw = ring.tile([P, DV], F32, name="gw", bufs=PACK)
+            gw = ring.tile([P, DV], F32, name="gw", bufs=2 * PACK)
             nc.scalar.copy(gw[:].rearrange("p (m j) -> p m j", j=PACK), acc[:].rearrange("p (j m) -> p m j", j=PACK))
-            nc.sync.dma_start(out_0[b, k * P : (k + 1) * P, :], gw[:])
+            queue.dma_start(out_0[b, k * P : (k + 1) * P, :], gw[:])
 
         def late_bank():
             return psum.tile([P, N], F32, name="dx_acc", tag="late")
@@ -242,43 +253,38 @@ def tile_attend_gex_sig_wx_kernel(tc, xT, dyT, hT, ts, wm, offs, out_0, out_1):
         make_dz(0, 2)
         gather_dy(0, 3)
         gather_dy(1, 2)
+        wm_bf0 = [wm_cast(0, half) for half in range(2)]
         make_dz(0, 3)
         dzf0 = dz_by_features(0, "dzf0")
-        wm0 = [wm_half(0, half) for half in range(2)]
-        dx0 = [dx_block(wm0, k, dzf0, late_bank(), "dx0_%d" % k) for k in range(PACK)]
         gather_dy(1, 3)
         make_dz(1, 2)
+        wm0 = wm_quantize(0, wm_bf0, "rest1_2")
+        dx0 = [dx_block(wm0, k, dzf0, late_bank(), staging("dx0_%d" % k, 1, 64)[:, 0, :]) for k in range(2)]
         make_dz(1, 3)
-        dzs = [dz_by_slots(b) for b in range(B)]
+        dzs = dz_by_slots()
         for k in range(2):
             scatter(0, k, dx0[k])
+        wm1 = wm_quantize(1, [wm_cast(1, half) for half in range(2)], "wm1")
         dzf1 = dz_by_features(1, "dx0_0")
-        wm1 = [wm_half(1, half) for half in range(2)]
-        for k in range(2, PACK):
-            scatter(0, k, dx0[k])
+        scatter(0, 2, dx_block(wm0, 2, dzf0, late_bank(), staging("dx0_2")[:, 0, :]))
 
         x_cast(1)
         x_gather(1)
         x_cast(2)
-        x_mx = [x_quantize(0, b) for b in range(B)]
-        staged_pair = keep.tile([P, 2, N], F32, name="staged_pair", tag="h2")
+        three = staging("h2", 3)
         for k in range(2):
-            acc = wide_bank()
-            product(acc, wm1[0], k, dzf1)
-            nc.scalar.copy(
-                staged_pair[:, k, :].rearrange("p (s u e) -> p s u e", u=2, e=2),
-                acc[:].rearrange("p (u s e) -> p s u e", u=2, e=2),
-            )
-            scatter(1, k, staged_pair[:, k, :])
+            scatter(1, k, dx_block(wm1, k, dzf1, late_bank(), three[:, k, :]))
+        x_mx = [x_quantize(0, b) for b in range(B)]
+        scatter(1, 2, dx_block(wm1, 2, dzf1, wide_bank(), three[:, 2, :]))
+        x_gather(2)
+        scatter(0, 3, dx_block(wm0, 3, dzf0, wide_bank(), staging("x_bf0")[:, 0, :]))
+        x_cast(3)
         for b in range(B):
             for k in range(2):
-                gw_block(b, k, x_mx[b], dzs[b])
-        x_gather(2)
-        scatter(1, 2, dx_block(wm1, 2, dzf1, wide_bank(), "x_bf0"))
-        x_cast(3)
+                gw_block(b, k, x_mx[b], dzs[b], nc.sync)
         x_gather(3)
         x_mx = [x_quantize(1, b) for b in range(B)]
-        scatter(1, 3, dx_block(wm1, 3, dzf1, wide_bank(), "x_g3"))
+        scatter(1, 3, dx_block(wm1, 3, dzf1, wide_bank(), staging("x_g3", 1, 64)[:, 0, :]))
         for b in range(B):
             for k in range(2, PACK):
-                gw_block(b, k, x_mx[b], dzs[b])
+                gw_block(b, k, x_mx[b], dzs[b], nc.scalar)

@@ -21,7 +21,8 @@ IDENTITY = mybir.ActivationFunctionType.Identity
 P = 128
 PACK = 4
 LIST_COLS = N // 16
-TS_ROW = 96
+LAST_QUADRANT = 96
+TS_ROW = P - 1
 
 
 def tile_attend_gex_sig_wx_kernel(tc, xT, dyT, hT, ts, wm, offs, out_0, out_1):
@@ -40,7 +41,8 @@ def tile_attend_gex_sig_wx_kernel(tc, xT, dyT, hT, ts, wm, offs, out_0, out_1):
 
         ts_pool = keep.tile([P, T], F32, name="ts_pool", tag="ts_then_wm", align_bytes=64)
         nc.sync.dma_start(ts_pool[TS_ROW:, :], ts[TS_ROW:, :])
-        nc.vector.memset(ts_pool[:TS_ROW, :], 0.0)
+        nc.vector.memset(ts_pool[:LAST_QUADRANT, :].bitcast(U32), 0)
+        nc.vector.memset(ts_pool[LAST_QUADRANT:TS_ROW, :].bitcast(U32), 0)
 
         ident = keep.tile([P, P], F32, name="ident")
         make_identity(nc, ident[:])
@@ -66,29 +68,32 @@ def tile_attend_gex_sig_wx_kernel(tc, xT, dyT, hT, ts, wm, offs, out_0, out_1):
         ts_g = keep.tile([P, B * N], F32, name="ts_g")
         nc.vector.tensor_copy(ts_g[:], ts_pool[:].indirect(offsets[:]))
         ts_pos = [keep.tile([P, PACK], F32, name="ts_pos%d" % b, tag="pos%d" % b) for b in range(B)]
-        ts_neg = [keep.tile([P, PACK], F32, name="ts_neg%d" % b, tag="neg%d" % b) for b in range(B)]
         for b in range(B):
             bank = psum.tile([P, PACK, P], F32, name="ts_bank", tag="early")
             turn(bank, ts_g, b)
             nc.scalar.activation(ts_pos[b][:], bank[:, :, TS_ROW], COPY)
-            nc.scalar.activation(ts_neg[b][:], bank[:, :, TS_ROW], COPY, scale=-1.0)
 
         h_g = [keep.tile([P, B * N], F32, name="h_g%d" % j, align_bytes=64) for j in range(PACK)]
         rest = {}
         for j in range(PACK):
             nc.vector.tensor_copy(h_g[j][:], h_pool[j][:].indirect(offsets[:]))
+            tag, align = (("dz_feat1", 64), ("x_bf1", None), ("om2", None), ("om3", None))[j]
+            one_less = keep.tile([P, B, PACK, P], F32, name="one_less", tag=tag, align_bytes=align)
+            nc.scalar.activation(
+                one_less[:].rearrange("p b t s -> p b s t"),
+                h_g[j][:].rearrange("p (b s t) -> p b s t", b=B, t=PACK),
+                IDENTITY, bias=1.0, scale=-1.0,
+            )
             for b in range(B):
                 bank = psum.tile([P, PACK, P], F32, name="h_bank", tag="early")
-                turn(bank, h_g[j], b)
+                for t in range(PACK):
+                    nc.tensor.transpose(bank[:, t, :], one_less[:, b, t, :], ident[:])
                 rest[b, j] = keep.tile([P, PACK, P], F32, name="rest%d_%d" % (b, j), tag="rest%d_%d" % (b, j), align_bytes=64)
                 for t in range(PACK):
-                    nc.scalar.activation(
-                        rest[b, j][:, t, :], bank[:, t, :], IDENTITY,
-                        bias=ts_pos[b][:, t : t + 1], scale=ts_neg[b][:, t : t + 1],
-                    )
+                    nc.scalar.activation(rest[b, j][:, t, :], bank[:, t, :], COPY, scale=ts_pos[b][:, t : t + 1])
 
         windows = []
-        for k, tag in enumerate(("pos0", "neg0", "pos1", "neg1")):
+        for k, tag in enumerate(("om2", "om3", "pos0", "pos1")):
             windows.append(keep.tile([P, T], F32, name="window%d" % k, tag=tag))
             nc.gpsimd.memset(windows[k][:], 0.0)
 
@@ -130,13 +135,22 @@ def tile_attend_gex_sig_wx_kernel(tc, xT, dyT, hT, ts, wm, offs, out_0, out_1):
         dz = {(b, j): quarter(j + 1, b) for b in range(B) for j in range(2)}
         for j in range(2, PACK):
             dz[0, j] = keep.tile([P, P * PACK], BF16, name="dz0_%d" % j, tag="dz0_%d" % j, align_bytes=64)[:]
-            dz[1, j] = quarter(0, j)
+
+        dz[1, 2] = quarter(0, 0)
 
         def gather_dy_both(j):
             nc.vector.tensor_tensor(dyh_tiles[j][:], dy_pool[j][:].indirect(offsets[:]), h_g[j][:], MULT)
 
-        def gather_dy(b, j):
-            nc.vector.tensor_tensor(dyh[b, j], dy_pool[j][:].indirect(expert_list(b)), h_g[j][:, b * N : (b + 1) * N], MULT)
+        def gather_dy(b, j, pieces):
+            width = N // pieces
+            for i in range(pieces):
+                first = b * N + i * width
+                nc.vector.tensor_tensor(
+                    dyh[b, j][:, i * width : (i + 1) * width],
+                    dy_pool[j][:].indirect(offsets[:, first // 16 : (first + width) // 16]),
+                    h_g[j][:, first : first + width],
+                    MULT,
+                )
 
         def make_dz(b, j):
             bank = psum.tile([P, PACK, P], F32, name="dyh_bank", tag="wide", bufs=PACK)
@@ -244,22 +258,24 @@ def tile_attend_gex_sig_wx_kernel(tc, xT, dyT, hT, ts, wm, offs, out_0, out_1):
         x_cast(0)
         x_gather(0)
         gather_dy_both(0)
-        gather_dy_both(1)
+        gather_dy(0, 1, 1)
+        gather_dy(1, 1, 1)
         make_dz(0, 0)
         make_dz(1, 0)
-        gather_dy(0, 2)
+        gather_dy(0, 2, 2)
         make_dz(0, 1)
         make_dz(1, 1)
         make_dz(0, 2)
-        gather_dy(0, 3)
-        gather_dy(1, 2)
+        gather_dy(0, 3, 2)
+        gather_dy(1, 2, 2)
         wm_bf0 = [wm_cast(0, half) for half in range(2)]
         make_dz(0, 3)
         dzf0 = dz_by_features(0, "dzf0")
-        gather_dy(1, 3)
+        gather_dy(1, 3, 1)
         make_dz(1, 2)
-        wm0 = wm_quantize(0, wm_bf0, "rest1_2")
+        wm0 = wm_quantize(0, wm_bf0, "wm0")
         dx0 = [dx_block(wm0, k, dzf0, late_bank(), staging("dx0_%d" % k, 1, 64)[:, 0, :]) for k in range(2)]
+        dz[1, 3] = keep.tile([P, P * PACK], BF16, name="dz1_3", tag="wm_bf0", align_bytes=64)[:]
         make_dz(1, 3)
         dzs = dz_by_slots()
         for k in range(2):

@@ -222,7 +222,7 @@ def tile_attend_gex_sig_wx_kernel(tc, xT, dyT, hT, ts, wm, offs, out_0, out_1):
             pieces = 2 if k == 1 else 1
             for i in range(pieces):
                 cols = slice(i * T // pieces, (i + 1) * T // pieces)
-                nc.scalar.activation(x_bf[k][:, cols], x_pool[k][:, cols], COPY)
+                nc.gpsimd.tensor_copy(x_bf[k][:, cols], x_pool[k][:, cols])
 
         def x_gather(k):
             x_g[k] = keep.tile([P, 2, B * P, 2], BF16, name="x_g", tag="x_g%d" % k, align_bytes=64)

@@ -16,6 +16,7 @@ E5M2 = mybir.dt.float8_e5m2_x4
 MULT = mybir.AluOpType.mult
 ADD = mybir.AluOpType.add
 COPY = mybir.ActivationFunctionType.Copy
+SQUARE = mybir.ActivationFunctionType.Square
 IDENTITY = mybir.ActivationFunctionType.Identity
 
 P = 128
@@ -30,88 +31,98 @@ def tile_attend_gex_sig_wx_kernel(tc, xT, dyT, hT, ts, wm, offs, out_0, out_1):
     with ExitStack() as ctx:
         lists = ctx.enter_context(tc.tile_pool(name="lists", bufs=1))
         keep = ctx.enter_context(tc.tile_pool(name="keep", bufs=1))
-        ring = ctx.enter_context(tc.tile_pool(name="ring", bufs=2))
-        psum = ctx.enter_context(tc.psum_pool(name="psum", bufs=2))
+        relay = ctx.enter_context(tc.tile_pool(name="relay", bufs=1))
+        psum = ctx.enter_context(tc.psum_pool(name="psum", bufs=1))
+
+        KIB = 1024
+        placed = {
+            "staged0_1": 0, "ts_quarter1": 0, "wm_raw1_0": 2 * KIB - 64, "x_bf1": 2 * KIB,
+            "staged1_1": 6 * KIB, "wm_raw0_1": 8 * KIB - 64, "x_bf2": 8 * KIB,
+            "staged0_2": 12 * KIB, "wm_raw1_1": 14 * KIB - 64, "x_g2": 14 * KIB,
+        }
+
+        def sb(shape, dtype, name, tag=None, bufs=1):
+            if (tag or name) in placed:
+                return relay.tile(shape, dtype, name=name, tag=tag or name, align_bytes=64, offset=placed[tag or name])
+            return keep.tile(shape, dtype, name=name, tag=tag or name, bufs=bufs, align_bytes=64)
 
         offsets = lists.tile([P, B * LIST_COLS], U16, name="offsets")
         nc.sync.dma_start(offsets[:], offs)
 
-        def expert_list(b):
-            return offsets[:, b * LIST_COLS : (b + 1) * LIST_COLS]
+        def entries(first, count):
+            return offsets[:, first // 16 : (first + count) // 16]
 
-        ts_pool = keep.tile([P, T], F32, name="ts_pool", tag="ts_then_wm", align_bytes=64)
+        ts_pool = sb([P, T], F32, "ts_pool")
         nc.sync.dma_start(ts_pool[TS_ROW:, :], ts[TS_ROW:, :])
         nc.vector.memset(ts_pool[:LAST_QUADRANT, :].bitcast(U32), 0)
-        nc.vector.memset(ts_pool[LAST_QUADRANT:TS_ROW, :].bitcast(U32), 0)
+        nc.gpsimd.memset(ts_pool[LAST_QUADRANT:TS_ROW, :].bitcast(U32), 0)
 
-        ident = keep.tile([P, P], F32, name="ident")
+        ident = sb([P, P], F32, "ident")
         make_identity(nc, ident[:])
+        minus_one = sb([P, 1], F32, "minus_one")
+        nc.vector.memset(minus_one[:], -1.0)
+        one = sb([P, 1], F32, "one")
+        nc.scalar.activation(one[:], minus_one[:], SQUARE)
 
-        def load(rows, shape, name, tag, align_bytes=None):
-            raw = keep.tile(shape, F32, name=name, tag=tag, align_bytes=align_bytes)
+        def load(rows, shape, name, tag=None):
+            raw = sb(shape, F32, name, tag)
             nc.sync.dma_start(raw[:], rows)
             return raw
 
         h_rows = hT.rearrange("(m j) c -> j m c", j=PACK)
         dy_rows = dyT.rearrange("(m j) c -> j m c", j=PACK)
-        wm_rows = [wm[b].rearrange("(m j) d -> m j d", j=PACK) for b in range(B)]
         x_rows = xT.rearrange("(k m) c -> k m c", m=P)
-        h_pool = [load(h_rows[j], [P, T], "h_pool%d" % j, "h%d" % j) for j in range(PACK)]
-        dy_pool = [load(dy_rows[j], [P, T], "dy_pool%d" % j, "dy%d" % j) for j in range(2)]
-        x_pool = [load(x_rows[0], [P, T], "x_pool0", "x0")]
-        dy_pool += [load(dy_rows[j], [P, T], "dy_pool%d" % j, "dy%d" % j) for j in range(2, PACK)]
-
-        def turn(bank, words, b):
-            for t in range(PACK):
-                nc.tensor.transpose(bank[:, t, :], words[:, b * N + t : (b + 1) * N : PACK], ident[:])
-
-        ts_g = keep.tile([P, B * N], F32, name="ts_g")
-        nc.vector.tensor_copy(ts_g[:], ts_pool[:].indirect(offsets[:]))
-        ts_pos = [keep.tile([P, PACK], F32, name="ts_pos%d" % b, tag="pos%d" % b) for b in range(B)]
-        for b in range(B):
-            bank = psum.tile([P, PACK, P], F32, name="ts_bank", tag="early")
-            turn(bank, ts_g, b)
-            nc.scalar.activation(ts_pos[b][:], bank[:, :, TS_ROW], COPY)
-
-        h_g = [keep.tile([P, B * N], F32, name="h_g%d" % j, align_bytes=64) for j in range(PACK)]
-        rest = {}
-        for j in range(PACK):
-            nc.vector.tensor_copy(h_g[j][:], h_pool[j][:].indirect(offsets[:]))
-            tag, align = (("dz_feat1", 64), ("x_bf1", None), ("om2", None), ("om3", None))[j]
-            one_less = keep.tile([P, B, PACK, P], F32, name="one_less", tag=tag, align_bytes=align)
-            nc.scalar.activation(
-                one_less[:].rearrange("p b t s -> p b s t"),
-                h_g[j][:].rearrange("p (b s t) -> p b s t", b=B, t=PACK),
-                IDENTITY, bias=1.0, scale=-1.0,
-            )
-            for b in range(B):
-                bank = psum.tile([P, PACK, P], F32, name="h_bank", tag="early")
-                for t in range(PACK):
-                    nc.tensor.transpose(bank[:, t, :], one_less[:, b, t, :], ident[:])
-                rest[b, j] = keep.tile([P, PACK, P], F32, name="rest%d_%d" % (b, j), tag="rest%d_%d" % (b, j), align_bytes=64)
-                for t in range(PACK):
-                    nc.scalar.activation(rest[b, j][:, t, :], bank[:, t, :], COPY, scale=ts_pos[b][:, t : t + 1])
+        h_pool = [load(h_rows[j], [P, T], "h%d" % j) for j in range(PACK)]
+        x_pool = {0: load(x_rows[0], [P, T], "x_pool0")}
+        dy_pool = [load(dy_rows[j], [P, T], "dy%d" % j) for j in range(PACK)]
 
         windows = []
-        for k, tag in enumerate(("om2", "om3", "pos0", "pos1")):
-            windows.append(keep.tile([P, T], F32, name="window%d" % k, tag=tag))
+        for k in range(PACK):
+            windows.append(sb([P, T], F32, "window%d" % k))
             nc.gpsimd.memset(windows[k][:], 0.0)
 
-        wm_raw = [load(wm_rows[0], [P, PACK, D], "wm_raw0", "ts_then_wm", 64)]
-        wm_raw.append(load(wm_rows[1], [P, PACK, D], "wm_raw1", "h0"))
-        x_pool.append(load(x_rows[1], [P, T], "x_pool1", "h1"))
-        x_pool.append(load(x_rows[2], [P, T], "x_pool2", "h2"))
-        x_pool.append(load(x_rows[3], [P, T], "x_pool3", "h3"))
+        ts_g = sb([P, B * N], F32, "ts_g")
+        nc.vector.tensor_copy(ts_g[:], ts_pool[:].indirect(offsets[:]))
+        ts_quarter = []
+        for b in range(B):
+            bank = psum.tile([P, PACK, P], F32, name="ts_bank", tag="fwd%d" % b)
+            for t in range(PACK):
+                nc.tensor.transpose(bank[:, t, :], ts_g[:, b * N + t : (b + 1) * N : PACK], ident[:])
+            ts_quarter.append(sb([P, PACK], F32, "ts_quarter%d" % b))
+            nc.scalar.activation(ts_quarter[b][:], bank[:, :, TS_ROW], COPY, scale=0.25)
 
-        def mx_tiles(width, name, tag):
-            codes = keep.tile([P, width], U32, name=name + "_codes", tag=tag, align_bytes=64)
-            scales = keep.tile([P, width], U8, name=name + "_scales", align_bytes=64)
-            return codes, scales
+        slope = []
+        for j in range(PACK):
+            h_g = sb([P, B * N], F32, "h_g", bufs=2)
+            nc.vector.tensor_copy(h_g[:], h_pool[j][:].indirect(offsets[:]))
+            square = sb([P, B * N], F32, "square", bufs=2)
+            nc.scalar.activation(square[:], h_g[:], SQUARE, bias=one[:], scale=-2.0)
+            slope.append(sb([P, B * N], F32, "slope%d" % j))
+            nc.scalar.activation(slope[j][:], square[:], IDENTITY, bias=one[:], scale=-1.0)
 
-        def quantize(src, width, fmt, name, tag):
-            codes, scales = mx_tiles(width, name, tag)
-            nc.vector.quantize_mx(out=codes[:].bitcast(fmt), scales=scales[:], in_=src)
-            return codes, scales
+        HALF = N // 2
+        wm_raw = {}
+
+        def load_wm(b, half):
+            rows = wm[b].rearrange("(m j) d -> m j d", j=PACK)[:, :, half * HALF : (half + 1) * HALF]
+            wm_raw[b, half] = load(rows, [P, PACK, HALF], "wm_raw%d_%d" % (b, half))
+
+        def load_x(k):
+            x_pool[k] = load(x_rows[k], [P, T], "x_pool%d" % k, "h%d" % k)
+
+        load_wm(0, 0)
+        load_wm(1, 0)
+        load_x(1)
+        load_wm(0, 1)
+        load_wm(1, 1)
+        for k in range(2, PACK):
+            load_x(k)
+
+        def mx_tiles(width, name):
+            return sb([P, width], U32, name + "_codes"), sb([P, width], U8, name + "_scales")
+
+        def quantize(mx, cols, src, fmt):
+            nc.vector.quantize_mx(out=mx[0][:, cols].bitcast(fmt), scales=mx[1][:, cols], in_=src)
 
         def product(acc, left, e, right):
             nc.tensor.matmul_mx(
@@ -124,183 +135,185 @@ def tile_attend_gex_sig_wx_kernel(tc, xT, dyT, hT, ts, wm, offs, out_0, out_1):
                 stop=True,
             )
 
-        dyh_tiles = [keep.tile([P, B * N], F32, name="dyh%d" % i) for i in range(2)]
-        dyh = {(b, j): dyh_tiles[j][:, b * N : (b + 1) * N] for b in range(B) for j in range(2)}
-        dyh[0, 2], dyh[0, 3], dyh[1, 3] = dyh[0, 0], dyh[1, 0], dyh[0, 1]
-        dyh[1, 2] = h_g[3][:, :N]
-
-        def quarter(j, i):
-            return h_g[j][:, i * 2 * P : (i + 1) * 2 * P].bitcast(BF16)
-
-        dz = {(b, j): quarter(j + 1, b) for b in range(B) for j in range(2)}
-        for j in range(2, PACK):
-            dz[0, j] = keep.tile([P, P * PACK], BF16, name="dz0_%d" % j, tag="dz0_%d" % j, align_bytes=64)[:]
-
-        dz[1, 2] = quarter(0, 0)
-
-        def gather_dy_both(j):
-            nc.vector.tensor_tensor(dyh_tiles[j][:], dy_pool[j][:].indirect(offsets[:]), h_g[j][:], MULT)
-
-        def gather_dy(b, j, pieces):
-            width = N // pieces
-            for i in range(pieces):
-                first = b * N + i * width
-                nc.vector.tensor_tensor(
-                    dyh[b, j][:, i * width : (i + 1) * width],
-                    dy_pool[j][:].indirect(offsets[:, first // 16 : (first + width) // 16]),
-                    h_g[j][:, first : first + width],
-                    MULT,
-                )
-
-        def make_dz(b, j):
-            bank = psum.tile([P, PACK, P], F32, name="dyh_bank", tag="wide", bufs=PACK)
-            turn(bank, dyh[b, j], 0)
-            nc.vector.tensor_tensor(
-                dz[b, j].rearrange("p (a e t) -> p a t e", e=2, t=PACK),
-                bank[:].rearrange("p t (a e) -> p a t e", e=2),
-                rest[b, j][:].rearrange("p t (a e) -> p a t e", e=2),
-                MULT,
+        def weave(dst, src):
+            return (
+                dst.rearrange("p (a e j) -> p a j e", e=PACK, j=PACK),
+                src.rearrange("p j (a e) -> p a j e", e=PACK),
             )
 
-        def dz_by_slots():
-            codes, scales = mx_tiles(B * DV, "dzs", "ts_then_wm")
-            for b in reversed(range(B)):
-                for j in range(PACK):
-                    cols = slice(b * DV + j * P, b * DV + (j + 1) * P)
-                    nc.vector.quantize_mx(out=codes[:, cols].bitcast(E5M2), scales=scales[:, cols], in_=dz[b, j])
-            return [(codes[:, b * DV : (b + 1) * DV], scales[:, b * DV : (b + 1) * DV]) for b in range(B)]
+        def gpsimd_cast(dst, src):
+            nc.gpsimd.tensor_scalar(dst, src, 1.0, 0.0, MULT, ADD)
 
-        def dz_by_features(b, tag):
-            dz_feat = keep.tile([P, 2, 2 * P, PACK], BF16, name="dz_feat", tag=("ts_then_wm", "dz_feat1")[b], align_bytes=64)
-            for u in range(2):
-                bank = psum.tile([P, PACK, P], F32, name="feat_bank", tag="late")
-                for j in range(PACK):
-                    nc.tensor.transpose(bank[:, j, :], dz[b, j].bitcast(F32)[:, u::2], ident[:])
-                nc.scalar.copy(
-                    dz_feat[:, u, :, :],
-                    bank[:].rearrange("p j s -> p (j s)").bitcast(BF16).rearrange("p (j q) -> p q j", j=PACK),
+        dzf = [mx_tiles(N, "dzf%d" % b) for b in range(B)]
+        grad, fwd, back = {}, {}, {}
+        dz_t = {}
+
+        def dz_part(b, u, t, count=1):
+            return dz_t[b, u][:, t * 2 * P : (t + count) * 2 * P]
+
+
+        def gather_grad(b, j):
+            grad[b, j] = sb([P, N], F32, "grad%d_%d" % (b, j))
+            nc.vector.tensor_tensor(grad[b, j][:], dy_pool[j][:].indirect(entries(b * N, N)), slope[j][:, b * N : (b + 1) * N], MULT)
+            for t in range(PACK):
+                if j % 2 == 0 and t % 2 == 0:
+                    fwd[b, t // 2] = psum.tile([P, 2, 2, P], F32, name="fwd", tag="fwd%d" % (2 * b + t // 2))
+                nc.tensor.transpose(fwd[b, t // 2][:, t % 2, j % 2, :], grad[b, j][:, t::PACK], ident[:])
+
+        def scalar_scale(dst, src, factor):
+            nc.scalar.activation(dst, src, COPY, scale=factor)
+
+        def vector_scale(dst, src, factor):
+            nc.vector.tensor_scalar(dst, src, factor, None, MULT)
+
+        def weigh(b, u, half, scale, tag=None):
+            if half == 0:
+                dz_t[b, u] = sb([P, PACK * 2 * P], BF16, "dz_t%d_%d" % (b, u), tag)
+            if u == 0:
+                back[b, half] = psum.tile([P, 2, 2, P], F32, name="back", tag="back%d" % (2 * b + half))
+            for i in range(2):
+                t = 2 * half + i
+                scale(
+                    dz_part(b, u, t).rearrange("p (m e) -> p m e", e=2),
+                    fwd[b, half][:, i].rearrange("p e m -> p m e"),
+                    ts_quarter[b][:, t : t + 1],
                 )
-            return quantize(dz_feat[:].rearrange("p u q j -> p (u q j)"), N, E5M2, "dzf%d" % b, tag)
+            for i in range(2):
+                nc.tensor.transpose(back[b, half][:, i, u, :], dz_part(b, u, 2 * half + i).bitcast(F32), ident[:])
 
-        def wm_cast(b, half):
-            wm_bf = keep.tile([P, 2 * P * PACK], BF16, name="wm_bf", tag=("wm_bf%d" % half, "dz0_%d" % (2 + half))[b], align_bytes=64)
-            dst = wm_bf[:].rearrange("p (a e j) -> p a j e", e=2, j=PACK)
-            src = wm_raw[b][:, :, half * 2 * P : (half + 1) * 2 * P].rearrange("p j (a e) -> p a j e", e=2)
-            if b == 0:
-                nc.scalar.copy(dst, src)
-            else:
-                nc.gpsimd.tensor_scalar(dst, src, 1.0, 0.0, MULT, ADD)
-            return wm_bf
+        def dz_by_features(b, half, copy, tag):
+            feat = sb([P, HALF * PACK], BF16, "feat", tag)
+            copy(
+                feat[:].bitcast(F32).rearrange("p (s i u) -> p s i u", i=2, u=2),
+                back[b, half][:].rearrange("p i u s -> p s i u"),
+            )
+            quantize(dzf[b], slice(half * HALF, (half + 1) * HALF), feat[:], E5M2)
 
-        def wm_quantize(b, halves, tag):
-            codes, scales = mx_tiles(D, "wm%d" % b, tag)
-            for half in range(2):
-                cols = slice(half * 2 * P, (half + 1) * 2 * P)
-                nc.vector.quantize_mx(out=codes[:, cols].bitcast(E4M3), scales=scales[:, cols], in_=halves[half][:])
-            return codes, scales
+        def wm_half(b, half, tag):
+            wm_bf = sb([P, HALF * PACK], BF16, "wm_bf", tag)
+            gpsimd_cast(*weave(wm_bf[:], wm_raw[b, half][:]))
+            mx = mx_tiles(HALF, "wm%d_%d" % (b, half))
+            quantize(mx, slice(0, HALF), wm_bf[:], E4M3)
+            return mx
 
-        def staging(tag, blocks=1, align_bytes=None):
-            return keep.tile([P, blocks, N], F32, name="dx_staged", tag=tag, align_bytes=align_bytes)
+        def dx_product(b, wm_mx, e, bank):
+            acc = psum.tile([P, N], F32, name="dx_acc", tag="fwd%d" % bank)
+            product(acc, wm_mx, e, dzf[b])
+            return acc
 
-        def dx_block(wm_mx, k, dz_mx, acc, staged):
-            product(acc, wm_mx, k, dz_mx)
+        def dx_block(b, wm_mx, e, tag):
+            return stage(dx_product(b, wm_mx, e, b), tag)
+
+        def stage(acc, tag):
+            staged = sb([P, N], F32, "staged", tag)
             nc.scalar.copy(
-                staged.rearrange("p (s u e) -> p s u e", u=2, e=2),
-                acc[:].rearrange("p (u s e) -> p s u e", u=2, e=2),
+                staged[:].rearrange("p (s h i) -> p s h i", h=2, i=2),
+                acc[:].rearrange("p (h s i) -> p s h i", h=2, i=2),
             )
             return staged
 
         def scatter(b, k, staged):
-            nc.vector.tensor_copy(windows[k][:].indirect(expert_list(b)), staged)
+            nc.vector.tensor_copy(windows[k][:].indirect(entries(b * N, N)), staged[:])
             if b == B - 1:
                 nc.sync.dma_start(out_1[k * P : (k + 1) * P, :], windows[k][:])
 
-        x_bf, x_g = {}, {}
+        def dz_by_slots(b, tag):
+            slots = sb([P, DV * PACK], BF16, "dz_slots", tag)
+            for u in range(2):
+                gpsimd_cast(
+                    slots[:].rearrange("p (m u e t) -> p u m e t", u=2, e=2, t=PACK)[:, u],
+                    dz_part(b, u, 0, PACK).rearrange("p (t m e) -> p m e t", t=PACK, e=2),
+                )
+            mx = mx_tiles(DV, "dzs%d" % b)
+            quantize(mx, slice(0, DV), slots[:], E5M2)
+            return mx
 
-        def x_cast(k):
-            x_bf[k] = keep.tile([P, T], BF16, name="x_bf", tag="x_bf%d" % (k % 2))
-            pieces = 2 if k == 1 else 1
-            for i in range(pieces):
-                cols = slice(i * T // pieces, (i + 1) * T // pieces)
-                nc.gpsimd.tensor_copy(x_bf[k][:, cols], x_pool[k][:, cols])
+        x_g = {}
+
+        x_bf = {}
+
+        def x_cast(k, on_vector=False):
+            x_bf[k] = sb([P, T], BF16, "x_bf", ("ts_pool", "x_bf1", "x_bf2", "dy3")[k])
+            if on_vector:
+                nc.vector.tensor_copy(x_bf[k][:], x_pool[k][:])
+            else:
+                nc.scalar.activation(x_bf[k][:], x_pool[k][:], COPY)
 
         def x_gather(k):
-            x_g[k] = keep.tile([P, 2, B * P, 2], BF16, name="x_g", tag="x_g%d" % k, align_bytes=64)
+            x_g[k] = sb([P, 2, B * P, 2], BF16, "x_g%d" % k)
             nc.scalar.activation(x_g[k][:].rearrange("p u s e -> p s u e"), x_bf[k][:].indirect(offsets[:]), COPY)
 
         def x_quantize(pair, b):
-            bank = psum.tile([P, 2, 2, P], F32, name="x_bank", tag="early")
+            bank = psum.tile([P, 2, 2, P], F32, name="x_bank", tag="back%d" % b)
             for e in range(2):
                 words = x_g[2 * pair + e][:].rearrange("p u s e -> p (u s e)").bitcast(F32)
                 for u in range(2):
                     first = (u * B + b) * P
                     nc.tensor.transpose(bank[:, e, u, :], words[:, first : first + P], ident[:])
-            x_slot = ring.tile([P, 2 * P * PACK], BF16, name="x_slot", align_bytes=64)
+            x_slot = sb([P, 2 * P * PACK], BF16, "x_slot", "grad%d_%d" % (b, pair))
             nc.scalar.copy(
                 x_slot[:].bitcast(F32).rearrange("p (e m u) -> p e m u", e=2, u=2),
                 bank[:].rearrange("p e u m -> p e m u"),
             )
-            return quantize(x_slot[:], 2 * P, E4M3, "x%d_%d" % (pair, b), "x%d_%d" % (pair, b))
+            mx = mx_tiles(2 * P, "x%d_%d" % (pair, b))
+            quantize(mx, slice(0, 2 * P), x_slot[:], E4M3)
+            return mx
 
-        def gw_block(b, k, x_mx, dz_mx, queue):
-            acc = psum.tile([P, DV], F32, name="gw_acc", tag="wide", bufs=PACK)
-            product(acc, x_mx, k % 2, dz_mx)
-            gw = ring.tile([P, DV], F32, name="gw", bufs=2 * PACK)
-            nc.scalar.copy(gw[:].rearrange("p (m j) -> p m j", j=PACK), acc[:].rearrange("p (j m) -> p m j", j=PACK))
-            queue.dma_start(out_0[b, k * P : (k + 1) * P, :], gw[:])
+        def gw_blocks(pair, x_mx, dzs, tag):
+            gw = sb([P, PACK, DV], F32, "gw", tag)
+            for b in range(B):
+                for e in range(2):
+                    acc = psum.tile([P, DV], F32, name="gw_acc", tag=("fwd2", "fwd3", "back2", "back3")[2 * b + e])
+                    product(acc, x_mx[b], e, dzs[b])
+                    nc.scalar.copy(gw[:, 2 * b + e, :], acc[:])
+                    k = 2 * pair + e
+                    nc.scalar.dma_start(out_0[b, k * P : (k + 1) * P, :], gw[:, 2 * b + e, :])
 
-        def late_bank():
-            return psum.tile([P, N], F32, name="dx_acc", tag="late")
-
-        def wide_bank():
-            return psum.tile([P, N], F32, name="dx_acc", tag="wide", bufs=PACK)
-
-        x_cast(0)
+        x_cast(0, True)
         x_gather(0)
-        gather_dy_both(0)
-        gather_dy(0, 1, 1)
-        gather_dy(1, 1, 1)
-        make_dz(0, 0)
-        make_dz(1, 0)
-        gather_dy(0, 2, 2)
-        make_dz(0, 1)
-        make_dz(1, 1)
-        make_dz(0, 2)
-        gather_dy(0, 3, 2)
-        gather_dy(1, 2, 2)
-        wm_bf0 = [wm_cast(0, half) for half in range(2)]
-        make_dz(0, 3)
-        dzf0 = dz_by_features(0, "dzf0")
-        gather_dy(1, 3, 1)
-        make_dz(1, 2)
-        wm0 = wm_quantize(0, wm_bf0, "wm0")
-        dx0 = [dx_block(wm0, k, dzf0, late_bank(), staging("dx0_%d" % k, 1, 64)[:, 0, :]) for k in range(2)]
-        dz[1, 3] = keep.tile([P, P * PACK], BF16, name="dz1_3", tag="wm_bf0", align_bytes=64)[:]
-        make_dz(1, 3)
-        dzs = dz_by_slots()
-        for k in range(2):
-            scatter(0, k, dx0[k])
-        wm1 = wm_quantize(1, [wm_cast(1, half) for half in range(2)], "wm1")
-        dzf1 = dz_by_features(1, "dx0_0")
-        scatter(0, 2, dx_block(wm0, 2, dzf0, late_bank(), staging("dx0_2")[:, 0, :]))
+        for j in range(PACK):
+            for b in range(B):
+                gather_grad(b, j)
+                if j == 1:
+                    for half in range(2):
+                        weigh(b, 0, half, scalar_scale)
+        weigh(0, 1, 0, scalar_scale)
+        weigh(0, 1, 1, vector_scale)
+        dz_by_features(0, 0, nc.scalar.copy, "slope0")
+        dz_by_features(0, 1, nc.vector.tensor_copy, "slope1")
 
+        first_mx = []
+        for e in range(2):
+            first_bf = sb([P, P * PACK], BF16, "first_bf%d" % e)
+            nc.scalar.copy(*weave(first_bf[:], wm_raw[0, 0][:, :, e * P : (e + 1) * P]))
+            first_mx.append(mx_tiles(P, "first%d" % e))
+            quantize(first_mx[e], slice(0, P), first_bf[:], E4M3)
+        accs = [dx_product(0, first_mx[e], 0, e) for e in range(2)]
+        scatter(0, 0, stage(accs[0], "staged0_0"))
+        for half in range(2):
+            weigh(1, 1, half, scalar_scale, "first1_codes")
+        for half in range(2):
+            dz_by_features(1, half, nc.scalar.copy, "slope%d" % (2 + half))
+        wm10 = wm_half(1, 0, "first_bf1")
+        scatter(0, 1, stage(accs[1], "staged0_1"))
+        accs = [dx_product(1, wm10, e, e) for e in range(2)]
+        wm01 = wm_half(0, 1, "first_bf1")
+        wm11 = wm_half(1, 1, "wm1_0_codes")
         x_cast(1)
+        scatter(1, 0, stage(accs[0], "staged1_0"))
         x_gather(1)
+        dzs = [dz_by_slots(0, "first_bf1")]
+        scatter(1, 1, stage(accs[1], "staged1_1"))
+        dzs.append(dz_by_slots(1, "wm1_0_codes"))
+        x_first = [x_quantize(0, b) for b in range(B)]
         x_cast(2)
-        three = staging("h2", 3)
-        for k in range(2):
-            scatter(1, k, dx_block(wm1, k, dzf1, late_bank(), three[:, k, :]))
-        x_mx = [x_quantize(0, b) for b in range(B)]
-        scatter(1, 2, dx_block(wm1, 2, dzf1, wide_bank(), three[:, 2, :]))
+        scatter(0, 2, dx_block(0, wm01, 0, "staged0_2"))
         x_gather(2)
-        scatter(0, 3, dx_block(wm0, 3, dzf0, wide_bank(), staging("x_bf0")[:, 0, :]))
         x_cast(3)
-        for b in range(B):
-            for k in range(2):
-                gw_block(b, k, x_mx[b], dzs[b], nc.sync)
+        scatter(1, 2, dx_block(1, wm11, 0, "h3"))
         x_gather(3)
-        x_mx = [x_quantize(1, b) for b in range(B)]
-        scatter(1, 3, dx_block(wm1, 3, dzf1, wide_bank(), staging("x_g3", 1, 64)[:, 0, :]))
-        for b in range(B):
-            for k in range(2, PACK):
-                gw_block(b, k, x_mx[b], dzs[b], nc.scalar)
+        x_second = [x_quantize(1, b) for b in range(B)]
+        scatter(0, 3, dx_block(0, wm01, 1, "x_g3"))
+        scatter(1, 3, dx_block(1, wm11, 1, "grad0_1"))
+        gw_blocks(0, x_first, dzs, "dy3")
+        gw_blocks(1, x_second, dzs, "dy1")

@@ -39,6 +39,9 @@ def tile_attend_gex_sig_wx_kernel(tc, xT, dyT, hT, ts, wm, offs, out_0, out_1):
             "staged0_1": 0, "ts_quarter1": 0, "wm_raw1_0": 2 * KIB - 64, "x_bf1": 2 * KIB,
             "staged1_1": 6 * KIB, "wm_raw0_1": 8 * KIB - 64, "x_bf2": 8 * KIB,
             "staged0_2": 12 * KIB, "wm_raw1_1": 14 * KIB - 64, "x_g2": 14 * KIB,
+            "window0": 32 * KIB - 14 * KIB, "x_pool0": 40 * KIB - 64 - 14 * KIB, "window1": 40 * KIB - 14 * KIB,
+            "staged0_0": 34 * KIB, "wm1_0_scales": 34 * KIB,
+            "wm0_1_scales": 0, "staged1_0": 36 * KIB, "wm1_1_scales": 36 * KIB,
         }
 
         def sb(shape, dtype, name, tag=None, bufs=1):
@@ -55,7 +58,7 @@ def tile_attend_gex_sig_wx_kernel(tc, xT, dyT, hT, ts, wm, offs, out_0, out_1):
         ts_pool = sb([P, T], F32, "ts_pool")
         nc.sync.dma_start(ts_pool[TS_ROW:, :], ts[TS_ROW:, :])
         nc.vector.memset(ts_pool[:LAST_QUADRANT, :].bitcast(U32), 0)
-        nc.gpsimd.memset(ts_pool[LAST_QUADRANT:TS_ROW, :].bitcast(U32), 0)
+        nc.vector.memset(ts_pool[LAST_QUADRANT:TS_ROW, :].bitcast(U32), 0)
 
         ident = sb([P, P], F32, "ident")
         make_identity(nc, ident[:])
@@ -76,10 +79,6 @@ def tile_attend_gex_sig_wx_kernel(tc, xT, dyT, hT, ts, wm, offs, out_0, out_1):
         x_pool = {0: load(x_rows[0], [P, T], "x_pool0")}
         dy_pool = [load(dy_rows[j], [P, T], "dy%d" % j) for j in range(PACK)]
 
-        windows = []
-        for k in range(PACK):
-            windows.append(sb([P, T], F32, "window%d" % k))
-            nc.gpsimd.memset(windows[k][:], 0.0)
 
         ts_g = sb([P, B * N], F32, "ts_g")
         nc.vector.tensor_copy(ts_g[:], ts_pool[:].indirect(offsets[:]))
@@ -250,7 +249,7 @@ def tile_attend_gex_sig_wx_kernel(tc, xT, dyT, hT, ts, wm, offs, out_0, out_1):
                 for u in range(2):
                     first = (u * B + b) * P
                     nc.tensor.transpose(bank[:, e, u, :], words[:, first : first + P], ident[:])
-            x_slot = sb([P, 2 * P * PACK], BF16, "x_slot", "grad%d_%d" % (b, pair))
+            x_slot = sb([P, 2 * P * PACK], BF16, "x_slot", "grad%d_%d" % (b, 1 + pair))
             nc.scalar.copy(
                 x_slot[:].bitcast(F32).rearrange("p (e m u) -> p e m u", e=2, u=2),
                 bank[:].rearrange("p e u m -> p e m u"),
@@ -269,14 +268,23 @@ def tile_attend_gex_sig_wx_kernel(tc, xT, dyT, hT, ts, wm, offs, out_0, out_1):
                     k = 2 * pair + e
                     nc.scalar.dma_start(out_0[b, k * P : (k + 1) * P, :], gw[:, 2 * b + e, :])
 
+        windows = []
+
+        def clear_window(tag):
+            windows.append(sb([P, T], F32, "window", tag))
+            nc.gpsimd.memset(windows[-1][:], 0.0)
+
         x_cast(0, True)
         x_gather(0)
+        for tag in ("window0", "window1", "ts_pool"):
+            clear_window(tag)
         for j in range(PACK):
             for b in range(B):
                 gather_grad(b, j)
                 if j == 1:
                     for half in range(2):
                         weigh(b, 0, half, scalar_scale)
+        clear_window("grad0_0")
         weigh(0, 1, 0, scalar_scale)
         weigh(0, 1, 1, vector_scale)
         dz_by_features(0, 0, nc.scalar.copy, "slope0")
@@ -294,15 +302,15 @@ def tile_attend_gex_sig_wx_kernel(tc, xT, dyT, hT, ts, wm, offs, out_0, out_1):
             weigh(1, 1, half, scalar_scale, "first1_codes")
         for half in range(2):
             dz_by_features(1, half, nc.scalar.copy, "slope%d" % (2 + half))
-        wm10 = wm_half(1, 0, "first_bf1")
+        wm10 = wm_half(1, 0, "first1_scales")
         scatter(0, 1, stage(accs[1], "staged0_1"))
         accs = [dx_product(1, wm10, e, e) for e in range(2)]
-        wm01 = wm_half(0, 1, "first_bf1")
-        wm11 = wm_half(1, 1, "wm1_0_codes")
+        wm01 = wm_half(0, 1, "first1_scales")
         x_cast(1)
         scatter(1, 0, stage(accs[0], "staged1_0"))
+        wm11 = wm_half(1, 1, "wm1_0_codes")
         x_gather(1)
-        dzs = [dz_by_slots(0, "first_bf1")]
+        dzs = [dz_by_slots(0, "first1_scales")]
         scatter(1, 1, stage(accs[1], "staged1_1"))
         dzs.append(dz_by_slots(1, "wm1_0_codes"))
         x_first = [x_quantize(0, b) for b in range(B)]
@@ -314,6 +322,6 @@ def tile_attend_gex_sig_wx_kernel(tc, xT, dyT, hT, ts, wm, offs, out_0, out_1):
         x_gather(3)
         x_second = [x_quantize(1, b) for b in range(B)]
         scatter(0, 3, dx_block(0, wm01, 1, "x_g3"))
-        scatter(1, 3, dx_block(1, wm11, 1, "grad0_1"))
+        scatter(1, 3, dx_block(1, wm11, 1, "grad0_2"))
         gw_blocks(0, x_first, dzs, "dy3")
         gw_blocks(1, x_second, dzs, "dy1")

@@ -36,12 +36,11 @@ def tile_attend_gex_sig_wx_kernel(tc, xT, dyT, hT, ts, wm, offs, out_0, out_1):
 
         KIB = 1024
         placed = {
-            "staged0_1": 0, "ts_quarter1": 0, "wm_raw1_0": 2 * KIB - 64, "x_bf1": 2 * KIB,
-            "staged1_1": 6 * KIB, "wm_raw0_1": 8 * KIB - 64, "x_bf2": 8 * KIB,
-            "staged0_2": 12 * KIB, "wm_raw1_1": 14 * KIB - 64, "x_g2": 14 * KIB,
-            "window0": 32 * KIB - 14 * KIB, "x_pool0": 40 * KIB - 64 - 14 * KIB, "window1": 40 * KIB - 14 * KIB,
-            "staged0_0": 34 * KIB, "wm1_0_scales": 34 * KIB,
-            "wm0_1_scales": 0, "staged1_0": 36 * KIB, "wm1_1_scales": 36 * KIB,
+            "ts_quarter1": 0, "staged0_1": 0,
+            "feat1_1": 2 * KIB, "wm_bf1_1": 4 * KIB, "dz_slots0": 3 * KIB,
+            "dy1": 8 * KIB, "dzs0_scales": 8 * KIB, "dzs1_scales": 8 * KIB + 512,
+            "x0_0_scales": 9 * KIB, "x0_1_scales": 9 * KIB + 256,
+            "window0": 16 * KIB, "x_pool0": 24 * KIB - 64, "window1": 24 * KIB,
         }
 
         def sb(shape, dtype, name, tag=None, bufs=1):
@@ -111,10 +110,9 @@ def tile_attend_gex_sig_wx_kernel(tc, xT, dyT, hT, ts, wm, offs, out_0, out_1):
 
         load_wm(0, 0)
         load_wm(1, 0)
-        load_x(1)
         load_wm(0, 1)
         load_wm(1, 1)
-        for k in range(2, PACK):
+        for k in range(1, PACK):
             load_x(k)
 
         def mx_tiles(width, name):
@@ -188,9 +186,9 @@ def tile_attend_gex_sig_wx_kernel(tc, xT, dyT, hT, ts, wm, offs, out_0, out_1):
             )
             quantize(dzf[b], slice(half * HALF, (half + 1) * HALF), feat[:], E5M2)
 
-        def wm_half(b, half, tag):
-            wm_bf = sb([P, HALF * PACK], BF16, "wm_bf", tag)
-            gpsimd_cast(*weave(wm_bf[:], wm_raw[b, half][:]))
+        def wm_half(b, half):
+            wm_bf = sb([P, HALF * PACK], BF16, "wm_bf%d_%d" % (b, half))
+            nc.vector.tensor_copy(*weave(wm_bf[:], wm_raw[b, half][:]))
             mx = mx_tiles(HALF, "wm%d_%d" % (b, half))
             quantize(mx, slice(0, HALF), wm_bf[:], E4M3)
             return mx
@@ -232,7 +230,7 @@ def tile_attend_gex_sig_wx_kernel(tc, xT, dyT, hT, ts, wm, offs, out_0, out_1):
         x_bf = {}
 
         def x_cast(k, on_vector=False):
-            x_bf[k] = sb([P, T], BF16, "x_bf", ("ts_pool", "x_bf1", "x_bf2", "dy3")[k])
+            x_bf[k] = sb([P, T], BF16, "x_bf", ("ts_pool", "dy1", "dy2", "dy3")[k])
             if on_vector:
                 nc.vector.tensor_copy(x_bf[k][:], x_pool[k][:])
             else:
@@ -296,32 +294,30 @@ def tile_attend_gex_sig_wx_kernel(tc, xT, dyT, hT, ts, wm, offs, out_0, out_1):
             nc.scalar.copy(*weave(first_bf[:], wm_raw[0, 0][:, :, e * P : (e + 1) * P]))
             first_mx.append(mx_tiles(P, "first%d" % e))
             quantize(first_mx[e], slice(0, P), first_bf[:], E4M3)
+        wm10 = wm_half(1, 0)
         accs = [dx_product(0, first_mx[e], 0, e) for e in range(2)]
+        wm01 = wm_half(0, 1)
         scatter(0, 0, stage(accs[0], "staged0_0"))
         for half in range(2):
             weigh(1, 1, half, scalar_scale, "first1_codes")
         for half in range(2):
-            dz_by_features(1, half, nc.scalar.copy, "slope%d" % (2 + half))
-        wm10 = wm_half(1, 0, "first1_scales")
+            dz_by_features(1, half, nc.scalar.copy, ("slope2", "feat1_1")[half])
+        wm11 = wm_half(1, 1)
         scatter(0, 1, stage(accs[1], "staged0_1"))
-        accs = [dx_product(1, wm10, e, e) for e in range(2)]
-        wm01 = wm_half(0, 1, "first1_scales")
         x_cast(1)
-        scatter(1, 0, stage(accs[0], "staged1_0"))
-        wm11 = wm_half(1, 1, "wm1_0_codes")
+        scatter(1, 0, stage(dx_product(1, wm10, 0, 0), "h1"))
         x_gather(1)
-        dzs = [dz_by_slots(0, "first1_scales")]
-        scatter(1, 1, stage(accs[1], "staged1_1"))
-        dzs.append(dz_by_slots(1, "wm1_0_codes"))
+        scatter(1, 1, stage(dx_product(1, wm10, 1, 1), "dy1"))
+        dzs = [dz_by_slots(0, "dz_slots0"), dz_by_slots(1, "dz_t0_1")]
         x_first = [x_quantize(0, b) for b in range(B)]
         x_cast(2)
-        scatter(0, 2, dx_block(0, wm01, 0, "staged0_2"))
+        scatter(0, 2, dx_block(0, wm01, 0, "h2"))
         x_gather(2)
+        scatter(1, 2, dx_block(1, wm11, 0, "dy2"))
         x_cast(3)
-        scatter(1, 2, dx_block(1, wm11, 0, "h3"))
+        scatter(0, 3, dx_block(0, wm01, 1, "h3"))
         x_gather(3)
         x_second = [x_quantize(1, b) for b in range(B)]
-        scatter(0, 3, dx_block(0, wm01, 1, "x_g3"))
-        scatter(1, 3, dx_block(1, wm11, 1, "grad0_2"))
+        scatter(1, 3, dx_block(1, wm11, 1, "x_g3"))
         gw_blocks(0, x_first, dzs, "dy3")
-        gw_blocks(1, x_second, dzs, "dy1")
+        gw_blocks(1, x_second, dzs, "dy0")

@@ -36,11 +36,13 @@ def tile_attend_gex_sig_wx_kernel(tc, xT, dyT, hT, ts, wm, offs, out_0, out_1):
 
         KIB = 1024
         placed = {
-            "ts_quarter1": 0, "staged0_1": 0,
-            "feat1_1": 2 * KIB, "wm_bf1_1": 4 * KIB, "dz_slots0": 3 * KIB,
-            "dy1": 8 * KIB, "dzs0_scales": 8 * KIB, "dzs1_scales": 8 * KIB + 512,
-            "x0_0_scales": 9 * KIB, "x0_1_scales": 9 * KIB + 256,
-            "window0": 16 * KIB, "x_pool0": 24 * KIB - 64, "window1": 24 * KIB,
+            "staged0_1": 0, "ts_quarter1": 2 * KIB - 64, "x_bf0": 2 * KIB,
+            "feat1_1": 6 * KIB, "wm_bf1_1": 8 * KIB, "x_bf1": 7 * KIB,
+            "x_g1": 12 * KIB, "dzs0_scales": 12 * KIB, "dzs1_scales": 12 * KIB + 512,
+            "x0_0_scales": 13 * KIB, "x0_1_scales": 13 * KIB + 256,
+            "window0": 14 * KIB, "h3": 22 * KIB - 64, "window1": 22 * KIB,
+            "staged1_2": 38 * KIB, "x_g0": 39 * KIB, "x_g2": 40 * KIB,
+            "h0": 30 * KIB, "staged1_0": 30 * KIB, "staged1_1": 32 * KIB,
         }
 
         def sb(shape, dtype, name, tag=None, bufs=1):
@@ -75,7 +77,6 @@ def tile_attend_gex_sig_wx_kernel(tc, xT, dyT, hT, ts, wm, offs, out_0, out_1):
         dy_rows = dyT.rearrange("(m j) c -> j m c", j=PACK)
         x_rows = xT.rearrange("(k m) c -> k m c", m=P)
         h_pool = [load(h_rows[j], [P, T], "h%d" % j) for j in range(PACK)]
-        x_pool = {0: load(x_rows[0], [P, T], "x_pool0")}
         dy_pool = [load(dy_rows[j], [P, T], "dy%d" % j) for j in range(PACK)]
 
 
@@ -86,8 +87,8 @@ def tile_attend_gex_sig_wx_kernel(tc, xT, dyT, hT, ts, wm, offs, out_0, out_1):
             bank = psum.tile([P, PACK, P], F32, name="ts_bank", tag="fwd%d" % b)
             for t in range(PACK):
                 nc.tensor.transpose(bank[:, t, :], ts_g[:, b * N + t : (b + 1) * N : PACK], ident[:])
-            ts_quarter.append(sb([P, PACK], F32, "ts_quarter%d" % b))
-            nc.scalar.activation(ts_quarter[b][:], bank[:, :, TS_ROW], COPY, scale=0.25)
+            ts_quarter.append(sb([P, 32], F32, "ts_quarter%d" % b))
+            nc.scalar.activation(ts_quarter[b][:, :PACK], bank[:, :, TS_ROW], COPY, scale=0.25)
 
         slope = []
         for j in range(PACK):
@@ -99,18 +100,19 @@ def tile_attend_gex_sig_wx_kernel(tc, xT, dyT, hT, ts, wm, offs, out_0, out_1):
             nc.scalar.activation(slope[j][:], square[:], IDENTITY, bias=one[:], scale=-1.0)
 
         HALF = N // 2
-        wm_raw = {}
+        wm_raw, x_pool = {}, {}
 
         def load_wm(b, half):
             rows = wm[b].rearrange("(m j) d -> m j d", j=PACK)[:, :, half * HALF : (half + 1) * HALF]
             wm_raw[b, half] = load(rows, [P, PACK, HALF], "wm_raw%d_%d" % (b, half))
 
         def load_x(k):
-            x_pool[k] = load(x_rows[k], [P, T], "x_pool%d" % k, "h%d" % k)
+            x_pool[k] = load(x_rows[k], [P, T], "x_pool%d" % k, ("h0", "h1", "h2", "x_pool3")[k])
 
         load_wm(0, 0)
         load_wm(1, 0)
         load_wm(0, 1)
+        load_x(0)
         load_wm(1, 1)
         for k in range(1, PACK):
             load_x(k)
@@ -214,13 +216,16 @@ def tile_attend_gex_sig_wx_kernel(tc, xT, dyT, hT, ts, wm, offs, out_0, out_1):
             if b == B - 1:
                 nc.sync.dma_start(out_1[k * P : (k + 1) * P, :], windows[k][:])
 
-        def dz_by_slots(b, tag):
+        def weave_slots(b, tag):
             slots = sb([P, DV * PACK], BF16, "dz_slots", tag)
             for u in range(2):
                 gpsimd_cast(
                     slots[:].rearrange("p (m u e t) -> p u m e t", u=2, e=2, t=PACK)[:, u],
                     dz_part(b, u, 0, PACK).rearrange("p (t m e) -> p m e t", t=PACK, e=2),
                 )
+            return slots
+
+        def dz_by_slots(b, slots):
             mx = mx_tiles(DV, "dzs%d" % b)
             quantize(mx, slice(0, DV), slots[:], E5M2)
             return mx
@@ -229,18 +234,18 @@ def tile_attend_gex_sig_wx_kernel(tc, xT, dyT, hT, ts, wm, offs, out_0, out_1):
 
         x_bf = {}
 
-        def x_cast(k, on_vector=False):
-            x_bf[k] = sb([P, T], BF16, "x_bf", ("ts_pool", "dy1", "dy2", "dy3")[k])
-            if on_vector:
-                nc.vector.tensor_copy(x_bf[k][:], x_pool[k][:])
-            else:
+        def x_cast(k, tag):
+            x_bf[k] = sb([P, T], BF16, "x_bf", tag)
+            if k == 0:
                 nc.scalar.activation(x_bf[k][:], x_pool[k][:], COPY)
+            else:
+                nc.gpsimd.tensor_copy(x_bf[k][:], x_pool[k][:])
 
         def x_gather(k):
             x_g[k] = sb([P, 2, B * P, 2], BF16, "x_g%d" % k)
             nc.scalar.activation(x_g[k][:].rearrange("p u s e -> p s u e"), x_bf[k][:].indirect(offsets[:]), COPY)
 
-        def x_quantize(pair, b):
+        def x_weave(pair, b):
             bank = psum.tile([P, 2, 2, P], F32, name="x_bank", tag="back%d" % b)
             for e in range(2):
                 words = x_g[2 * pair + e][:].rearrange("p u s e -> p (u s e)").bitcast(F32)
@@ -252,6 +257,9 @@ def tile_attend_gex_sig_wx_kernel(tc, xT, dyT, hT, ts, wm, offs, out_0, out_1):
                 x_slot[:].bitcast(F32).rearrange("p (e m u) -> p e m u", e=2, u=2),
                 bank[:].rearrange("p e u m -> p e m u"),
             )
+            return x_slot
+
+        def x_quantize(pair, b, x_slot):
             mx = mx_tiles(2 * P, "x%d_%d" % (pair, b))
             quantize(mx, slice(0, 2 * P), x_slot[:], E4M3)
             return mx
@@ -272,9 +280,7 @@ def tile_attend_gex_sig_wx_kernel(tc, xT, dyT, hT, ts, wm, offs, out_0, out_1):
             windows.append(sb([P, T], F32, "window", tag))
             nc.gpsimd.memset(windows[-1][:], 0.0)
 
-        x_cast(0, True)
-        x_gather(0)
-        for tag in ("window0", "window1", "ts_pool"):
+        for tag in ("window0", "window1"):
             clear_window(tag)
         for j in range(PACK):
             for b in range(B):
@@ -282,7 +288,8 @@ def tile_attend_gex_sig_wx_kernel(tc, xT, dyT, hT, ts, wm, offs, out_0, out_1):
                 if j == 1:
                     for half in range(2):
                         weigh(b, 0, half, scalar_scale)
-        clear_window("grad0_0")
+        for tag in ("grad0_0", "grad1_0"):
+            clear_window(tag)
         weigh(0, 1, 0, scalar_scale)
         weigh(0, 1, 1, vector_scale)
         dz_by_features(0, 0, nc.scalar.copy, "slope0")
@@ -304,20 +311,25 @@ def tile_attend_gex_sig_wx_kernel(tc, xT, dyT, hT, ts, wm, offs, out_0, out_1):
             dz_by_features(1, half, nc.scalar.copy, ("slope2", "feat1_1")[half])
         wm11 = wm_half(1, 1)
         scatter(0, 1, stage(accs[1], "staged0_1"))
-        x_cast(1)
-        scatter(1, 0, stage(dx_product(1, wm10, 0, 0), "h1"))
+        x_cast(0, "x_bf0")
+        scatter(1, 0, stage(dx_product(1, wm10, 0, 0), "staged1_0"))
+        scatter(1, 1, stage(dx_product(1, wm10, 1, 1), "staged1_1"))
+        x_gather(0)
+        x_cast(1, "x_bf1")
+        x_cast(2, "h1")
+        slots = [weave_slots(0, "h2")]
+        x_cast(3, "dz_t0_1")
+        slots.append(weave_slots(1, "x_pool3"))
         x_gather(1)
-        scatter(1, 1, stage(dx_product(1, wm10, 1, 1), "dy1"))
-        dzs = [dz_by_slots(0, "dz_slots0"), dz_by_slots(1, "dz_t0_1")]
-        x_first = [x_quantize(0, b) for b in range(B)]
-        x_cast(2)
-        scatter(0, 2, dx_block(0, wm01, 0, "h2"))
+        x_woven = [x_weave(0, b) for b in range(B)]
+        scatter(0, 2, dx_block(0, wm01, 0, "x_g1"))
+        dzs = [dz_by_slots(b, slots[b]) for b in range(B)]
+        x_first = [x_quantize(0, b, x_woven[b]) for b in range(B)]
+        scatter(1, 2, dx_block(1, wm11, 0, "staged1_2"))
         x_gather(2)
-        scatter(1, 2, dx_block(1, wm11, 0, "dy2"))
-        x_cast(3)
-        scatter(0, 3, dx_block(0, wm01, 1, "h3"))
         x_gather(3)
-        x_second = [x_quantize(1, b) for b in range(B)]
-        scatter(1, 3, dx_block(1, wm11, 1, "x_g3"))
-        gw_blocks(0, x_first, dzs, "dy3")
+        x_second = [x_quantize(1, b, x_weave(1, b)) for b in range(B)]
+        scatter(0, 3, dx_block(0, wm01, 1, "x_g3"))
+        scatter(1, 3, dx_block(1, wm11, 1, "staged0_0"))
+        gw_blocks(0, x_first, dzs, "dz_t0_1")
         gw_blocks(1, x_second, dzs, "dy0")

@@ -21,9 +21,12 @@ IDENTITY = mybir.ActivationFunctionType.Identity
 
 P = 128
 PACK = 4
-LIST_COLS = N // 16
-LAST_QUADRANT = 96
+HALF = N // 2
+GROUP = 16
+ALIGN = 64
+KIB = 1024
 TS_ROW = P - 1
+LAST_QUADRANT = 96
 
 
 def tile_attend_gex_sig_wx_kernel(tc, xT, dyT, hT, ts, wm, offs, out_0, out_1):
@@ -34,27 +37,27 @@ def tile_attend_gex_sig_wx_kernel(tc, xT, dyT, hT, ts, wm, offs, out_0, out_1):
         relay = ctx.enter_context(tc.tile_pool(name="relay", bufs=1))
         psum = ctx.enter_context(tc.psum_pool(name="psum", bufs=1))
 
-        KIB = 1024
         placed = {
-            "staged0_1": 0, "ts_quarter1": 2 * KIB - 64, "x_bf0": 2 * KIB,
+            "ts_quarter1": 2 * KIB - ALIGN, "staged0_1": 0, "x_bf0": 2 * KIB,
             "feat1_1": 6 * KIB, "wm_bf1_1": 8 * KIB, "x_bf1": 7 * KIB,
-            "x_g1": 12 * KIB, "dzs0_scales": 12 * KIB, "dzs1_scales": 12 * KIB + 512,
-            "x0_0_scales": 13 * KIB, "x0_1_scales": 13 * KIB + 256,
-            "window0": 14 * KIB, "h3": 22 * KIB - 64, "window1": 22 * KIB,
-            "staged1_2": 38 * KIB, "x_g0": 39 * KIB, "x_g2": 40 * KIB,
+            "x_g1": 12 * KIB, "dzs0_scales": 12 * KIB, "dzs1_scales": 12 * KIB + DV,
+            "x0_0_scales": 13 * KIB, "x0_1_scales": 13 * KIB + 2 * P,
+            "h3": 22 * KIB - ALIGN, "window0": 14 * KIB, "window1": 22 * KIB,
             "h0": 30 * KIB, "staged1_0": 30 * KIB, "staged1_1": 32 * KIB,
+            "x_g0": 39 * KIB, "staged1_2": 38 * KIB, "x_g2": 40 * KIB,
         }
 
-        def sb(shape, dtype, name, tag=None, bufs=1):
-            if (tag or name) in placed:
-                return relay.tile(shape, dtype, name=name, tag=tag or name, align_bytes=64, offset=placed[tag or name])
-            return keep.tile(shape, dtype, name=name, tag=tag or name, bufs=bufs, align_bytes=64)
+        def sb(shape, dtype, name, after=None, bufs=1):
+            tag = after or name
+            if tag in placed:
+                return relay.tile(shape, dtype, name=name, tag=tag, align_bytes=ALIGN, offset=placed[tag])
+            return keep.tile(shape, dtype, name=name, tag=tag, bufs=bufs, align_bytes=ALIGN)
 
-        offsets = lists.tile([P, B * LIST_COLS], U16, name="offsets")
+        offsets = lists.tile([P, B * N // GROUP], U16, name="offsets")
         nc.sync.dma_start(offsets[:], offs)
 
         def entries(first, count):
-            return offsets[:, first // 16 : (first + count) // 16]
+            return offsets[:, first // GROUP : (first + count) // GROUP]
 
         ts_pool = sb([P, T], F32, "ts_pool")
         nc.sync.dma_start(ts_pool[TS_ROW:, :], ts[TS_ROW:, :])
@@ -68,8 +71,8 @@ def tile_attend_gex_sig_wx_kernel(tc, xT, dyT, hT, ts, wm, offs, out_0, out_1):
         one = sb([P, 1], F32, "one")
         nc.scalar.activation(one[:], minus_one[:], SQUARE)
 
-        def load(rows, shape, name, tag=None):
-            raw = sb(shape, F32, name, tag)
+        def load(rows, shape, name, after=None):
+            raw = sb(shape, F32, name, after)
             nc.sync.dma_start(raw[:], rows)
             return raw
 
@@ -79,15 +82,14 @@ def tile_attend_gex_sig_wx_kernel(tc, xT, dyT, hT, ts, wm, offs, out_0, out_1):
         h_pool = [load(h_rows[j], [P, T], "h%d" % j) for j in range(PACK)]
         dy_pool = [load(dy_rows[j], [P, T], "dy%d" % j) for j in range(PACK)]
 
-
         ts_g = sb([P, B * N], F32, "ts_g")
         nc.vector.tensor_copy(ts_g[:], ts_pool[:].indirect(offsets[:]))
         ts_quarter = []
         for b in range(B):
-            bank = psum.tile([P, PACK, P], F32, name="ts_bank", tag="fwd%d" % b)
+            bank = psum.tile([P, PACK, P], F32, name="ts_bank", tag="low%d" % b)
             for t in range(PACK):
                 nc.tensor.transpose(bank[:, t, :], ts_g[:, b * N + t : (b + 1) * N : PACK], ident[:])
-            ts_quarter.append(sb([P, 32], F32, "ts_quarter%d" % b))
+            ts_quarter.append(sb([P, 2 * ALIGN // 4], F32, "ts_quarter%d" % b))
             nc.scalar.activation(ts_quarter[b][:, :PACK], bank[:, :, TS_ROW], COPY, scale=0.25)
 
         slope = []
@@ -99,23 +101,12 @@ def tile_attend_gex_sig_wx_kernel(tc, xT, dyT, hT, ts, wm, offs, out_0, out_1):
             slope.append(sb([P, B * N], F32, "slope%d" % j))
             nc.scalar.activation(slope[j][:], square[:], IDENTITY, bias=one[:], scale=-1.0)
 
-        HALF = N // 2
-        wm_raw, x_pool = {}, {}
-
-        def load_wm(b, half):
-            rows = wm[b].rearrange("(m j) d -> m j d", j=PACK)[:, :, half * HALF : (half + 1) * HALF]
-            wm_raw[b, half] = load(rows, [P, PACK, HALF], "wm_raw%d_%d" % (b, half))
-
-        def load_x(k):
-            x_pool[k] = load(x_rows[k], [P, T], "x_pool%d" % k, ("h0", "h1", "h2", "x_pool3")[k])
-
-        load_wm(0, 0)
-        load_wm(1, 0)
-        load_wm(0, 1)
-        load_x(0)
-        load_wm(1, 1)
-        for k in range(1, PACK):
-            load_x(k)
+        wm_raw = {}
+        for half in range(2):
+            for b in range(B):
+                rows = wm[b].rearrange("(m j) d -> m j d", j=PACK)[:, :, half * HALF : (half + 1) * HALF]
+                wm_raw[b, half] = load(rows, [P, PACK, HALF], "wm_raw%d_%d" % (b, half))
+        x_pool = [load(x_rows[k], [P, T], "x_pool%d" % k, ("h0", "h1", "h2", None)[k]) for k in range(PACK)]
 
         def mx_tiles(width, name):
             return sb([P, width], U32, name + "_codes"), sb([P, width], U8, name + "_scales")
@@ -134,55 +125,42 @@ def tile_attend_gex_sig_wx_kernel(tc, xT, dyT, hT, ts, wm, offs, out_0, out_1):
                 stop=True,
             )
 
-        def weave(dst, src):
-            return (
-                dst.rearrange("p (a e j) -> p a j e", e=PACK, j=PACK),
-                src.rearrange("p j (a e) -> p a j e", e=PACK),
-            )
-
-        def gpsimd_cast(dst, src):
-            nc.gpsimd.tensor_scalar(dst, src, 1.0, 0.0, MULT, ADD)
-
         dzf = [mx_tiles(N, "dzf%d" % b) for b in range(B)]
-        grad, fwd, back = {}, {}, {}
-        dz_t = {}
+        grad, fwd, back, dz_t = {}, {}, {}, {}
 
         def dz_part(b, u, t, count=1):
             return dz_t[b, u][:, t * 2 * P : (t + count) * 2 * P]
 
-
         def gather_grad(b, j):
             grad[b, j] = sb([P, N], F32, "grad%d_%d" % (b, j))
-            nc.vector.tensor_tensor(grad[b, j][:], dy_pool[j][:].indirect(entries(b * N, N)), slope[j][:, b * N : (b + 1) * N], MULT)
+            nc.vector.tensor_tensor(
+                grad[b, j][:], dy_pool[j][:].indirect(entries(b * N, N)), slope[j][:, b * N : (b + 1) * N], MULT
+            )
             for t in range(PACK):
                 if j % 2 == 0 and t % 2 == 0:
-                    fwd[b, t // 2] = psum.tile([P, 2, 2, P], F32, name="fwd", tag="fwd%d" % (2 * b + t // 2))
+                    tag = "%s%d" % (("low", "high")[j // 2], 2 * b + t // 2)
+                    fwd[b, t // 2] = psum.tile([P, 2, 2, P], F32, name="fwd", tag=tag)
                 nc.tensor.transpose(fwd[b, t // 2][:, t % 2, j % 2, :], grad[b, j][:, t::PACK], ident[:])
 
-        def scalar_scale(dst, src, factor):
-            nc.scalar.activation(dst, src, COPY, scale=factor)
-
-        def vector_scale(dst, src, factor):
-            nc.vector.tensor_scalar(dst, src, factor, None, MULT)
-
-        def weigh(b, u, half, scale, tag=None):
+        def weigh(b, u, half, after=None):
             if half == 0:
-                dz_t[b, u] = sb([P, PACK * 2 * P], BF16, "dz_t%d_%d" % (b, u), tag)
-            if u == 0:
-                back[b, half] = psum.tile([P, 2, 2, P], F32, name="back", tag="back%d" % (2 * b + half))
+                dz_t[b, u] = sb([P, PACK * 2 * P], BF16, "dz_t%d_%d" % (b, u), after)
             for i in range(2):
                 t = 2 * half + i
-                scale(
+                nc.scalar.activation(
                     dz_part(b, u, t).rearrange("p (m e) -> p m e", e=2),
                     fwd[b, half][:, i].rearrange("p e m -> p m e"),
-                    ts_quarter[b][:, t : t + 1],
+                    COPY,
+                    scale=ts_quarter[b][:, t : t + 1],
                 )
+            if u == 0:
+                back[b, half] = psum.tile([P, 2, 2, P], F32, name="back", tag="low%d" % (2 * b + half))
             for i in range(2):
                 nc.tensor.transpose(back[b, half][:, i, u, :], dz_part(b, u, 2 * half + i).bitcast(F32), ident[:])
 
-        def dz_by_features(b, half, copy, tag):
-            feat = sb([P, HALF * PACK], BF16, "feat", tag)
-            copy(
+        def dz_by_features(b, half, after):
+            feat = sb([P, HALF * PACK], BF16, "feat", after)
+            nc.scalar.copy(
                 feat[:].bitcast(F32).rearrange("p (s i u) -> p s i u", i=2, u=2),
                 back[b, half][:].rearrange("p i u s -> p s i u"),
             )
@@ -190,38 +168,52 @@ def tile_attend_gex_sig_wx_kernel(tc, xT, dyT, hT, ts, wm, offs, out_0, out_1):
 
         def wm_half(b, half):
             wm_bf = sb([P, HALF * PACK], BF16, "wm_bf%d_%d" % (b, half))
-            nc.vector.tensor_copy(*weave(wm_bf[:], wm_raw[b, half][:]))
+            nc.vector.tensor_copy(
+                wm_bf[:].rearrange("p (a c j) -> p a j c", c=PACK, j=PACK),
+                wm_raw[b, half][:].rearrange("p j (a c) -> p a j c", c=PACK),
+            )
             mx = mx_tiles(HALF, "wm%d_%d" % (b, half))
             quantize(mx, slice(0, HALF), wm_bf[:], E4M3)
             return mx
 
         def dx_product(b, wm_mx, e, bank):
-            acc = psum.tile([P, N], F32, name="dx_acc", tag="fwd%d" % bank)
+            acc = psum.tile([P, N], F32, name="dx_acc", tag="high%d" % bank)
             product(acc, wm_mx, e, dzf[b])
             return acc
 
-        def dx_block(b, wm_mx, e, tag):
-            return stage(dx_product(b, wm_mx, e, b), tag)
-
-        def stage(acc, tag):
-            staged = sb([P, N], F32, "staged", tag)
+        def unpermute(staged, acc, first=0, count=P):
+            rows = slice(first, first + count)
             nc.scalar.copy(
-                staged[:].rearrange("p (s h i) -> p s h i", h=2, i=2),
-                acc[:].rearrange("p (h s i) -> p s h i", h=2, i=2),
+                staged.rearrange("p (s h i) -> p s h i", h=2, i=2)[:, rows],
+                acc[:].rearrange("p (h s i) -> p s h i", h=2, i=2)[:, rows],
             )
-            return staged
 
-        def scatter(b, k, staged):
+        windows = []
+
+        def clear_window(after):
+            windows.append(sb([P, T], F32, "window", after))
+            nc.gpsimd.memset(windows[-1][:], 0.0)
+
+        def store_window(k):
+            nc.sync.dma_start(out_1[k * P : (k + 1) * P, :], windows[k][:])
+
+        def scatter(b, k, acc, after):
+            staged = sb([P, N], F32, "staged", after)
+            unpermute(staged[:], acc)
             nc.vector.tensor_copy(windows[k][:].indirect(entries(b * N, N)), staged[:])
             if b == B - 1:
-                nc.sync.dma_start(out_1[k * P : (k + 1) * P, :], windows[k][:])
+                store_window(k)
 
-        def weave_slots(b, tag):
-            slots = sb([P, DV * PACK], BF16, "dz_slots", tag)
+        def weave_slots(b, after):
+            slots = sb([P, DV * PACK], BF16, "dz_slots", after)
             for u in range(2):
-                gpsimd_cast(
+                nc.gpsimd.tensor_scalar(
                     slots[:].rearrange("p (m u e t) -> p u m e t", u=2, e=2, t=PACK)[:, u],
                     dz_part(b, u, 0, PACK).rearrange("p (t m e) -> p m e t", t=PACK, e=2),
+                    1.0,
+                    0.0,
+                    MULT,
+                    ADD,
                 )
             return slots
 
@@ -230,12 +222,10 @@ def tile_attend_gex_sig_wx_kernel(tc, xT, dyT, hT, ts, wm, offs, out_0, out_1):
             quantize(mx, slice(0, DV), slots[:], E5M2)
             return mx
 
-        x_g = {}
+        x_bf, x_g = {}, {}
 
-        x_bf = {}
-
-        def x_cast(k, tag):
-            x_bf[k] = sb([P, T], BF16, "x_bf", tag)
+        def x_cast(k, after):
+            x_bf[k] = sb([P, T], BF16, "x_bf", after)
             if k == 0:
                 nc.scalar.activation(x_bf[k][:], x_pool[k][:], COPY)
             else:
@@ -243,19 +233,19 @@ def tile_attend_gex_sig_wx_kernel(tc, xT, dyT, hT, ts, wm, offs, out_0, out_1):
 
         def x_gather(k):
             x_g[k] = sb([P, 2, B * P, 2], BF16, "x_g%d" % k)
-            nc.scalar.activation(x_g[k][:].rearrange("p u s e -> p s u e"), x_bf[k][:].indirect(offsets[:]), COPY)
+            nc.scalar.activation(x_g[k][:].rearrange("p v s w -> p s v w"), x_bf[k][:].indirect(offsets[:]), COPY)
 
         def x_weave(pair, b):
-            bank = psum.tile([P, 2, 2, P], F32, name="x_bank", tag="back%d" % b)
-            for e in range(2):
-                words = x_g[2 * pair + e][:].rearrange("p u s e -> p (u s e)").bitcast(F32)
-                for u in range(2):
-                    first = (u * B + b) * P
-                    nc.tensor.transpose(bank[:, e, u, :], words[:, first : first + P], ident[:])
+            bank = psum.tile([P, 2, 2, P], F32, name="x_bank", tag="low%d" % b)
+            for i in range(2):
+                words = x_g[2 * pair + i][:].rearrange("p v s w -> p (v s w)").bitcast(F32)
+                for v in range(2):
+                    first = (v * B + b) * P
+                    nc.tensor.transpose(bank[:, i, v, :], words[:, first : first + P], ident[:])
             x_slot = sb([P, 2 * P * PACK], BF16, "x_slot", "grad%d_%d" % (b, 1 + pair))
             nc.scalar.copy(
-                x_slot[:].bitcast(F32).rearrange("p (e m u) -> p e m u", e=2, u=2),
-                bank[:].rearrange("p e u m -> p e m u"),
+                x_slot[:].bitcast(F32).rearrange("p (i d v) -> p i d v", i=2, v=2),
+                bank[:].rearrange("p i v d -> p i d v"),
             )
             return x_slot
 
@@ -264,72 +254,76 @@ def tile_attend_gex_sig_wx_kernel(tc, xT, dyT, hT, ts, wm, offs, out_0, out_1):
             quantize(mx, slice(0, 2 * P), x_slot[:], E4M3)
             return mx
 
-        def gw_blocks(pair, x_mx, dzs, tag):
-            gw = sb([P, PACK, DV], F32, "gw", tag)
+        def gw_blocks(pair, x_mx, dzs, banks, after):
+            gw = sb([P, PACK, DV], F32, "gw", after)
             for b in range(B):
-                for e in range(2):
-                    acc = psum.tile([P, DV], F32, name="gw_acc", tag=("fwd2", "fwd3", "back2", "back3")[2 * b + e])
-                    product(acc, x_mx[b], e, dzs[b])
-                    nc.scalar.copy(gw[:, 2 * b + e, :], acc[:])
-                    k = 2 * pair + e
-                    nc.scalar.dma_start(out_0[b, k * P : (k + 1) * P, :], gw[:, 2 * b + e, :])
+                for i in range(2):
+                    acc = psum.tile([P, DV], F32, name="gw_acc", tag=banks[2 * b + i])
+                    product(acc, x_mx[b], i, dzs[b])
+                    nc.scalar.copy(gw[:, 2 * b + i, :], acc[:])
+                rows = out_0[b, 2 * pair * P : 2 * (pair + 1) * P, :].rearrange("(i p) n -> p i n", i=2)
+                nc.scalar.dma_start(rows, gw[:, 2 * b : 2 * b + 2, :])
 
-        windows = []
-
-        def clear_window(tag):
-            windows.append(sb([P, T], F32, "window", tag))
-            nc.gpsimd.memset(windows[-1][:], 0.0)
-
-        for tag in ("window0", "window1"):
-            clear_window(tag)
+        for after in ("window0", "window1"):
+            clear_window(after)
         for j in range(PACK):
             for b in range(B):
                 gather_grad(b, j)
                 if j == 1:
                     for half in range(2):
-                        weigh(b, 0, half, scalar_scale)
-        for tag in ("grad0_0", "grad1_0"):
-            clear_window(tag)
-        weigh(0, 1, 0, scalar_scale)
-        weigh(0, 1, 1, vector_scale)
-        dz_by_features(0, 0, nc.scalar.copy, "slope0")
-        dz_by_features(0, 1, nc.vector.tensor_copy, "slope1")
+                        weigh(b, 0, half)
+        for after in ("grad0_0", "grad1_0"):
+            clear_window(after)
 
-        first_mx = []
-        for e in range(2):
-            first_bf = sb([P, P * PACK], BF16, "first_bf%d" % e)
-            nc.scalar.copy(*weave(first_bf[:], wm_raw[0, 0][:, :, e * P : (e + 1) * P]))
-            first_mx.append(mx_tiles(P, "first%d" % e))
-            quantize(first_mx[e], slice(0, P), first_bf[:], E4M3)
+        wm00 = wm_half(0, 0)
+        for half in range(2):
+            weigh(0, 1, half)
+        for half in range(2):
+            dz_by_features(0, half, "slope%d" % half)
+        first_accs = [dx_product(0, wm00, e, e) for e in range(2)]
         wm10 = wm_half(1, 0)
-        accs = [dx_product(0, first_mx[e], 0, e) for e in range(2)]
         wm01 = wm_half(0, 1)
-        scatter(0, 0, stage(accs[0], "staged0_0"))
-        for half in range(2):
-            weigh(1, 1, half, scalar_scale, "first1_codes")
-        for half in range(2):
-            dz_by_features(1, half, nc.scalar.copy, ("slope2", "feat1_1")[half])
         wm11 = wm_half(1, 1)
-        scatter(0, 1, stage(accs[1], "staged0_1"))
+
+        first_staged = sb([P, N], F32, "staged0_0")
+        for half in range(2):
+            unpermute(first_staged[:], first_accs[0], half * P // 2, P // 2)
+            nc.vector.tensor_copy(
+                windows[0][:].indirect(entries(half * HALF, HALF)), first_staged[:, half * HALF : (half + 1) * HALF]
+            )
+
+        for half in range(2):
+            weigh(1, 1, half, "wm0_0_codes")
+        for half in range(2):
+            dz_by_features(1, half, ("slope2", "feat1_1")[half])
+        scatter(0, 1, first_accs[1], "staged0_1")
         x_cast(0, "x_bf0")
-        scatter(1, 0, stage(dx_product(1, wm10, 0, 0), "staged1_0"))
-        scatter(1, 1, stage(dx_product(1, wm10, 1, 1), "staged1_1"))
+        for k in range(2):
+            scatter(1, k, dx_product(1, wm10, k, k), "staged1_%d" % k)
         x_gather(0)
+
         x_cast(1, "x_bf1")
         x_cast(2, "h1")
         slots = [weave_slots(0, "h2")]
         x_cast(3, "dz_t0_1")
         slots.append(weave_slots(1, "x_pool3"))
+
         x_gather(1)
         x_woven = [x_weave(0, b) for b in range(B)]
-        scatter(0, 2, dx_block(0, wm01, 0, "x_g1"))
+        scatter(0, 2, dx_product(0, wm01, 0, 0), "x_g1")
         dzs = [dz_by_slots(b, slots[b]) for b in range(B)]
         x_first = [x_quantize(0, b, x_woven[b]) for b in range(B)]
-        scatter(1, 2, dx_block(1, wm11, 0, "staged1_2"))
+        scatter(1, 2, dx_product(1, wm11, 0, 1), "staged1_2")
         x_gather(2)
         x_gather(3)
         x_second = [x_quantize(1, b, x_weave(1, b)) for b in range(B)]
-        scatter(0, 3, dx_block(0, wm01, 1, "x_g3"))
-        scatter(1, 3, dx_block(1, wm11, 1, "staged0_0"))
-        gw_blocks(0, x_first, dzs, "dz_t0_1")
-        gw_blocks(1, x_second, dzs, "dy0")
+
+        last = PACK - 1
+        last_staged = sb([P, B * N], F32, "staged_last", "x_g3")
+        for b, wm_mx in enumerate((wm01, wm11)):
+            unpermute(last_staged[:, b * N : (b + 1) * N], dx_product(b, wm_mx, 1, b))
+        nc.vector.tensor_copy(windows[last][:].indirect(offsets[:]), last_staged[:])
+        store_window(last)
+
+        gw_blocks(0, x_first, dzs, ("low0", "low1", "low0", "low1"), "dy1")
+        gw_blocks(1, x_second, dzs, ("low2", "low3", "high2", "high3"), "dy0")

@@ -26,7 +26,6 @@ GROUP = 16
 ALIGN = 64
 KIB = 1024
 TS_ROW = P - 1
-LAST_QUADRANT = 96
 
 
 def tile_attend_gex_sig_wx_kernel(tc, xT, dyT, hT, ts, wm, offs, out_0, out_1):
@@ -61,8 +60,7 @@ def tile_attend_gex_sig_wx_kernel(tc, xT, dyT, hT, ts, wm, offs, out_0, out_1):
 
         ts_pool = sb([P, T], F32, "ts_pool")
         nc.sync.dma_start(ts_pool[TS_ROW:, :], ts[TS_ROW:, :])
-        nc.vector.memset(ts_pool[:LAST_QUADRANT, :].bitcast(U32), 0)
-        nc.vector.memset(ts_pool[LAST_QUADRANT:TS_ROW, :].bitcast(U32), 0)
+        nc.vector.memset(ts_pool[:TS_ROW, :].bitcast(U32), 0)
 
         ident = sb([P, P], F32, "ident")
         make_identity(nc, ident[:])

@@ -37,13 +37,9 @@ def tile_attend_gex_sig_wx_kernel(tc, xT, dyT, hT, ts, wm, offs, out_0, out_1):
         psum = ctx.enter_context(tc.psum_pool(name="psum", bufs=1))
 
         placed = {
-            "ts_quarter1": 2 * KIB - ALIGN, "staged0_1": 0, "x_bf0": 2 * KIB,
-            "feat1_1": 6 * KIB, "wm_bf1_1": 8 * KIB, "x_bf1": 7 * KIB,
-            "x_g1": 12 * KIB, "dzs0_scales": 12 * KIB, "dzs1_scales": 12 * KIB + DV,
-            "x0_0_scales": 13 * KIB, "x0_1_scales": 13 * KIB + 2 * P,
+            "wm_raw1": 0, "staged0_0": 0, "staged0_1": 2 * KIB, "staged0_2": 4 * KIB, "staged1_0": 6 * KIB,
+            "feat1_1": 8 * KIB, "wm_bf1": 10 * KIB, "x_bf0": 9 * KIB,
             "h3": 22 * KIB - ALIGN, "window0": 14 * KIB, "window1": 22 * KIB,
-            "h0": 30 * KIB, "staged1_0": 30 * KIB, "staged1_1": 32 * KIB,
-            "x_g0": 39 * KIB, "staged1_2": 38 * KIB, "x_g2": 40 * KIB,
         }
 
         def sb(shape, dtype, name, after=None, bufs=1):
@@ -87,23 +83,23 @@ def tile_attend_gex_sig_wx_kernel(tc, xT, dyT, hT, ts, wm, offs, out_0, out_1):
             bank = psum.tile([P, PACK, P], F32, name="ts_bank", tag="low%d" % b)
             for t in range(PACK):
                 nc.tensor.transpose(bank[:, t, :], ts_g[:, b * N + t : (b + 1) * N : PACK], ident[:])
-            ts_quarter.append(sb([P, 2 * ALIGN // 4], F32, "ts_quarter%d" % b))
-            nc.scalar.activation(ts_quarter[b][:, :PACK], bank[:, :, TS_ROW], COPY, scale=0.25)
+            ts_quarter.append(sb([P, PACK], F32, "ts_quarter%d" % b))
+            nc.scalar.activation(ts_quarter[b][:], bank[:, :, TS_ROW], COPY, scale=0.25)
 
-        slope = []
+        slope = {}
         for j in range(PACK):
             h_g = sb([P, B * N], F32, "h_g", bufs=2)
             nc.vector.tensor_copy(h_g[:], h_pool[j][:].indirect(offsets[:]))
             square = sb([P, B * N], F32, "square", bufs=2)
             nc.scalar.activation(square[:], h_g[:], SQUARE, bias=one[:], scale=-2.0)
-            slope.append(sb([P, B * N], F32, "slope%d" % j))
-            nc.scalar.activation(slope[j][:], square[:], IDENTITY, bias=one[:], scale=-1.0)
+            pieces = [(0, B * N)] if j < PACK - 1 else [(0, HALF), (HALF, HALF), (N, N)]
+            for first, count in pieces:
+                slope[j, first] = sb([P, count], F32, "slope%d_%d" % (j, first))
+                nc.scalar.activation(
+                    slope[j, first][:], square[:, first : first + count], IDENTITY, bias=one[:], scale=-1.0
+                )
 
-        wm_raw = {}
-        for half in range(2):
-            for b in range(B):
-                rows = wm[b].rearrange("(m j) d -> m j d", j=PACK)[:, :, half * HALF : (half + 1) * HALF]
-                wm_raw[b, half] = load(rows, [P, PACK, HALF], "wm_raw%d_%d" % (b, half))
+        wm_raw = [load(wm[b].rearrange("(m j) d -> m j d", j=PACK), [P, PACK, D], "wm_raw%d" % b) for b in range(B)]
         x_pool = [load(x_rows[k], [P, T], "x_pool%d" % k, ("h0", "h1", "h2", None)[k]) for k in range(PACK)]
 
         def mx_tiles(width, name):
@@ -129,14 +125,23 @@ def tile_attend_gex_sig_wx_kernel(tc, xT, dyT, hT, ts, wm, offs, out_0, out_1):
         def dz_part(b, u, t, count=1):
             return dz_t[b, u][:, t * 2 * P : (t + count) * 2 * P]
 
-        def gather_grad(b, j):
-            grad[b, j] = sb([P, N], F32, "grad%d_%d" % (b, j))
-            nc.vector.tensor_tensor(
-                grad[b, j][:], dy_pool[j][:].indirect(entries(b * N, N)), slope[j][:, b * N : (b + 1) * N], MULT
-            )
+        def gather_grad(b, j, after=None):
+            grad[b, j] = sb([P, N], F32, "grad%d_%d" % (b, j), after)
+            if j < PACK - 1:
+                pieces = [(b * N, slope[j, 0][:, b * N : (b + 1) * N])]
+            else:
+                pieces = [(first, slope[j, first][:]) for first in ((0, HALF), (N,))[b]]
+            for first, factor in pieces:
+                count = factor.shape[1]
+                nc.vector.tensor_tensor(
+                    grad[b, j][:, first - b * N : first - b * N + count],
+                    dy_pool[j][:].indirect(entries(first, count)),
+                    factor,
+                    MULT,
+                )
             for t in range(PACK):
                 if j % 2 == 0 and t % 2 == 0:
-                    tag = "%s%d" % (("low", "high")[j // 2], 2 * b + t // 2)
+                    tag = "low%d" % (2 * b + t // 2) if j == 0 else "high%d" % (t // 2)
                     fwd[b, t // 2] = psum.tile([P, 2, 2, P], F32, name="fwd", tag=tag)
                 nc.tensor.transpose(fwd[b, t // 2][:, t % 2, j % 2, :], grad[b, j][:, t::PACK], ident[:])
 
@@ -164,26 +169,22 @@ def tile_attend_gex_sig_wx_kernel(tc, xT, dyT, hT, ts, wm, offs, out_0, out_1):
             )
             quantize(dzf[b], slice(half * HALF, (half + 1) * HALF), feat[:], E5M2)
 
-        def wm_half(b, half):
-            wm_bf = sb([P, HALF * PACK], BF16, "wm_bf%d_%d" % (b, half))
+        def wm_operand(b):
+            wm_bf = sb([P, D * PACK], BF16, "wm_bf%d" % b)
             nc.vector.tensor_copy(
                 wm_bf[:].rearrange("p (a c j) -> p a j c", c=PACK, j=PACK),
-                wm_raw[b, half][:].rearrange("p j (a c) -> p a j c", c=PACK),
+                wm_raw[b][:].rearrange("p j (a c) -> p a j c", c=PACK),
             )
-            mx = mx_tiles(HALF, "wm%d_%d" % (b, half))
-            quantize(mx, slice(0, HALF), wm_bf[:], E4M3)
+            mx = mx_tiles(D, "wm%d" % b)
+            quantize(mx, slice(0, D), wm_bf[:], E4M3)
             return mx
 
-        def dx_product(b, wm_mx, e, bank):
+        def dx_block(b, k, bank, staged):
             acc = psum.tile([P, N], F32, name="dx_acc", tag="high%d" % bank)
-            product(acc, wm_mx, e, dzf[b])
-            return acc
-
-        def unpermute(staged, acc, first=0, count=P):
-            rows = slice(first, first + count)
+            product(acc, wm_mx[b], k, dzf[b])
             nc.scalar.copy(
-                staged.rearrange("p (s h i) -> p s h i", h=2, i=2)[:, rows],
-                acc[:].rearrange("p (h s i) -> p s h i", h=2, i=2)[:, rows],
+                staged.rearrange("p (s h i) -> p s h i", h=2, i=2),
+                acc[:].rearrange("p (h s i) -> p s h i", h=2, i=2),
             )
 
         windows = []
@@ -195,9 +196,9 @@ def tile_attend_gex_sig_wx_kernel(tc, xT, dyT, hT, ts, wm, offs, out_0, out_1):
         def store_window(k):
             nc.sync.dma_start(out_1[k * P : (k + 1) * P, :], windows[k][:])
 
-        def scatter(b, k, acc, after):
-            staged = sb([P, N], F32, "staged", after)
-            unpermute(staged[:], acc)
+        def scatter(b, k, bank, after=None):
+            staged = sb([P, N], F32, "staged%d_%d" % (b, k), after)
+            dx_block(b, k, bank, staged[:])
             nc.vector.tensor_copy(windows[k][:].indirect(entries(b * N, N)), staged[:])
             if b == B - 1:
                 store_window(k)
@@ -224,47 +225,41 @@ def tile_attend_gex_sig_wx_kernel(tc, xT, dyT, hT, ts, wm, offs, out_0, out_1):
 
         def x_cast(k, after):
             x_bf[k] = sb([P, T], BF16, "x_bf", after)
-            if k == 0:
-                nc.scalar.activation(x_bf[k][:], x_pool[k][:], COPY)
-            else:
-                nc.gpsimd.tensor_copy(x_bf[k][:], x_pool[k][:])
+            nc.gpsimd.tensor_copy(x_bf[k][:], x_pool[k][:])
 
         def x_gather(k):
-            x_g[k] = sb([P, 2, B * P, 2], BF16, "x_g%d" % k)
-            nc.scalar.activation(x_g[k][:].rearrange("p v s w -> p s v w"), x_bf[k][:].indirect(offsets[:]), COPY)
+            x_g[k] = sb([P, B * N], BF16, "x_g%d" % k)
+            nc.scalar.activation(x_g[k][:], x_bf[k][:].indirect(offsets[:]), COPY)
 
-        def x_weave(pair, b):
-            bank = psum.tile([P, 2, 2, P], F32, name="x_bank", tag="low%d" % b)
+        def x_weave(pair, b, bank_tag, x_slot):
+            bank = psum.tile([P, 2, 2, P], F32, name="x_bank", tag=bank_tag)
             for i in range(2):
-                words = x_g[2 * pair + i][:].rearrange("p v s w -> p (v s w)").bitcast(F32)
+                words = x_g[2 * pair + i][:].bitcast(F32)
                 for v in range(2):
-                    first = (v * B + b) * P
-                    nc.tensor.transpose(bank[:, i, v, :], words[:, first : first + P], ident[:])
-            x_slot = sb([P, 2 * P * PACK], BF16, "x_slot", "grad%d_%d" % (b, 1 + pair))
+                    nc.tensor.transpose(bank[:, i, v, :], words[:, b * HALF + v : (b + 1) * HALF : 2], ident[:])
             nc.scalar.copy(
-                x_slot[:].bitcast(F32).rearrange("p (i d v) -> p i d v", i=2, v=2),
+                x_slot[:].bitcast(F32)[:, b * N : (b + 1) * N].rearrange("p (i d v) -> p i d v", i=2, v=2),
                 bank[:].rearrange("p i v d -> p i d v"),
             )
-            return x_slot
 
-        def x_quantize(pair, b, x_slot):
-            mx = mx_tiles(2 * P, "x%d_%d" % (pair, b))
-            quantize(mx, slice(0, 2 * P), x_slot[:], E4M3)
+        def x_operand(pair, x_slot):
+            mx = mx_tiles(N, "x%d" % pair)
+            quantize(mx, slice(0, N), x_slot[:], E4M3)
             return mx
 
-        def gw_blocks(pair, x_mx, dzs, banks, after):
+        def gw_blocks(pair, x_mx, banks, after):
             gw = sb([P, PACK, DV], F32, "gw", after)
             for b in range(B):
                 for i in range(2):
                     acc = psum.tile([P, DV], F32, name="gw_acc", tag=banks[2 * b + i])
-                    product(acc, x_mx[b], i, dzs[b])
+                    product(acc, x_mx, 2 * b + i, dzs[b])
                     nc.scalar.copy(gw[:, 2 * b + i, :], acc[:])
                 rows = out_0[b, 2 * pair * P : 2 * (pair + 1) * P, :].rearrange("(i p) n -> p i n", i=2)
                 nc.scalar.dma_start(rows, gw[:, 2 * b : 2 * b + 2, :])
 
         for after in ("window0", "window1"):
             clear_window(after)
-        for j in range(PACK):
+        for j in range(2):
             for b in range(B):
                 gather_grad(b, j)
                 if j == 1:
@@ -273,55 +268,48 @@ def tile_attend_gex_sig_wx_kernel(tc, xT, dyT, hT, ts, wm, offs, out_0, out_1):
         for after in ("grad0_0", "grad1_0"):
             clear_window(after)
 
-        wm00 = wm_half(0, 0)
+        gather_grad(0, 2)
+        gather_grad(0, 3)
         for half in range(2):
             weigh(0, 1, half)
         for half in range(2):
-            dz_by_features(0, half, "slope%d" % half)
-        first_accs = [dx_product(0, wm00, e, e) for e in range(2)]
-        wm10 = wm_half(1, 0)
-        wm01 = wm_half(0, 1)
-        wm11 = wm_half(1, 1)
-
-        first_staged = sb([P, N], F32, "staged0_0")
+            dz_by_features(0, half, ("feat0_0", "slope0_0")[half])
+        gather_grad(1, 2, "slope3_0")
+        gather_grad(1, 3)
+        wm_mx = [wm_operand(b) for b in range(B)]
         for half in range(2):
-            unpermute(first_staged[:], first_accs[0], half * P // 2, P // 2)
-            nc.vector.tensor_copy(
-                windows[0][:].indirect(entries(half * HALF, HALF)), first_staged[:, half * HALF : (half + 1) * HALF]
-            )
-
+            weigh(1, 1, half, "feat0_0")
         for half in range(2):
-            weigh(1, 1, half, "wm0_0_codes")
-        for half in range(2):
-            dz_by_features(1, half, ("slope2", "feat1_1")[half])
-        scatter(0, 1, first_accs[1], "staged0_1")
-        x_cast(0, "x_bf0")
-        for k in range(2):
-            scatter(1, k, dx_product(1, wm10, k, k), "staged1_%d" % k)
-        x_gather(0)
+            dz_by_features(1, half, ("slope1_0", "feat1_1")[half])
 
-        x_cast(1, "x_bf1")
-        x_cast(2, "h1")
-        slots = [weave_slots(0, "h2")]
-        x_cast(3, "dz_t0_1")
-        slots.append(weave_slots(1, "x_pool3"))
+        scatter(0, 0, 2)
+        scatter(0, 1, 3)
+        scatter(0, 2, 0)
+        scatter(1, 0, 1)
+        scatter(1, 1, 2)
 
-        x_gather(1)
-        x_woven = [x_weave(0, b) for b in range(B)]
-        scatter(0, 2, dx_product(0, wm01, 0, 0), "x_g1")
+        for k, after in enumerate(("x_bf0", "h0", "h1", "h2")):
+            x_cast(k, after)
+        slots = [weave_slots(0, "x_pool3"), weave_slots(1, "dz_t0_1")]
+
+        for k in range(PACK):
+            x_gather(k)
+        x_slot = [sb([P, N * PACK], BF16, "x_slot", after) for after in ("h1", "ts_g")]
+        for b in range(B):
+            x_weave(0, b, "low%d" % b, x_slot[0])
+        x_weave(1, 1, "low2", x_slot[1])
+        x_first = x_operand(0, x_slot[0])
         dzs = [dz_by_slots(b, slots[b]) for b in range(B)]
-        x_first = [x_quantize(0, b, x_woven[b]) for b in range(B)]
-        scatter(1, 2, dx_product(1, wm11, 0, 1), "staged1_2")
-        x_gather(2)
-        x_gather(3)
-        x_second = [x_quantize(1, b, x_weave(1, b)) for b in range(B)]
 
+        scatter(1, 2, 3, "feat0_0")
+        x_weave(1, 0, "high3", x_slot[1])
+        x_second = x_operand(1, x_slot[1])
         last = PACK - 1
         last_staged = sb([P, B * N], F32, "staged_last", "x_g3")
-        for b, wm_mx in enumerate((wm01, wm11)):
-            unpermute(last_staged[:, b * N : (b + 1) * N], dx_product(b, wm_mx, 1, b))
+        for b in range(B):
+            dx_block(b, last, b, last_staged[:, b * N : (b + 1) * N])
         nc.vector.tensor_copy(windows[last][:].indirect(offsets[:]), last_staged[:])
         store_window(last)
 
-        gw_blocks(0, x_first, dzs, ("low0", "low1", "low0", "low1"), "dy1")
-        gw_blocks(1, x_second, dzs, ("low2", "low3", "high2", "high3"), "dy0")
+        gw_blocks(0, x_first, ("high3", "high0", "high1", "high2"), "dy0")
+        gw_blocks(1, x_second, ("low0", "low1", "low2", "low3"), "dy1")

@@ -228,15 +228,16 @@ def tile_attend_gex_sig_wx_kernel(tc, xT, dyT, hT, ts, wm, offs, out_0, out_1):
             nc.gpsimd.tensor_copy(x_bf[k][:], x_pool[k][:])
 
         def x_gather(k):
-            x_g[k] = sb([P, B * N], BF16, "x_g%d" % k)
-            nc.scalar.activation(x_g[k][:], x_bf[k][:].indirect(offsets[:]), COPY)
+            x_g[k] = sb([P, 2, B * P, 2], BF16, "x_g%d" % k)
+            nc.scalar.activation(x_g[k][:].rearrange("p v s w -> p s v w"), x_bf[k][:].indirect(offsets[:]), COPY)
 
         def x_weave(pair, b, bank_tag, x_slot):
             bank = psum.tile([P, 2, 2, P], F32, name="x_bank", tag=bank_tag)
             for i in range(2):
-                words = x_g[2 * pair + i][:].bitcast(F32)
+                words = x_g[2 * pair + i][:].rearrange("p v s w -> p (v s w)").bitcast(F32)
                 for v in range(2):
-                    nc.tensor.transpose(bank[:, i, v, :], words[:, b * HALF + v : (b + 1) * HALF : 2], ident[:])
+                    first = (v * B + b) * P
+                    nc.tensor.transpose(bank[:, i, v, :], words[:, first : first + P], ident[:])
             nc.scalar.copy(
                 x_slot[:].bitcast(F32)[:, b * N : (b + 1) * N].rearrange("p (i d v) -> p i d v", i=2, v=2),
                 bank[:].rearrange("p i v d -> p i d v"),
@@ -311,5 +312,5 @@ def tile_attend_gex_sig_wx_kernel(tc, xT, dyT, hT, ts, wm, offs, out_0, out_1):
         nc.vector.tensor_copy(windows[last][:].indirect(offsets[:]), last_staged[:])
         store_window(last)
 
-        gw_blocks(0, x_first, ("high3", "high0", "high1", "high2"), "dy0")
+        gw_blocks(0, x_first, ("high3", "high0", "high1", "high3"), "dy0")
         gw_blocks(1, x_second, ("low0", "low1", "low2", "low3"), "dy1")

@@ -37,9 +37,10 @@ def tile_attend_gex_sig_wx_kernel(tc, xT, dyT, hT, ts, wm, offs, out_0, out_1):
         psum = ctx.enter_context(tc.psum_pool(name="psum", bufs=1))
 
         placed = {
-            "wm_raw1": 0, "staged0_0": 0, "staged0_1": 2 * KIB, "staged0_2": 4 * KIB, "staged1_0": 6 * KIB,
+            "wm_raw1": 0, "staged0_0": 0, "staged0_1": 2 * KIB, "staged0_2": 4 * KIB, "dz_slots0_0": 6 * KIB,
             "feat1_1": 8 * KIB, "wm_bf1": 10 * KIB, "x_bf0": 9 * KIB,
             "h3": 22 * KIB - ALIGN, "window0": 14 * KIB, "window1": 22 * KIB,
+            "dz_t0_1": 34 * KIB - ALIGN, "dz_slots1": 30 * KIB, "dzs0_scales": 34 * KIB,
         }
 
         def sb(shape, dtype, name, after=None, bufs=1):
@@ -196,30 +197,21 @@ def tile_attend_gex_sig_wx_kernel(tc, xT, dyT, hT, ts, wm, offs, out_0, out_1):
         def store_window(k):
             nc.sync.dma_start(out_1[k * P : (k + 1) * P, :], windows[k][:])
 
-        def scatter(b, k, bank, after=None):
-            staged = sb([P, N], F32, "staged%d_%d" % (b, k), after)
+        def scatter(b, k, bank):
+            staged = sb([P, N], F32, "staged%d_%d" % (b, k))
             dx_block(b, k, bank, staged[:])
             nc.vector.tensor_copy(windows[k][:].indirect(entries(b * N, N)), staged[:])
             if b == B - 1:
                 store_window(k)
 
-        def weave_slots(b, after):
-            slots = sb([P, DV * PACK], BF16, "dz_slots", after)
-            for u in range(2):
-                nc.gpsimd.tensor_scalar(
-                    slots[:].rearrange("p (m u e t) -> p u m e t", u=2, e=2, t=PACK)[:, u],
-                    dz_part(b, u, 0, PACK).rearrange("p (t m e) -> p m e t", t=PACK, e=2),
-                    1.0,
-                    0.0,
-                    MULT,
-                    ADD,
-                )
-            return slots
+        def slot_views(slots, b, u):
+            return (
+                slots.rearrange("p (c t) -> p c t", t=PACK),
+                dz_part(b, u, 0, PACK).rearrange("p (t c) -> p c t", t=PACK),
+            )
 
-        def dz_by_slots(b, slots):
-            mx = mx_tiles(DV, "dzs%d" % b)
-            quantize(mx, slice(0, DV), slots[:], E5M2)
-            return mx
+        def weave_slots(slots, b, u):
+            nc.gpsimd.tensor_scalar(*slot_views(slots, b, u), 1.0, 0.0, MULT, ADD)
 
         x_bf, x_g = {}, {}
 
@@ -254,7 +246,10 @@ def tile_attend_gex_sig_wx_kernel(tc, xT, dyT, hT, ts, wm, offs, out_0, out_1):
                 for i in range(2):
                     acc = psum.tile([P, DV], F32, name="gw_acc", tag=banks[2 * b + i])
                     product(acc, x_mx, 2 * b + i, dzs[b])
-                    nc.scalar.copy(gw[:, 2 * b + i, :], acc[:])
+                    nc.scalar.copy(
+                        gw[:, 2 * b + i, :].rearrange("p (m u e) -> p m u e", u=2, e=2),
+                        acc[:].rearrange("p (u m e) -> p m u e", u=2, e=2),
+                    )
                 rows = out_0[b, 2 * pair * P : 2 * (pair + 1) * P, :].rearrange("(i p) n -> p i n", i=2)
                 nc.scalar.dma_start(rows, gw[:, 2 * b : 2 * b + 2, :])
 
@@ -283,34 +278,37 @@ def tile_attend_gex_sig_wx_kernel(tc, xT, dyT, hT, ts, wm, offs, out_0, out_1):
         for half in range(2):
             dz_by_features(1, half, ("slope1_0", "feat1_1")[half])
 
-        scatter(0, 0, 2)
-        scatter(0, 1, 3)
-        scatter(0, 2, 0)
-        scatter(1, 0, 1)
-        scatter(1, 1, 2)
+        for b, k, bank in ((0, 0, 2), (0, 1, 3), (0, 2, 0), (1, 0, 1), (1, 1, 2), (1, 2, 3)):
+            scatter(b, k, bank)
+        slots00 = sb([P, HALF * PACK], BF16, "dz_slots0_0")
+        nc.scalar.copy(*slot_views(slots00[:], 0, 0))
 
         for k, after in enumerate(("x_bf0", "h0", "h1", "h2")):
             x_cast(k, after)
-        slots = [weave_slots(0, "x_pool3"), weave_slots(1, "dz_t0_1")]
+        slots01 = sb([P, HALF * PACK], BF16, "dz_slots0_1", "x_pool3")
+        weave_slots(slots01[:], 0, 1)
+        slots1 = sb([P, DV * PACK], BF16, "dz_slots1")
+        for u in range(2):
+            weave_slots(slots1[:, u * HALF * PACK : (u + 1) * HALF * PACK], 1, u)
 
         for k in range(PACK):
             x_gather(k)
         x_slot = [sb([P, N * PACK], BF16, "x_slot", after) for after in ("h1", "ts_g")]
-        for b in range(B):
-            x_weave(0, b, "low%d" % b, x_slot[0])
-        x_weave(1, 1, "low2", x_slot[1])
-        x_first = x_operand(0, x_slot[0])
-        dzs = [dz_by_slots(b, slots[b]) for b in range(B)]
+        for pair in range(2):
+            for b in range(B):
+                x_weave(pair, b, "low%d" % (2 * pair + b), x_slot[pair])
+        x_mx = [x_operand(pair, x_slot[pair]) for pair in range(2)]
+        dzs = [mx_tiles(DV, "dzs%d" % b) for b in range(B)]
+        quantize(dzs[0], slice(0, HALF), slots00[:], E5M2)
+        quantize(dzs[0], slice(HALF, DV), slots01[:], E5M2)
+        quantize(dzs[1], slice(0, DV), slots1[:], E5M2)
 
-        scatter(1, 2, 3, "feat0_0")
-        x_weave(1, 0, "high3", x_slot[1])
-        x_second = x_operand(1, x_slot[1])
         last = PACK - 1
-        last_staged = sb([P, B * N], F32, "staged_last", "x_g3")
+        last_staged = sb([P, B * N], F32, "staged_last", "feat0_0")
         for b in range(B):
             dx_block(b, last, b, last_staged[:, b * N : (b + 1) * N])
         nc.vector.tensor_copy(windows[last][:].indirect(offsets[:]), last_staged[:])
         store_window(last)
 
-        gw_blocks(0, x_first, ("high3", "high0", "high1", "high3"), "dy0")
-        gw_blocks(1, x_second, ("low0", "low1", "low2", "low3"), "dy1")
+        gw_blocks(0, x_mx[0], ("high0", "high1", "low0", "low1"), "dy0")
+        gw_blocks(1, x_mx[1], ("high0", "high1", "low2", "low3"), "dy1")

@@ -37,10 +37,12 @@ def tile_attend_gex_sig_wx_kernel(tc, xT, dyT, hT, ts, wm, offs, out_0, out_1):
         psum = ctx.enter_context(tc.psum_pool(name="psum", bufs=1))
 
         placed = {
-            "wm_raw1": 0, "staged0_0": 0, "staged0_1": 2 * KIB, "staged0_2": 4 * KIB, "dz_slots0_0": 6 * KIB,
-            "feat1_1": 8 * KIB, "wm_bf1": 10 * KIB, "x_bf0": 9 * KIB,
-            "h3": 22 * KIB - ALIGN, "window0": 14 * KIB, "window1": 22 * KIB,
-            "dz_t0_1": 34 * KIB - ALIGN, "dz_slots1": 30 * KIB, "dzs0_scales": 34 * KIB,
+            "wm_raw1": 0, "staged0_1": 2 * KIB, "feat1_0": 4 * KIB, "feat1_1": 6 * KIB,
+            "x_bf1": 8 * KIB - ALIGN,
+            "wm_bf1_0": 12 * KIB, "wm_bf1_1": 14 * KIB, "slots0_a": 13 * KIB, "slots0_b": 15 * KIB,
+            "h3": 24 * KIB - ALIGN, "window0": 16 * KIB, "window1": 24 * KIB,
+            "dz_t0_1": 36 * KIB - ALIGN, "dz_slots1": 32 * KIB, "dzs0_scales": 36 * KIB,
+            "feat0_0": 38 * KIB, "dz_t1_1": 38 * KIB, "x1_scales": 38 * KIB, "staged_last": 39 * KIB,
         }
 
         def sb(shape, dtype, name, after=None, bufs=1):
@@ -56,7 +58,7 @@ def tile_attend_gex_sig_wx_kernel(tc, xT, dyT, hT, ts, wm, offs, out_0, out_1):
             return offsets[:, first // GROUP : (first + count) // GROUP]
 
         ts_pool = sb([P, T], F32, "ts_pool")
-        nc.sync.dma_start(ts_pool[TS_ROW:, :], ts[TS_ROW:, :])
+        nc.scalar.dma_start(ts_pool[TS_ROW:, :], ts[TS_ROW:, :])
         nc.vector.memset(ts_pool[:TS_ROW, :].bitcast(U32), 0)
 
         ident = sb([P, P], F32, "ident")
@@ -88,6 +90,7 @@ def tile_attend_gex_sig_wx_kernel(tc, xT, dyT, hT, ts, wm, offs, out_0, out_1):
             nc.scalar.activation(ts_quarter[b][:], bank[:, :, TS_ROW], COPY, scale=0.25)
 
         slope = {}
+        late_grad = sb([P, N], F32, "grad1_2")
         for j in range(PACK):
             h_g = sb([P, B * N], F32, "h_g", bufs=2)
             nc.vector.tensor_copy(h_g[:], h_pool[j][:].indirect(offsets[:]))
@@ -95,9 +98,12 @@ def tile_attend_gex_sig_wx_kernel(tc, xT, dyT, hT, ts, wm, offs, out_0, out_1):
             nc.scalar.activation(square[:], h_g[:], SQUARE, bias=one[:], scale=-2.0)
             pieces = [(0, B * N)] if j < PACK - 1 else [(0, HALF), (HALF, HALF), (N, N)]
             for first, count in pieces:
-                slope[j, first] = sb([P, count], F32, "slope%d_%d" % (j, first))
+                if (j, first) == (PACK - 1, 0):
+                    slope[j, first] = late_grad[:, HALF:]
+                else:
+                    slope[j, first] = sb([P, count], F32, "slope%d_%d" % (j, first))[:]
                 nc.scalar.activation(
-                    slope[j, first][:], square[:, first : first + count], IDENTITY, bias=one[:], scale=-1.0
+                    slope[j, first], square[:, first : first + count], IDENTITY, bias=one[:], scale=-1.0
                 )
 
         wm_raw = [load(wm[b].rearrange("(m j) d -> m j d", j=PACK), [P, PACK, D], "wm_raw%d" % b) for b in range(B)]
@@ -126,12 +132,16 @@ def tile_attend_gex_sig_wx_kernel(tc, xT, dyT, hT, ts, wm, offs, out_0, out_1):
         def dz_part(b, u, t, count=1):
             return dz_t[b, u][:, t * 2 * P : (t + count) * 2 * P]
 
-        def gather_grad(b, j, after=None):
-            grad[b, j] = sb([P, N], F32, "grad%d_%d" % (b, j), after)
-            if j < PACK - 1:
+        def gather_grad(b, j):
+            if (b, j) == (1, 2):
+                grad[b, j] = late_grad
+                pieces = [(first, slope[j, 0][:, first : first + HALF]) for first in (N, N + HALF)]
+            elif j < PACK - 1:
+                grad[b, j] = sb([P, N], F32, "grad%d_%d" % (b, j))
                 pieces = [(b * N, slope[j, 0][:, b * N : (b + 1) * N])]
             else:
-                pieces = [(first, slope[j, first][:]) for first in ((0, HALF), (N,))[b]]
+                grad[b, j] = sb([P, N], F32, "grad%d_%d" % (b, j))
+                pieces = [(first, slope[j, first]) for first in ((0, HALF), (N,))[b]]
             for first, factor in pieces:
                 count = factor.shape[1]
                 nc.vector.tensor_tensor(
@@ -171,17 +181,20 @@ def tile_attend_gex_sig_wx_kernel(tc, xT, dyT, hT, ts, wm, offs, out_0, out_1):
             quantize(dzf[b], slice(half * HALF, (half + 1) * HALF), feat[:], E5M2)
 
         def wm_operand(b):
-            wm_bf = sb([P, D * PACK], BF16, "wm_bf%d" % b)
-            nc.vector.tensor_copy(
-                wm_bf[:].rearrange("p (a c j) -> p a j c", c=PACK, j=PACK),
-                wm_raw[b][:].rearrange("p j (a c) -> p a j c", c=PACK),
-            )
             mx = mx_tiles(D, "wm%d" % b)
-            quantize(mx, slice(0, D), wm_bf[:], E4M3)
+            halves = [slice(0, HALF), slice(HALF, D)]
+            wm_bf = [sb([P, HALF * PACK], BF16, "wm_bf%d_%d" % (b, half)) for half in range(2)]
+            for half in range(2):
+                nc.vector.tensor_copy(
+                    wm_bf[half][:].rearrange("p (a c j) -> p a j c", c=PACK, j=PACK),
+                    wm_raw[b][:, :, halves[half]].rearrange("p j (a c) -> p a j c", c=PACK),
+                )
+            for half in range(2):
+                quantize(mx, halves[half], wm_bf[half][:], E4M3)
             return mx
 
         def dx_block(b, k, bank, staged):
-            acc = psum.tile([P, N], F32, name="dx_acc", tag="high%d" % bank)
+            acc = psum.tile([P, N], F32, name="dx_acc", tag=bank)
             product(acc, wm_mx[b], k, dzf[b])
             nc.scalar.copy(
                 staged.rearrange("p (s h i) -> p s h i", h=2, i=2),
@@ -204,14 +217,10 @@ def tile_attend_gex_sig_wx_kernel(tc, xT, dyT, hT, ts, wm, offs, out_0, out_1):
             if b == B - 1:
                 store_window(k)
 
-        def slot_views(slots, b, u):
-            return (
-                slots.rearrange("p (c t) -> p c t", t=PACK),
-                dz_part(b, u, 0, PACK).rearrange("p (t c) -> p c t", t=PACK),
-            )
-
-        def weave_slots(slots, b, u):
-            nc.gpsimd.tensor_scalar(*slot_views(slots, b, u), 1.0, 0.0, MULT, ADD)
+        def weave_slots(slots, b, u, first):
+            words = slots.rearrange("p (c t) -> p c t", t=PACK)
+            source = dz_part(b, u, 0, PACK).rearrange("p (t c) -> p c t", t=PACK)
+            nc.gpsimd.tensor_scalar(words, source[:, first : first + words.shape[1], :], 1.0, 0.0, MULT, ADD)
 
         x_bf, x_g = {}, {}
 
@@ -250,8 +259,8 @@ def tile_attend_gex_sig_wx_kernel(tc, xT, dyT, hT, ts, wm, offs, out_0, out_1):
                         gw[:, 2 * b + i, :].rearrange("p (m u e) -> p m u e", u=2, e=2),
                         acc[:].rearrange("p (u m e) -> p m u e", u=2, e=2),
                     )
-                rows = out_0[b, 2 * pair * P : 2 * (pair + 1) * P, :].rearrange("(i p) n -> p i n", i=2)
-                nc.scalar.dma_start(rows, gw[:, 2 * b : 2 * b + 2, :])
+                    k = 2 * pair + i
+                    nc.sync.dma_start(out_0[b, k * P : (k + 1) * P, :], gw[:, 2 * b + i, :])
 
         for after in ("window0", "window1"):
             clear_window(after)
@@ -268,28 +277,33 @@ def tile_attend_gex_sig_wx_kernel(tc, xT, dyT, hT, ts, wm, offs, out_0, out_1):
         gather_grad(0, 3)
         for half in range(2):
             weigh(0, 1, half)
+        gather_grad(1, 2)
+        gather_grad(1, 3)
+        wm_mx = [wm_operand(0)]
         for half in range(2):
             dz_by_features(0, half, ("feat0_0", "slope0_0")[half])
-        gather_grad(1, 2, "slope3_0")
-        gather_grad(1, 3)
-        wm_mx = [wm_operand(b) for b in range(B)]
+        wm_mx.append(wm_operand(1))
         for half in range(2):
-            weigh(1, 1, half, "feat0_0")
+            weigh(1, 1, half)
+        scatter(0, 0, "high2")
         for half in range(2):
-            dz_by_features(1, half, ("slope1_0", "feat1_1")[half])
-
-        for b, k, bank in ((0, 0, 2), (0, 1, 3), (0, 2, 0), (1, 0, 1), (1, 1, 2), (1, 2, 3)):
+            dz_by_features(1, half, "feat1_%d" % half)
+        for b, k, bank in ((0, 1, "high3"), (0, 2, "low2"), (1, 0, "low3"), (1, 1, "high2"), (1, 2, "high3")):
             scatter(b, k, bank)
-        slots00 = sb([P, HALF * PACK], BF16, "dz_slots0_0")
-        nc.scalar.copy(*slot_views(slots00[:], 0, 0))
 
-        for k, after in enumerate(("x_bf0", "h0", "h1", "h2")):
+        slots0 = [sb([P, HALF * PACK], BF16, "slots0_a"), sb([P, P * PACK], BF16, "slots0_b")]
+        weave_slots(slots0[0][:], 0, 0, 0)
+        weave_slots(slots0[1][:], 0, 1, 0)
+        x_bf[0] = sb([P, T], BF16, "x_bf0")
+        nc.scalar.activation(x_bf[0][:], x_pool[0][:], COPY)
+
+        for k, after in ((1, "x_bf1"), (2, "h1"), (3, "h2")):
             x_cast(k, after)
-        slots01 = sb([P, HALF * PACK], BF16, "dz_slots0_1", "x_pool3")
-        weave_slots(slots01[:], 0, 1)
+        slots0.append(sb([P, P * PACK], BF16, "slots0_c", "x_pool3"))
+        weave_slots(slots0[2][:], 0, 1, P)
         slots1 = sb([P, DV * PACK], BF16, "dz_slots1")
         for u in range(2):
-            weave_slots(slots1[:, u * HALF * PACK : (u + 1) * HALF * PACK], 1, u)
+            weave_slots(slots1[:, u * HALF * PACK : (u + 1) * HALF * PACK], 1, u, 0)
 
         for k in range(PACK):
             x_gather(k)
@@ -297,18 +311,19 @@ def tile_attend_gex_sig_wx_kernel(tc, xT, dyT, hT, ts, wm, offs, out_0, out_1):
         for pair in range(2):
             for b in range(B):
                 x_weave(pair, b, "low%d" % (2 * pair + b), x_slot[pair])
-        x_mx = [x_operand(pair, x_slot[pair]) for pair in range(2)]
+        x_mx = [x_operand(0, x_slot[0])]
         dzs = [mx_tiles(DV, "dzs%d" % b) for b in range(B)]
-        quantize(dzs[0], slice(0, HALF), slots00[:], E5M2)
-        quantize(dzs[0], slice(HALF, DV), slots01[:], E5M2)
+        for piece, cols in zip(slots0, (slice(0, HALF), slice(HALF, HALF + P), slice(HALF + P, DV))):
+            quantize(dzs[0], cols, piece[:], E5M2)
         quantize(dzs[1], slice(0, DV), slots1[:], E5M2)
+        x_mx.append(x_operand(1, x_slot[1]))
 
         last = PACK - 1
-        last_staged = sb([P, B * N], F32, "staged_last", "feat0_0")
+        last_staged = sb([P, B * N], F32, "staged_last")
         for b in range(B):
-            dx_block(b, last, b, last_staged[:, b * N : (b + 1) * N])
+            dx_block(b, last, "high%d" % b, last_staged[:, b * N : (b + 1) * N])
         nc.vector.tensor_copy(windows[last][:].indirect(offsets[:]), last_staged[:])
-        store_window(last)
 
         gw_blocks(0, x_mx[0], ("high0", "high1", "low0", "low1"), "dy0")
         gw_blocks(1, x_mx[1], ("high0", "high1", "low2", "low3"), "dy1")
+        nc.scalar.dma_start(out_1[last * P :, :], windows[last][:])

@@ -37,12 +37,12 @@ def tile_attend_gex_sig_wx_kernel(tc, xT, dyT, hT, ts, wm, offs, out_0, out_1):
         psum = ctx.enter_context(tc.psum_pool(name="psum", bufs=1))
 
         placed = {
-            "wm_raw1": 0, "staged0_1": 2 * KIB, "feat1_0": 4 * KIB, "feat1_1": 6 * KIB,
+            "wm_raw1": 0, "slots0_0": 0, "staged0_1": 2 * KIB, "feat1_0": 4 * KIB, "feat1_1": 6 * KIB,
             "x_bf1": 8 * KIB - ALIGN,
-            "wm_bf1_0": 12 * KIB, "wm_bf1_1": 14 * KIB, "slots0_a": 13 * KIB, "slots0_b": 15 * KIB,
+            "wm_bf1_0": 12 * KIB, "wm_bf1_1": 14 * KIB, "x_bf0": 12 * KIB,
             "h3": 24 * KIB - ALIGN, "window0": 16 * KIB, "window1": 24 * KIB,
             "dz_t0_1": 36 * KIB - ALIGN, "dz_slots1": 32 * KIB, "dzs0_scales": 36 * KIB,
-            "feat0_0": 38 * KIB, "dz_t1_1": 38 * KIB, "x1_scales": 38 * KIB, "staged_last": 39 * KIB,
+            "feat0_0": 38 * KIB, "dz_t1_1": 38 * KIB, "x1_scales": 38 * KIB,
         }
 
         def sb(shape, dtype, name, after=None, bufs=1):
@@ -217,10 +217,14 @@ def tile_attend_gex_sig_wx_kernel(tc, xT, dyT, hT, ts, wm, offs, out_0, out_1):
             if b == B - 1:
                 store_window(k)
 
-        def weave_slots(slots, b, u, first):
-            words = slots.rearrange("p (c t) -> p c t", t=PACK)
-            source = dz_part(b, u, 0, PACK).rearrange("p (t c) -> p c t", t=PACK)
-            nc.gpsimd.tensor_scalar(words, source[:, first : first + words.shape[1], :], 1.0, 0.0, MULT, ADD)
+        def slot_views(slots, b, u):
+            return (
+                slots.rearrange("p (c t) -> p c t", t=PACK),
+                dz_part(b, u, 0, PACK).rearrange("p (t c) -> p c t", t=PACK),
+            )
+
+        def weave_slots(slots, b, u):
+            nc.gpsimd.tensor_scalar(*slot_views(slots, b, u), 1.0, 0.0, MULT, ADD)
 
         x_bf, x_g = {}, {}
 
@@ -291,19 +295,16 @@ def tile_attend_gex_sig_wx_kernel(tc, xT, dyT, hT, ts, wm, offs, out_0, out_1):
         for b, k, bank in ((0, 1, "high3"), (0, 2, "low2"), (1, 0, "low3"), (1, 1, "high2"), (1, 2, "high3")):
             scatter(b, k, bank)
 
-        slots0 = [sb([P, HALF * PACK], BF16, "slots0_a"), sb([P, P * PACK], BF16, "slots0_b")]
-        weave_slots(slots0[0][:], 0, 0, 0)
-        weave_slots(slots0[1][:], 0, 1, 0)
-        x_bf[0] = sb([P, T], BF16, "x_bf0")
-        nc.scalar.activation(x_bf[0][:], x_pool[0][:], COPY)
+        slots0 = [sb([P, HALF * PACK], BF16, "slots0_0")]
+        nc.scalar.copy(*slot_views(slots0[0][:], 0, 0))
 
-        for k, after in ((1, "x_bf1"), (2, "h1"), (3, "h2")):
+        for k, after in enumerate(("x_bf0", "x_bf1", "h1", "h2")):
             x_cast(k, after)
-        slots0.append(sb([P, P * PACK], BF16, "slots0_c", "x_pool3"))
-        weave_slots(slots0[2][:], 0, 1, P)
+        slots0.append(sb([P, HALF * PACK], BF16, "slots0_1", "x_pool3"))
+        weave_slots(slots0[1][:], 0, 1)
         slots1 = sb([P, DV * PACK], BF16, "dz_slots1")
         for u in range(2):
-            weave_slots(slots1[:, u * HALF * PACK : (u + 1) * HALF * PACK], 1, u, 0)
+            weave_slots(slots1[:, u * HALF * PACK : (u + 1) * HALF * PACK], 1, u)
 
         for k in range(PACK):
             x_gather(k)
@@ -313,17 +314,17 @@ def tile_attend_gex_sig_wx_kernel(tc, xT, dyT, hT, ts, wm, offs, out_0, out_1):
                 x_weave(pair, b, "low%d" % (2 * pair + b), x_slot[pair])
         x_mx = [x_operand(0, x_slot[0])]
         dzs = [mx_tiles(DV, "dzs%d" % b) for b in range(B)]
-        for piece, cols in zip(slots0, (slice(0, HALF), slice(HALF, HALF + P), slice(HALF + P, DV))):
-            quantize(dzs[0], cols, piece[:], E5M2)
+        for u in range(2):
+            quantize(dzs[0], slice(u * HALF, (u + 1) * HALF), slots0[u][:], E5M2)
         quantize(dzs[1], slice(0, DV), slots1[:], E5M2)
         x_mx.append(x_operand(1, x_slot[1]))
 
         last = PACK - 1
-        last_staged = sb([P, B * N], F32, "staged_last")
+        last_staged = sb([P, B * N], F32, "staged_last", "dz_t1_0")
         for b in range(B):
             dx_block(b, last, "high%d" % b, last_staged[:, b * N : (b + 1) * N])
         nc.vector.tensor_copy(windows[last][:].indirect(offsets[:]), last_staged[:])
 
         gw_blocks(0, x_mx[0], ("high0", "high1", "low0", "low1"), "dy0")
-        gw_blocks(1, x_mx[1], ("high0", "high1", "low2", "low3"), "dy1")
+        gw_blocks(1, x_mx[1], ("low2", "low3", "high2", "high3"), "dy1")
         nc.scalar.dma_start(out_1[last * P :, :], windows[last][:])

@@ -40,9 +40,9 @@ def tile_attend_gex_sig_wx_kernel(tc, xT, dyT, hT, ts, wm, offs, out_0, out_1):
             "wm_raw1": 0, "slots0_0": 0, "staged0_1": 2 * KIB, "feat1_0": 4 * KIB, "feat1_1": 6 * KIB,
             "x_bf1": 8 * KIB - ALIGN,
             "wm_bf1_0": 12 * KIB, "wm_bf1_1": 14 * KIB, "x_bf0": 12 * KIB,
-            "h3": 24 * KIB - ALIGN, "window0": 16 * KIB, "window1": 24 * KIB,
-            "dz_t0_1": 36 * KIB - ALIGN, "dz_slots1": 32 * KIB, "dzs0_scales": 36 * KIB,
-            "feat0_0": 38 * KIB, "dz_t1_1": 38 * KIB, "x1_scales": 38 * KIB,
+
+            "dz_t0_1": 20 * KIB - ALIGN, "dz_slots1": 16 * KIB, "dzs0_scales": 20 * KIB,
+            "feat0_0": 22 * KIB, "dz_t1_1": 22 * KIB, "x1_scales": 22 * KIB,
         }
 
         def sb(shape, dtype, name, after=None, bufs=1):
@@ -266,7 +266,7 @@ def tile_attend_gex_sig_wx_kernel(tc, xT, dyT, hT, ts, wm, offs, out_0, out_1):
                     k = 2 * pair + i
                     nc.sync.dma_start(out_0[b, k * P : (k + 1) * P, :], gw[:, 2 * b + i, :])
 
-        for after in ("window0", "window1"):
+        for after in ("ts_pool", "h3"):
             clear_window(after)
         for j in range(2):
             for b in range(B):
@@ -287,9 +287,9 @@ def tile_attend_gex_sig_wx_kernel(tc, xT, dyT, hT, ts, wm, offs, out_0, out_1):
         for half in range(2):
             dz_by_features(0, half, ("feat0_0", "slope0_0")[half])
         wm_mx.append(wm_operand(1))
+        scatter(0, 0, "high2")
         for half in range(2):
             weigh(1, 1, half)
-        scatter(0, 0, "high2")
         for half in range(2):
             dz_by_features(1, half, "feat1_%d" % half)
         for b, k, bank in ((0, 1, "high3"), (0, 2, "low2"), (1, 0, "low3"), (1, 1, "high2"), (1, 2, "high3")):

@@ -17,15 +17,14 @@ MULT = mybir.AluOpType.mult
 ADD = mybir.AluOpType.add
 COPY = mybir.ActivationFunctionType.Copy
 SQUARE = mybir.ActivationFunctionType.Square
-IDENTITY = mybir.ActivationFunctionType.Identity
 
 P = 128
 PACK = 4
 HALF = N // 2
 GROUP = 16
 ALIGN = 64
-KIB = 1024
 TS_ROW = P - 1
+LAST = PACK - 1
 
 
 def tile_attend_gex_sig_wx_kernel(tc, xT, dyT, hT, ts, wm, offs, out_0, out_1):
@@ -33,23 +32,13 @@ def tile_attend_gex_sig_wx_kernel(tc, xT, dyT, hT, ts, wm, offs, out_0, out_1):
     with ExitStack() as ctx:
         lists = ctx.enter_context(tc.tile_pool(name="lists", bufs=1))
         keep = ctx.enter_context(tc.tile_pool(name="keep", bufs=1))
-        relay = ctx.enter_context(tc.tile_pool(name="relay", bufs=1))
         psum = ctx.enter_context(tc.psum_pool(name="psum", bufs=1))
 
-        placed = {
-            "wm_raw1": 0, "slots0_0": 0, "staged0_1": 2 * KIB, "feat1_0": 4 * KIB, "feat1_1": 6 * KIB,
-            "x_bf1": 8 * KIB - ALIGN,
-            "wm_bf1_0": 12 * KIB, "wm_bf1_1": 14 * KIB, "x_bf0": 12 * KIB,
-
-            "dz_t0_1": 20 * KIB - ALIGN, "dz_slots1": 16 * KIB, "dzs0_scales": 20 * KIB,
-            "feat0_0": 22 * KIB, "dz_t1_1": 22 * KIB, "x1_scales": 22 * KIB,
-        }
-
         def sb(shape, dtype, name, after=None, bufs=1):
-            tag = after or name
-            if tag in placed:
-                return relay.tile(shape, dtype, name=name, tag=tag, align_bytes=ALIGN, offset=placed[tag])
-            return keep.tile(shape, dtype, name=name, tag=tag, bufs=bufs, align_bytes=ALIGN)
+            return keep.tile(shape, dtype, name=name, tag=after or name, bufs=bufs, align_bytes=ALIGN)
+
+        def bank(shape, tag):
+            return psum.tile(shape, F32, name="bank_" + tag, tag=tag)
 
         offsets = lists.tile([P, B * N // GROUP], U16, name="offsets")
         nc.sync.dma_start(offsets[:], offs)
@@ -76,38 +65,29 @@ def tile_attend_gex_sig_wx_kernel(tc, xT, dyT, hT, ts, wm, offs, out_0, out_1):
         h_rows = hT.rearrange("(m j) c -> j m c", j=PACK)
         dy_rows = dyT.rearrange("(m j) c -> j m c", j=PACK)
         x_rows = xT.rearrange("(k m) c -> k m c", m=P)
-        h_pool = [load(h_rows[j], [P, T], "h%d" % j) for j in range(PACK)]
-        dy_pool = [load(dy_rows[j], [P, T], "dy%d" % j) for j in range(PACK)]
+        h_pool, dy_pool = [], []
+        for j in range(PACK):
+            h_pool.append(load(h_rows[j], [P, T], "h%d" % j))
+            dy_pool.append(load(dy_rows[j], [P, T], "dy%d" % j))
+        wm_raw = [load(wm[b].rearrange("(m j) d -> m j d", j=PACK), [P, PACK, D], "wm_raw%d" % b) for b in range(B)]
+
+        windows = [sb([P, T], F32, "window%d" % k) for k in range(PACK)]
+        for k in (LAST, 0, 1, 2):
+            nc.gpsimd.memset(windows[k][:], 0.0)
 
         ts_g = sb([P, B * N], F32, "ts_g")
         nc.vector.tensor_copy(ts_g[:], ts_pool[:].indirect(offsets[:]))
-        ts_quarter = []
+        ts_wide = []
         for b in range(B):
-            bank = psum.tile([P, PACK, P], F32, name="ts_bank", tag="low%d" % b)
-            for t in range(PACK):
-                nc.tensor.transpose(bank[:, t, :], ts_g[:, b * N + t : (b + 1) * N : PACK], ident[:])
-            ts_quarter.append(sb([P, PACK], F32, "ts_quarter%d" % b))
-            nc.scalar.activation(ts_quarter[b][:], bank[:, :, TS_ROW], COPY, scale=0.25)
-
-        slope = {}
-        late_grad = sb([P, N], F32, "grad1_2")
-        for j in range(PACK):
-            h_g = sb([P, B * N], F32, "h_g", bufs=2)
-            nc.vector.tensor_copy(h_g[:], h_pool[j][:].indirect(offsets[:]))
-            square = sb([P, B * N], F32, "square", bufs=2)
-            nc.scalar.activation(square[:], h_g[:], SQUARE, bias=one[:], scale=-2.0)
-            pieces = [(0, B * N)] if j < PACK - 1 else [(0, HALF), (HALF, HALF), (N, N)]
-            for first, count in pieces:
-                if (j, first) == (PACK - 1, 0):
-                    slope[j, first] = late_grad[:, HALF:]
-                else:
-                    slope[j, first] = sb([P, count], F32, "slope%d_%d" % (j, first))[:]
-                nc.scalar.activation(
-                    slope[j, first], square[:, first : first + count], IDENTITY, bias=one[:], scale=-1.0
-                )
-
-        wm_raw = [load(wm[b].rearrange("(m j) d -> m j d", j=PACK), [P, PACK, D], "wm_raw%d" % b) for b in range(B)]
-        x_pool = [load(x_rows[k], [P, T], "x_pool%d" % k, ("h0", "h1", "h2", None)[k]) for k in range(PACK)]
+            turned = bank([P, PACK, P], "f%d" % b)
+            for q in range(PACK):
+                nc.tensor.transpose(turned[:, q, :], ts_g[:, b * N + q * P : b * N + (q + 1) * P], ident[:])
+            column = sb([P, PACK], F32, "ts_column%d" % b)
+            nc.vector.tensor_scalar_mul(column[:], turned[:, :, TS_ROW], -0.25)
+            wide = bank([P, PACK, P], "ts%d" % b)
+            for q in range(PACK):
+                nc.tensor.transpose(wide[:, q, :], column[:, q : q + 1].to_broadcast([P, P]), ident[:])
+            ts_wide.append(wide)
 
         def mx_tiles(width, name):
             return sb([P, width], U32, name + "_codes"), sb([P, width], U8, name + "_scales")
@@ -126,205 +106,145 @@ def tile_attend_gex_sig_wx_kernel(tc, xT, dyT, hT, ts, wm, offs, out_0, out_1):
                 stop=True,
             )
 
-        dzf = [mx_tiles(N, "dzf%d" % b) for b in range(B)]
-        grad, fwd, back, dz_t = {}, {}, {}, {}
-
-        def dz_part(b, u, t, count=1):
-            return dz_t[b, u][:, t * 2 * P : (t + count) * 2 * P]
-
-        def gather_grad(b, j):
-            if (b, j) == (1, 2):
-                grad[b, j] = late_grad
-                pieces = [(first, slope[j, 0][:, first : first + HALF]) for first in (N, N + HALF)]
-            elif j < PACK - 1:
-                grad[b, j] = sb([P, N], F32, "grad%d_%d" % (b, j))
-                pieces = [(b * N, slope[j, 0][:, b * N : (b + 1) * N])]
-            else:
-                grad[b, j] = sb([P, N], F32, "grad%d_%d" % (b, j))
-                pieces = [(first, slope[j, first]) for first in ((0, HALF), (N,))[b]]
-            for first, factor in pieces:
-                count = factor.shape[1]
-                nc.vector.tensor_tensor(
-                    grad[b, j][:, first - b * N : first - b * N + count],
-                    dy_pool[j][:].indirect(entries(first, count)),
-                    factor,
-                    MULT,
-                )
-            for t in range(PACK):
-                if j % 2 == 0 and t % 2 == 0:
-                    tag = "low%d" % (2 * b + t // 2) if j == 0 else "high%d" % (t // 2)
-                    fwd[b, t // 2] = psum.tile([P, 2, 2, P], F32, name="fwd", tag=tag)
-                nc.tensor.transpose(fwd[b, t // 2][:, t % 2, j % 2, :], grad[b, j][:, t::PACK], ident[:])
-
-        def weigh(b, u, half, after=None):
-            if half == 0:
-                dz_t[b, u] = sb([P, PACK * 2 * P], BF16, "dz_t%d_%d" % (b, u), after)
-            for i in range(2):
-                t = 2 * half + i
-                nc.scalar.activation(
-                    dz_part(b, u, t).rearrange("p (m e) -> p m e", e=2),
-                    fwd[b, half][:, i].rearrange("p e m -> p m e"),
-                    COPY,
-                    scale=ts_quarter[b][:, t : t + 1],
-                )
-            if u == 0:
-                back[b, half] = psum.tile([P, 2, 2, P], F32, name="back", tag="low%d" % (2 * b + half))
-            for i in range(2):
-                nc.tensor.transpose(back[b, half][:, i, u, :], dz_part(b, u, 2 * half + i).bitcast(F32), ident[:])
-
-        def dz_by_features(b, half, after):
-            feat = sb([P, HALF * PACK], BF16, "feat", after)
-            nc.scalar.copy(
-                feat[:].bitcast(F32).rearrange("p (s i u) -> p s i u", i=2, u=2),
-                back[b, half][:].rearrange("p i u s -> p s i u"),
+        def interleave(dst, planes):
+            nc.vector.tensor_copy(
+                dst.rearrange("p (a c j) -> p a j c", c=PACK, j=PACK),
+                planes.rearrange("p j (a c) -> p a j c", c=PACK),
             )
-            quantize(dzf[b], slice(half * HALF, (half + 1) * HALF), feat[:], E5M2)
+
+        halves = [slice(0, HALF), slice(HALF, N)]
+        dz = [sb([P, PACK, N], F32, "dz%d" % b) for b in range(B)]
+        dzs = [mx_tiles(DV, "dzs%d" % b) for b in range(B)]
+        dzf = [mx_tiles(N, "dzf%d" % b) for b in range(B)]
+
+        def factor_of(b, j):
+            h_g = sb([P, N], F32, "h_g", bufs=2)
+            nc.scalar.activation(h_g[:], h_pool[j][:].indirect(entries(b * N, N)), COPY)
+            square = sb([P, N], F32, "square", bufs=2)
+            nc.scalar.activation(square[:], h_g[:], SQUARE, bias=one[:], scale=-2.0)
+            factor = sb([P, N], F32, "factor", bufs=2)
+            nc.vector.scalar_tensor_tensor(
+                factor[:], square[:], -1.0, ts_wide[b][:].rearrange("p q s -> p (q s)"), ADD, MULT
+            )
+            return factor
+
+        def dz_plane(b, j):
+            nc.vector.tensor_tensor(dz[b][:, j, :], dy_pool[j][:].indirect(entries(b * N, N)), factor_of(b, j)[:], MULT)
+
+        def dz_by_slots(b, j):
+            turned = bank([P, PACK, P], "f%d" % ((2 * j + b) % PACK))
+            for t in range(PACK):
+                nc.tensor.transpose(turned[:, t, :], dz[b][:, j, t::PACK], ident[:])
+            slots = sb([P, N], BF16, "dz_slots%d_%d" % (b, j))
+            nc.scalar.copy(slots[:].rearrange("p (m t) -> p m t", t=PACK), turned[:].rearrange("p t m -> p m t"))
+            quantize(dzs[b], slice(j * P, (j + 1) * P), slots[:], E5M2)
+
+        def dz_by_features(b):
+            feat = [sb([P, HALF * PACK], BF16, "feat%d_%d" % (b, half)) for half in range(2)]
+            for half in range(2):
+                interleave(feat[half][:], dz[b][:, :, halves[half]])
+            for half in range(2):
+                quantize(dzf[b], halves[half], feat[half][:], E5M2)
 
         def wm_operand(b):
             mx = mx_tiles(D, "wm%d" % b)
-            halves = [slice(0, HALF), slice(HALF, D)]
             wm_bf = [sb([P, HALF * PACK], BF16, "wm_bf%d_%d" % (b, half)) for half in range(2)]
-            for half in range(2):
-                nc.vector.tensor_copy(
-                    wm_bf[half][:].rearrange("p (a c j) -> p a j c", c=PACK, j=PACK),
-                    wm_raw[b][:, :, halves[half]].rearrange("p j (a c) -> p a j c", c=PACK),
-                )
-            for half in range(2):
+            for half in (1, 0):
+                interleave(wm_bf[half][:], wm_raw[b][:, :, halves[half]])
+            for half in (1, 0):
                 quantize(mx, halves[half], wm_bf[half][:], E4M3)
             return mx
 
-        def dx_block(b, k, bank, staged):
-            acc = psum.tile([P, N], F32, name="dx_acc", tag=bank)
+        def dx_block(b, k, tag, staged):
+            acc = bank([P, N], tag)
             product(acc, wm_mx[b], k, dzf[b])
-            nc.scalar.copy(
-                staged.rearrange("p (s h i) -> p s h i", h=2, i=2),
-                acc[:].rearrange("p (h s i) -> p s h i", h=2, i=2),
-            )
-
-        windows = []
-
-        def clear_window(after):
-            windows.append(sb([P, T], F32, "window", after))
-            nc.gpsimd.memset(windows[-1][:], 0.0)
+            nc.scalar.copy(staged, acc[:])
 
         def store_window(k):
             nc.sync.dma_start(out_1[k * P : (k + 1) * P, :], windows[k][:])
 
-        def scatter(b, k, bank):
-            staged = sb([P, N], F32, "staged%d_%d" % (b, k))
-            dx_block(b, k, bank, staged[:])
-            nc.vector.tensor_copy(windows[k][:].indirect(entries(b * N, N)), staged[:])
-            if b == B - 1:
-                store_window(k)
+        def scatter_vector(b, k, staged):
+            nc.vector.tensor_copy(windows[k][:].indirect(entries(b * N, N)), staged)
 
-        def slot_views(slots, b, u):
-            return (
-                slots.rearrange("p (c t) -> p c t", t=PACK),
-                dz_part(b, u, 0, PACK).rearrange("p (t c) -> p c t", t=PACK),
-            )
+        def scatter_scalar(b, k, staged):
+            for half in range(2):
+                nc.scalar.activation(
+                    windows[k][:].indirect(entries(b * N + half * HALF, HALF)), staged[:, halves[half]], COPY
+                )
 
-        def weave_slots(slots, b, u):
-            nc.gpsimd.tensor_scalar(*slot_views(slots, b, u), 1.0, 0.0, MULT, ADD)
+        for j in range(PACK):
+            for b in range(B):
+                dz_plane(b, j)
+                if j == LAST:
+                    dz_by_features(b)
+                dz_by_slots(b, j)
 
-        x_bf, x_g = {}, {}
+        x_pool = [load(x_rows[k], [P, T], "x_pool%d" % k, "h%d" % k) for k in range(PACK)]
+        wm_mx = [wm_operand(b) for b in range(B)]
 
-        def x_cast(k, after):
-            x_bf[k] = sb([P, T], BF16, "x_bf", after)
-            nc.gpsimd.tensor_copy(x_bf[k][:], x_pool[k][:])
+        x_g = {}
 
         def x_gather(k):
-            x_g[k] = sb([P, 2, B * P, 2], BF16, "x_g%d" % k)
-            nc.scalar.activation(x_g[k][:].rearrange("p v s w -> p s v w"), x_bf[k][:].indirect(offsets[:]), COPY)
+            x_g[k] = sb([P, B * N], BF16, "x_g%d" % k)
+            nc.scalar.activation(x_g[k][:], x_pool[k][:].indirect(offsets[:]), COPY)
 
-        def x_weave(pair, b, bank_tag, x_slot):
-            bank = psum.tile([P, 2, 2, P], F32, name="x_bank", tag=bank_tag)
-            for i in range(2):
-                words = x_g[2 * pair + i][:].rearrange("p v s w -> p (v s w)").bitcast(F32)
-                for v in range(2):
-                    first = (v * B + b) * P
-                    nc.tensor.transpose(bank[:, i, v, :], words[:, first : first + P], ident[:])
-            nc.scalar.copy(
-                x_slot[:].bitcast(F32)[:, b * N : (b + 1) * N].rearrange("p (i d v) -> p i d v", i=2, v=2),
-                bank[:].rearrange("p i v d -> p i d v"),
-            )
-
-        def x_operand(pair, x_slot):
+        def x_operand(pair):
+            x_slot = sb([P, N * PACK], BF16, "x_slot%d" % pair)
+            for b in range(B):
+                turned = bank([P, 2, 2, P], "f%d" % (2 * pair + b))
+                for i in range(2):
+                    words = x_g[2 * pair + i][:].bitcast(F32)
+                    for v in range(2):
+                        nc.tensor.transpose(turned[:, i, v, :], words[:, b * HALF + v : (b + 1) * HALF : 2], ident[:])
+                nc.scalar.copy(
+                    x_slot[:].bitcast(F32)[:, b * N : (b + 1) * N].rearrange("p (i d v) -> p i d v", i=2, v=2),
+                    turned[:].rearrange("p i v d -> p i d v"),
+                )
             mx = mx_tiles(N, "x%d" % pair)
             quantize(mx, slice(0, N), x_slot[:], E4M3)
             return mx
 
-        def gw_blocks(pair, x_mx, banks, after):
+        def gw_blocks(pair, tags, after):
             gw = sb([P, PACK, DV], F32, "gw", after)
             for b in range(B):
                 for i in range(2):
-                    acc = psum.tile([P, DV], F32, name="gw_acc", tag=banks[2 * b + i])
-                    product(acc, x_mx, 2 * b + i, dzs[b])
+                    acc = bank([P, DV], tags[2 * b + i])
+                    product(acc, x_mx[pair], 2 * b + i, dzs[b])
                     nc.scalar.copy(
-                        gw[:, 2 * b + i, :].rearrange("p (m u e) -> p m u e", u=2, e=2),
-                        acc[:].rearrange("p (u m e) -> p m u e", u=2, e=2),
+                        gw[:, 2 * b + i, :].rearrange("p (m j) -> p m j", j=PACK),
+                        acc[:].rearrange("p (j m) -> p m j", j=PACK),
                     )
                     k = 2 * pair + i
                     nc.sync.dma_start(out_0[b, k * P : (k + 1) * P, :], gw[:, 2 * b + i, :])
 
-        for after in ("ts_pool", "h3"):
-            clear_window(after)
-        for j in range(2):
-            for b in range(B):
-                gather_grad(b, j)
-                if j == 1:
-                    for half in range(2):
-                        weigh(b, 0, half)
-        for after in ("grad0_0", "grad1_0"):
-            clear_window(after)
+        staged = sb([P, N], F32, "staged0_3")
+        dx_block(0, LAST, "a0", staged[:])
+        scatter_scalar(0, LAST, staged)
+        for k, tag, after in ((0, "a1", "wm_raw1"), (1, "ts0", None)):
+            staged = sb([P, N], F32, "staged0_%d" % k, after)
+            dx_block(0, k, tag, staged[:])
+            scatter_vector(0, k, staged[:])
 
-        gather_grad(0, 2)
-        gather_grad(0, 3)
-        for half in range(2):
-            weigh(0, 1, half)
-        gather_grad(1, 2)
-        gather_grad(1, 3)
-        wm_mx = [wm_operand(0)]
-        for half in range(2):
-            dz_by_features(0, half, ("feat0_0", "slope0_0")[half])
-        wm_mx.append(wm_operand(1))
-        scatter(0, 0, "high2")
-        for half in range(2):
-            weigh(1, 1, half)
-        for half in range(2):
-            dz_by_features(1, half, "feat1_%d" % half)
-        for b, k, bank in ((0, 1, "high3"), (0, 2, "low2"), (1, 0, "low3"), (1, 1, "high2"), (1, 2, "high3")):
-            scatter(b, k, bank)
+        x_gather(0)
+        staged = sb([P, 3, N], F32, "staged1", "h0")
+        dx_block(1, LAST, "a0", staged[:, 0, :])
+        for k, tag in ((0, "a1"), (1, "ts1")):
+            dx_block(1, k, tag, staged[:, 1 + k, :])
+        scatter_scalar(1, LAST, staged[:, 0, :])
+        store_window(LAST)
+        for k in range(2):
+            scatter_vector(1, k, staged[:, 1 + k, :])
+            store_window(k)
 
-        slots0 = [sb([P, HALF * PACK], BF16, "slots0_0")]
-        nc.scalar.copy(*slot_views(slots0[0][:], 0, 0))
-
-        for k, after in enumerate(("x_bf0", "x_bf1", "h1", "h2")):
-            x_cast(k, after)
-        slots0.append(sb([P, HALF * PACK], BF16, "slots0_1", "x_pool3"))
-        weave_slots(slots0[1][:], 0, 1)
-        slots1 = sb([P, DV * PACK], BF16, "dz_slots1")
-        for u in range(2):
-            weave_slots(slots1[:, u * HALF * PACK : (u + 1) * HALF * PACK], 1, u)
-
-        for k in range(PACK):
-            x_gather(k)
-        x_slot = [sb([P, N * PACK], BF16, "x_slot", after) for after in ("h1", "ts_g")]
+        x_mx = []
         for pair in range(2):
-            for b in range(B):
-                x_weave(pair, b, "low%d" % (2 * pair + b), x_slot[pair])
-        x_mx = [x_operand(0, x_slot[0])]
-        dzs = [mx_tiles(DV, "dzs%d" % b) for b in range(B)]
-        for u in range(2):
-            quantize(dzs[0], slice(u * HALF, (u + 1) * HALF), slots0[u][:], E5M2)
-        quantize(dzs[1], slice(0, DV), slots1[:], E5M2)
-        x_mx.append(x_operand(1, x_slot[1]))
+            for k in range(max(2 * pair, 1), 2 * pair + 2):
+                x_gather(k)
+            x_mx.append(x_operand(pair))
+            staged = sb([P, N], F32, "staged%d_2" % pair)
+            dx_block(pair, 2, "f%d" % (2 * pair + 1), staged[:])
+            scatter_vector(pair, 2, staged[:])
 
-        last = PACK - 1
-        last_staged = sb([P, B * N], F32, "staged_last", "dz_t1_0")
-        for b in range(B):
-            dx_block(b, last, "high%d" % b, last_staged[:, b * N : (b + 1) * N])
-        nc.vector.tensor_copy(windows[last][:].indirect(offsets[:]), last_staged[:])
-
-        gw_blocks(0, x_mx[0], ("high0", "high1", "low0", "low1"), "dy0")
-        gw_blocks(1, x_mx[1], ("low2", "low3", "high2", "high3"), "dy1")
-        nc.scalar.dma_start(out_1[last * P :, :], windows[last][:])
+        gw_blocks(0, ("a0", "a1", "ts0", "ts1"), "h3")
+        gw_blocks(1, ("f0", "f2", "a0", "a1"), "dy1")
+        nc.scalar.dma_start(out_1[2 * P : 3 * P, :], windows[2][:])

@@ -1,3 +1,4 @@
+import math
 from contextlib import ExitStack
 
 import concourse.mybir as mybir
@@ -16,13 +17,16 @@ E5M2 = mybir.dt.float8_e5m2_x4
 MULT = mybir.AluOpType.mult
 ADD = mybir.AluOpType.add
 COPY = mybir.ActivationFunctionType.Copy
-SQUARE = mybir.ActivationFunctionType.Square
 
 P = 128
 PACK = 4
 HALF = N // 2
 GROUP = 16
 ALIGN = 64
+WIDTH = {F32: 4, BF16: 2, U32: 4, U8: 1}
+BANKS = ["l0", "l1", "l2", "l3", "u0", "u1", "u2", "u3"]
+BANK_BYTES = 2048
+LIST_BYTES = B * N * 4
 TS_ROW = P - 1
 LAST = PACK - 1
 
@@ -34,11 +38,25 @@ def tile_attend_gex_sig_wx_kernel(tc, xT, dyT, hT, ts, wm, offs, out_0, out_1):
         keep = ctx.enter_context(tc.tile_pool(name="keep", bufs=1))
         psum = ctx.enter_context(tc.psum_pool(name="psum", bufs=1))
 
-        def sb(shape, dtype, name, after=None, bufs=1):
-            return keep.tile(shape, dtype, name=name, tag=after or name, bufs=bufs, align_bytes=ALIGN)
+
+        place = {}
+        free = [0]
+
+        def sb(shape, dtype, name, after=None, skip=0, lead=0):
+            if after is None:
+                place[name] = free[0] + lead
+                size = lead + math.prod(shape[1:]) * WIDTH[dtype]
+                free[0] = free[0] + -(-size // ALIGN) * ALIGN
+            else:
+                place[name] = place[after] + skip
+            return keep.tile(shape, dtype, name=name, tag=name, align_bytes=ALIGN, offset=place[name])
+
+        banks = []
 
         def bank(shape, tag):
-            return psum.tile(shape, F32, name="bank_" + tag, tag=tag)
+            banks.append(tag)
+            name = "bank%d_%s" % (len(banks), tag)
+            return psum.tile(shape, F32, name=name, tag=name, offset=BANKS.index(tag) * BANK_BYTES)
 
         offsets = lists.tile([P, B * N // GROUP], U16, name="offsets")
         nc.sync.dma_start(offsets[:], offs)
@@ -52,13 +70,13 @@ def tile_attend_gex_sig_wx_kernel(tc, xT, dyT, hT, ts, wm, offs, out_0, out_1):
 
         ident = sb([P, P], F32, "ident")
         make_identity(nc, ident[:])
-        minus_one = sb([P, 1], F32, "minus_one")
-        nc.vector.memset(minus_one[:], -1.0)
         one = sb([P, 1], F32, "one")
-        nc.scalar.activation(one[:], minus_one[:], SQUARE)
+        nc.vector.memset(one[:], 1.0)
+        minus_one = sb([P, 1], F32, "minus_one")
+        nc.scalar.activation(minus_one[:], one[:], COPY, scale=-1.0)
 
-        def load(rows, shape, name, after=None):
-            raw = sb(shape, F32, name, after)
+        def load(rows, shape, name, after=None, lead=0):
+            raw = sb(shape, F32, name, after, lead=lead)
             nc.sync.dma_start(raw[:], rows)
             return raw
 
@@ -72,22 +90,19 @@ def tile_attend_gex_sig_wx_kernel(tc, xT, dyT, hT, ts, wm, offs, out_0, out_1):
         wm_raw = [load(wm[b].rearrange("(m j) d -> m j d", j=PACK), [P, PACK, D], "wm_raw%d" % b) for b in range(B)]
 
         windows = [sb([P, T], F32, "window%d" % k) for k in range(PACK)]
-        for k in (LAST, 0, 1, 2):
+        for k in range(PACK):
             nc.gpsimd.memset(windows[k][:], 0.0)
 
         ts_g = sb([P, B * N], F32, "ts_g")
-        nc.vector.tensor_copy(ts_g[:], ts_pool[:].indirect(offsets[:]))
-        ts_wide = []
+        nc.vector.tensor_copy(ts_g[:, :N], ts_pool[:].indirect(entries(0, N)))
+        nc.scalar.activation(ts_g[:, N:], ts_pool[:].indirect(entries(N, N)), COPY)
+        minus_ts = []
         for b in range(B):
-            turned = bank([P, PACK, P], "f%d" % b)
-            for q in range(PACK):
-                nc.tensor.transpose(turned[:, q, :], ts_g[:, b * N + q * P : b * N + (q + 1) * P], ident[:])
-            column = sb([P, PACK], F32, "ts_column%d" % b)
-            nc.vector.tensor_scalar_mul(column[:], turned[:, :, TS_ROW], -0.25)
-            wide = bank([P, PACK, P], "ts%d" % b)
-            for q in range(PACK):
-                nc.tensor.transpose(wide[:, q, :], column[:, q : q + 1].to_broadcast([P, P]), ident[:])
-            ts_wide.append(wide)
+            turned = bank([P, PACK, P], "l%d" % b)
+            for t in range(PACK):
+                nc.tensor.transpose(turned[:, t, :], ts_g[:, b * N + t : (b + 1) * N : PACK], ident[:])
+            minus_ts.append(sb([P, PACK], F32, "minus_ts%d" % b))
+            nc.vector.tensor_scalar_mul(minus_ts[b][:], turned[:, :, TS_ROW], -1.0)
 
         def mx_tiles(width, name):
             return sb([P, width], U32, name + "_codes"), sb([P, width], U8, name + "_scales")
@@ -95,70 +110,78 @@ def tile_attend_gex_sig_wx_kernel(tc, xT, dyT, hT, ts, wm, offs, out_0, out_1):
         def quantize(mx, cols, src, fmt):
             nc.vector.quantize_mx(out=mx[0][:, cols].bitcast(fmt), scales=mx[1][:, cols], in_=src)
 
-        def product(acc, left, e, right):
+        def product(acc, left, e, right, cols):
             nc.tensor.matmul_mx(
-                out=acc[:],
+                out=acc,
                 lhsT=left[0][:, e * P : (e + 1) * P].bitcast(E4M3),
                 lhsT_scale=left[1][:, e * P : (e + 1) * P],
-                rhs=right[0][:].bitcast(E5M2),
-                rhs_scale=right[1][:],
+                rhs=right[0][:, cols].bitcast(E5M2),
+                rhs_scale=right[1][:, cols],
                 start=True,
                 stop=True,
             )
 
-        def interleave(dst, planes):
-            nc.vector.tensor_copy(
+        def interleave(dst, planes, copy=nc.vector.tensor_copy):
+            copy(
                 dst.rearrange("p (a c j) -> p a j c", c=PACK, j=PACK),
                 planes.rearrange("p j (a c) -> p a j c", c=PACK),
             )
 
         halves = [slice(0, HALF), slice(HALF, N)]
-        dz = [sb([P, PACK, N], F32, "dz%d" % b) for b in range(B)]
-        dzs = [mx_tiles(DV, "dzs%d" % b) for b in range(B)]
         dzf = [mx_tiles(N, "dzf%d" % b) for b in range(B)]
+        wm_mx = [mx_tiles(D, "wm%d" % b) for b in range(B)]
+        fwd, back, dz_t = {}, {}, {}
 
-        def factor_of(b, j):
-            h_g = sb([P, N], F32, "h_g", bufs=2)
+        def reuse(name, j, first):
+            return (name % j, name % first if j != first else None)
+
+        def grad_plane(b, j, slope_after):
+            h_g = sb([P, N], F32, *reuse("h_g%d_%%d" % b, j, 0))
             nc.scalar.activation(h_g[:], h_pool[j][:].indirect(entries(b * N, N)), COPY)
-            square = sb([P, N], F32, "square", bufs=2)
-            nc.scalar.activation(square[:], h_g[:], SQUARE, bias=one[:], scale=-2.0)
-            factor = sb([P, N], F32, "factor", bufs=2)
-            nc.vector.scalar_tensor_tensor(
-                factor[:], square[:], -1.0, ts_wide[b][:].rearrange("p q s -> p (q s)"), ADD, MULT
-            )
-            return factor
-
-        def dz_plane(b, j):
-            nc.vector.tensor_tensor(dz[b][:, j, :], dy_pool[j][:].indirect(entries(b * N, N)), factor_of(b, j)[:], MULT)
-
-        def dz_by_slots(b, j):
-            turned = bank([P, PACK, P], "f%d" % ((2 * j + b) % PACK))
+            slope = sb([P, N], F32, "slope%d_%d" % (b, j), slope_after)
+            nc.vector.scalar_tensor_tensor(slope[:], h_g[:], minus_one[:], h_g[:], ADD, MULT)
+            grad = sb([P, N], F32, *reuse("grad%d_%%d" % b, j, j % 2))
+            nc.vector.tensor_tensor(grad[:], dy_pool[j][:].indirect(entries(b * N, N)), slope[:], MULT)
             for t in range(PACK):
-                nc.tensor.transpose(turned[:, t, :], dz[b][:, j, t::PACK], ident[:])
-            slots = sb([P, N], BF16, "dz_slots%d_%d" % (b, j))
-            nc.scalar.copy(slots[:].rearrange("p (m t) -> p m t", t=PACK), turned[:].rearrange("p t m -> p m t"))
-            quantize(dzs[b], slice(j * P, (j + 1) * P), slots[:], E5M2)
+                if j % 2 == 0 and t % 2 == 0:
+                    fwd[b, t // 2] = bank([P, 2, 2, P], "%s%d" % ("lu"[j // 2], 2 * b + t // 2))
+                nc.tensor.transpose(fwd[b, t // 2][:, t % 2, j % 2, :], grad[:, t::PACK], ident[:])
 
-        def dz_by_features(b):
-            feat = [sb([P, HALF * PACK], BF16, "feat%d_%d" % (b, half)) for half in range(2)]
+        def dz_part(b, u, t, count=1):
+            return dz_t[b, u][:, t * 2 * P : (t + count) * 2 * P]
+
+        def weigh(b, u, turned, after):
+            dz_t[b, u] = sb([P, PACK * 2 * P], BF16, "dz_t%d_%d" % (b, u), after)
             for half in range(2):
-                interleave(feat[half][:], dz[b][:, :, halves[half]])
-            for half in range(2):
-                quantize(dzf[b], halves[half], feat[half][:], E5M2)
+                for i in range(2):
+                    t = 2 * half + i
+                    nc.scalar.activation(
+                        dz_part(b, u, t).rearrange("p (m e) -> p m e", e=2),
+                        turned[b, half][:, i].rearrange("p e m -> p m e"),
+                        COPY,
+                        scale=minus_ts[b][:, t : t + 1],
+                    )
+                if u == 0:
+                    back[b, half] = bank([P, 2, 2, P], "l%d" % (2 * b + half))
+                for i in range(2):
+                    nc.tensor.transpose(back[b, half][:, i, u, :], dz_part(b, u, 2 * half + i).bitcast(F32), ident[:])
 
-        def wm_operand(b):
-            mx = mx_tiles(D, "wm%d" % b)
-            wm_bf = [sb([P, HALF * PACK], BF16, "wm_bf%d_%d" % (b, half)) for half in range(2)]
-            for half in (1, 0):
-                interleave(wm_bf[half][:], wm_raw[b][:, :, halves[half]])
-            for half in (1, 0):
-                quantize(mx, halves[half], wm_bf[half][:], E4M3)
-            return mx
+        def features(b, half, feat):
+            nc.scalar.copy(
+                feat.bitcast(F32).rearrange("p (s i u) -> p s i u", i=2, u=2),
+                back[b, half][:].rearrange("p i u s -> p s i u"),
+            )
 
-        def dx_block(b, k, tag, staged):
+        def dx_block(b, k, tag, after=None, copy=nc.scalar.copy, staged=None):
             acc = bank([P, N], tag)
-            product(acc, wm_mx[b], k, dzf[b])
-            nc.scalar.copy(staged, acc[:])
+            product(acc[:], wm_mx[b], k, dzf[b], slice(0, N))
+            if staged is None:
+                staged = sb([P, N], F32, "staged%d_%d" % (b, k), after)[:]
+            copy(
+                staged.rearrange("p (s h i) -> p s h i", h=2, i=2),
+                acc[:].rearrange("p (h s i) -> p s h i", h=2, i=2),
+            )
+            return staged
 
         def store_window(k):
             nc.sync.dma_start(out_1[k * P : (k + 1) * P, :], windows[k][:])
@@ -166,32 +189,62 @@ def tile_attend_gex_sig_wx_kernel(tc, xT, dyT, hT, ts, wm, offs, out_0, out_1):
         def scatter_vector(b, k, staged):
             nc.vector.tensor_copy(windows[k][:].indirect(entries(b * N, N)), staged)
 
-        def scatter_scalar(b, k, staged):
-            for half in range(2):
-                nc.scalar.activation(
-                    windows[k][:].indirect(entries(b * N + half * HALF, HALF)), staged[:, halves[half]], COPY
-                )
-
-        for j in range(PACK):
+        for j in range(2):
             for b in range(B):
-                dz_plane(b, j)
-                if j == LAST:
-                    dz_by_features(b)
-                dz_by_slots(b, j)
+                grad_plane(b, j, "slope%d_0" % b if j else None)
+        first_pair = dict(fwd)
+        for b in range(B):
+            grad_plane(b, 2, "slope%d_0" % b)
+        weigh(0, 0, first_pair, "h2")
+        for b in range(B):
+            grad_plane(b, LAST, "slope0_0")
+        weigh(1, 0, first_pair, "h3")
+        x_pool = [load(x_rows[k], [P, T], "x_pool%d" % k, ("h0", "h1", None, None)[k], (0, 0, LIST_BYTES, 0)[k]) for k in range(PACK)]
 
-        x_pool = [load(x_rows[k], [P, T], "x_pool%d" % k, "h%d" % k) for k in range(PACK)]
-        wm_mx = [wm_operand(b) for b in range(B)]
+        wm_bf = [sb([P, D * PACK], BF16, "wm_bf0")]
+        feat = [sb([P, HALF * PACK], BF16, "feat0_%d" % half, (None, "dy0")[half]) for half in range(2)]
+        weigh(0, 1, fwd, None)
+        for half in range(2):
+            features(0, half, feat[half][:])
+        interleave(wm_bf[0][:], wm_raw[0][:])
+        quantize(dzf[0], halves[0], feat[0][:], E5M2)
+        quantize(wm_mx[0], slice(0, D), wm_bf[0][:], E4M3)
+        quantize(dzf[0], halves[1], feat[1][:], E5M2)
+        weigh(1, 1, fwd, "feat0_0")
+        wm_bf.append(sb([P, D * PACK], BF16, "wm_bf1", "dy0"))
+        nc.gpsimd.tensor_copy(wm_bf[1][:].rearrange("p (c j) -> p c j", j=PACK), wm_raw[1][:].rearrange("p j c -> p c j"))
+        staged = dx_block(0, 0, "u0", None, nc.vector.tensor_copy)
+        feat1 = sb([P, N * PACK], BF16, "feat1", "dy2")
+        for half in range(2):
+            features(1, half, feat1[:, half * HALF * PACK : (half + 1) * HALF * PACK])
+        scatter_vector(0, 0, staged)
+        dzf[1] = (sb([P, N], U32, "dzf1_late", "staged0_0"), dzf[1][1])
+        quantize(wm_mx[1], slice(0, D), wm_bf[1][:], E4M3)
+        quantize(dzf[1], slice(0, N), feat1[:], E5M2)
+
+        weave = sb([P, B, DV * PACK], BF16, "dz_slots", "dy2")
+        slots = [weave[:, b, :] for b in range(B)]
+        for b in range(B):
+            for u in range(2):
+                nc.gpsimd.tensor_scalar(
+                    slots[b][:, u * HALF * PACK : (u + 1) * HALF * PACK].rearrange("p (c t) -> p c t", t=PACK),
+                    dz_part(b, u, 0, PACK).rearrange("p (t c) -> p c t", t=PACK),
+                    1.0, 0.0, MULT, ADD,
+                )
 
         x_g = {}
 
-        def x_gather(k):
-            x_g[k] = sb([P, B * N], BF16, "x_g%d" % k)
-            nc.scalar.activation(x_g[k][:], x_pool[k][:].indirect(offsets[:]), COPY)
+        def x_gather(k, after=None):
+            x_g[k] = sb([P, B * N], BF16, "x_g%d" % k, after)
+            if k != LAST:
+                nc.scalar.activation(x_g[k][:], x_pool[k][:].indirect(offsets[:]), COPY)
+            else:
+                nc.vector.tensor_copy(x_g[k][:], x_pool[k][:].indirect(offsets[:]))
 
-        def x_operand(pair):
-            x_slot = sb([P, N * PACK], BF16, "x_slot%d" % pair)
+        def x_turned(pair, tags, after=None, skip=0):
+            x_slot = sb([P, N * PACK], BF16, "x_slot%d" % pair, after, skip)
             for b in range(B):
-                turned = bank([P, 2, 2, P], "f%d" % (2 * pair + b))
+                turned = bank([P, 2, 2, P], tags[b])
                 for i in range(2):
                     words = x_g[2 * pair + i][:].bitcast(F32)
                     for v in range(2):
@@ -200,51 +253,55 @@ def tile_attend_gex_sig_wx_kernel(tc, xT, dyT, hT, ts, wm, offs, out_0, out_1):
                     x_slot[:].bitcast(F32)[:, b * N : (b + 1) * N].rearrange("p (i d v) -> p i d v", i=2, v=2),
                     turned[:].rearrange("p i v d -> p i d v"),
                 )
-            mx = mx_tiles(N, "x%d" % pair)
+            return x_slot
+
+        def x_operand(pair, x_slot, after=None):
+            mx = sb([P, N], U32, "x%d_codes" % pair, after), sb([P, N], U8, "x%d_scales" % pair)
             quantize(mx, slice(0, N), x_slot[:], E4M3)
             return mx
 
-        def gw_blocks(pair, tags, after):
-            gw = sb([P, PACK, DV], F32, "gw", after)
+        def gw_blocks(pair, x_mx, tags, after):
+            gw = sb([P, PACK, DV], F32, "gw%d" % pair, after)
             for b in range(B):
                 for i in range(2):
                     acc = bank([P, DV], tags[2 * b + i])
-                    product(acc, x_mx[pair], 2 * b + i, dzs[b])
+                    product(acc[:], x_mx, 2 * b + i, dzs[b], slice(0, DV))
                     nc.scalar.copy(
-                        gw[:, 2 * b + i, :].rearrange("p (m j) -> p m j", j=PACK),
-                        acc[:].rearrange("p (j m) -> p m j", j=PACK),
+                        gw[:, 2 * b + i, :].rearrange("p (m u e) -> p m u e", u=2, e=2),
+                        acc[:].rearrange("p (u m e) -> p m u e", u=2, e=2),
                     )
                     k = 2 * pair + i
                     nc.sync.dma_start(out_0[b, k * P : (k + 1) * P, :], gw[:, 2 * b + i, :])
 
-        staged = sb([P, N], F32, "staged0_3")
-        dx_block(0, LAST, "a0", staged[:])
-        scatter_scalar(0, LAST, staged)
-        for k, tag, after in ((0, "a1", "wm_raw1"), (1, "ts0", None)):
-            staged = sb([P, N], F32, "staged0_%d" % k, after)
-            dx_block(0, k, tag, staged[:])
-            scatter_vector(0, k, staged[:])
-
+        by_vector = nc.vector.tensor_copy
+        scatter_vector(0, 1, dx_block(0, 1, "u1", "wm_raw1"))
         x_gather(0)
-        staged = sb([P, 3, N], F32, "staged1", "h0")
-        dx_block(1, LAST, "a0", staged[:, 0, :])
-        for k, tag in ((0, "a1"), (1, "ts1")):
-            dx_block(1, k, tag, staged[:, 1 + k, :])
-        scatter_scalar(1, LAST, staged[:, 0, :])
-        store_window(LAST)
+        x_gather(1)
+        staged = sb([P, 2, N], F32, "staged_pair", "x_pool1")
         for k in range(2):
-            scatter_vector(1, k, staged[:, 1 + k, :])
+            scatter_vector(1, k, dx_block(1, k, "u%d" % (2 + k), staged=staged[:, k, :]))
             store_window(k)
+        x_slot = x_turned(0, ("l0", "l1"))
+        x_gather(2, "dy0")
+        dzs = [
+            (sb([P, DV], U32, "dzs%d_codes" % b, "staged_pair", b * DV * WIDTH[U32]), sb([P, DV], U8, "dzs%d_scales" % b))
+            for b in range(B)
+        ]
+        for b in range(B):
+            quantize(dzs[b], slice(0, DV), slots[b], E5M2)
+        x_mx = [x_operand(0, x_slot)]
 
-        x_mx = []
-        for pair in range(2):
-            for k in range(max(2 * pair, 1), 2 * pair + 2):
-                x_gather(k)
-            x_mx.append(x_operand(pair))
-            staged = sb([P, N], F32, "staged%d_2" % pair)
-            dx_block(pair, 2, "f%d" % (2 * pair + 1), staged[:])
-            scatter_vector(pair, 2, staged[:])
+        staged = sb([P, B * N], F32, "staged_last", "x_pool2", -LIST_BYTES // 2)
+        for b in range(B):
+            dx_block(b, LAST, "l%d" % b, staged=staged[:, b * N : (b + 1) * N])
+        for first, count in ((0, 384), (384, 384), (768, 256)):
+            nc.scalar.activation(windows[LAST][:].indirect(entries(first, count)), staged[:, first : first + count], COPY)
+        nc.scalar.dma_start(out_1[LAST * P :, :], windows[LAST][:])
 
-        gw_blocks(0, ("a0", "a1", "ts0", "ts1"), "h3")
-        gw_blocks(1, ("f0", "f2", "a0", "a1"), "dy1")
+        x_gather(3)
+        scatter_vector(0, 2, dx_block(0, 2, "l2", "x_pool3", by_vector))
+        x_mx.append(x_operand(1, x_turned(1, ("u0", "u1"), "x_pool2", -LIST_BYTES)))
+        scatter_vector(1, 2, dx_block(1, 2, "u1"))
+        gw_blocks(0, x_mx[0], ("l3", "u2", "u3", "l0"), "x_pool2")
+        gw_blocks(1, x_mx[1], ("l1", "u0", "l3", "u2"), "dy1")
         nc.scalar.dma_start(out_1[2 * P : 3 * P, :], windows[2][:])

@@ -26,7 +26,6 @@ ALIGN = 64
 WIDTH = {F32: 4, BF16: 2, U32: 4, U8: 1}
 BANKS = ["l0", "l1", "l2", "l3", "u0", "u1", "u2", "u3"]
 BANK_BYTES = 2048
-LIST_BYTES = B * N * 4
 TS_ROW = P - 1
 LAST = PACK - 1
 
@@ -42,10 +41,10 @@ def tile_attend_gex_sig_wx_kernel(tc, xT, dyT, hT, ts, wm, offs, out_0, out_1):
         place = {}
         free = [0]
 
-        def sb(shape, dtype, name, after=None, skip=0, lead=0):
+        def sb(shape, dtype, name, after=None, skip=0):
             if after is None:
-                place[name] = free[0] + lead
-                size = lead + math.prod(shape[1:]) * WIDTH[dtype]
+                place[name] = free[0]
+                size = math.prod(shape[1:]) * WIDTH[dtype]
                 free[0] = free[0] + -(-size // ALIGN) * ALIGN
             else:
                 place[name] = place[after] + skip
@@ -75,8 +74,8 @@ def tile_attend_gex_sig_wx_kernel(tc, xT, dyT, hT, ts, wm, offs, out_0, out_1):
         minus_one = sb([P, 1], F32, "minus_one")
         nc.scalar.activation(minus_one[:], one[:], COPY, scale=-1.0)
 
-        def load(rows, shape, name, after=None, lead=0):
-            raw = sb(shape, F32, name, after, lead=lead)
+        def load(rows, shape, name, after=None):
+            raw = sb(shape, F32, name, after)
             nc.sync.dma_start(raw[:], rows)
             return raw
 
@@ -199,7 +198,7 @@ def tile_attend_gex_sig_wx_kernel(tc, xT, dyT, hT, ts, wm, offs, out_0, out_1):
         for b in range(B):
             grad_plane(b, LAST, "slope0_0")
         weigh(1, 0, first_pair, "h3")
-        x_pool = [load(x_rows[k], [P, T], "x_pool%d" % k, ("h0", "h1", None, None)[k], (0, 0, LIST_BYTES, 0)[k]) for k in range(PACK)]
+        x_pool = [load(x_rows[k], [P, T], "x_pool%d" % k, ("h0", "h1", None, None)[k]) for k in range(PACK)]
 
         wm_bf = [sb([P, D * PACK], BF16, "wm_bf0")]
         feat = [sb([P, HALF * PACK], BF16, "feat0_%d" % half, (None, "dy0")[half]) for half in range(2)]
@@ -236,13 +235,10 @@ def tile_attend_gex_sig_wx_kernel(tc, xT, dyT, hT, ts, wm, offs, out_0, out_1):
 
         def x_gather(k, after=None):
             x_g[k] = sb([P, B * N], BF16, "x_g%d" % k, after)
-            if k != LAST:
-                nc.scalar.activation(x_g[k][:], x_pool[k][:].indirect(offsets[:]), COPY)
-            else:
-                nc.vector.tensor_copy(x_g[k][:], x_pool[k][:].indirect(offsets[:]))
+            nc.scalar.activation(x_g[k][:], x_pool[k][:].indirect(offsets[:]), COPY)
 
-        def x_turned(pair, tags, after=None, skip=0):
-            x_slot = sb([P, N * PACK], BF16, "x_slot%d" % pair, after, skip)
+        def x_turned(pair, tags):
+            x_slot = sb([P, N * PACK], BF16, "x_slot%d" % pair)
             for b in range(B):
                 turned = bank([P, 2, 2, P], tags[b])
                 for i in range(2):
@@ -282,7 +278,6 @@ def tile_attend_gex_sig_wx_kernel(tc, xT, dyT, hT, ts, wm, offs, out_0, out_1):
             scatter_vector(1, k, dx_block(1, k, "u%d" % (2 + k), staged=staged[:, k, :]))
             store_window(k)
         x_slot = x_turned(0, ("l0", "l1"))
-        x_gather(2, "dy0")
         dzs = [
             (sb([P, DV], U32, "dzs%d_codes" % b, "staged_pair", b * DV * WIDTH[U32]), sb([P, DV], U8, "dzs%d_scales" % b))
             for b in range(B)
@@ -291,17 +286,17 @@ def tile_attend_gex_sig_wx_kernel(tc, xT, dyT, hT, ts, wm, offs, out_0, out_1):
             quantize(dzs[b], slice(0, DV), slots[b], E5M2)
         x_mx = [x_operand(0, x_slot)]
 
-        staged = sb([P, B * N], F32, "staged_last", "x_pool2", -LIST_BYTES // 2)
-        for b in range(B):
-            dx_block(b, LAST, "l%d" % b, staged=staged[:, b * N : (b + 1) * N])
-        for first, count in ((0, 384), (384, 384), (768, 256)):
-            nc.scalar.activation(windows[LAST][:].indirect(entries(first, count)), staged[:, first : first + count], COPY)
-        nc.scalar.dma_start(out_1[LAST * P :, :], windows[LAST][:])
+        staged = [dx_block(b, LAST, "l%d" % b) for b in range(B)]
+        for half in range(2):
+            nc.scalar.activation(windows[LAST][:].indirect(entries(half * HALF, HALF)), staged[0][:, halves[half]], COPY)
+        scatter_vector(1, LAST, staged[1])
+        store_window(LAST)
 
-        x_gather(3)
-        scatter_vector(0, 2, dx_block(0, 2, "l2", "x_pool3", by_vector))
-        x_mx.append(x_operand(1, x_turned(1, ("u0", "u1"), "x_pool2", -LIST_BYTES)))
+        x_gather(2, "staged0_3")
+        scatter_vector(0, 2, dx_block(0, 2, "l2", "x_pool2"))
+        x_gather(3, "dy0")
+        x_mx.append(x_operand(1, x_turned(1, ("u0", "u1"))))
         scatter_vector(1, 2, dx_block(1, 2, "u1"))
-        gw_blocks(0, x_mx[0], ("l3", "u2", "u3", "l0"), "x_pool2")
+        gw_blocks(0, x_mx[0], ("l3", "u2", "u3", "l0"), "x_g3")
         gw_blocks(1, x_mx[1], ("l1", "u0", "l3", "u2"), "dy1")
         nc.scalar.dma_start(out_1[2 * P : 3 * P, :], windows[2][:])

@@ -26,6 +26,7 @@ ALIGN = 64
 WIDTH = {F32: 4, BF16: 2, U32: 4, U8: 1}
 BANKS = ["l0", "l1", "l2", "l3", "u0", "u1", "u2", "u3"]
 BANK_BYTES = 2048
+PIECE = 384
 TS_ROW = P - 1
 LAST = PACK - 1
 
@@ -233,26 +234,28 @@ def tile_attend_gex_sig_wx_kernel(tc, xT, dyT, hT, ts, wm, offs, out_0, out_1):
 
         x_g = {}
 
-        def x_gather(k, after=None):
-            x_g[k] = sb([P, B * N], BF16, "x_g%d" % k, after)
-            nc.scalar.activation(x_g[k][:], x_pool[k][:].indirect(offsets[:]), COPY)
+        def x_gather(k):
+            both = sb([P, B * N], BF16, "x_g%d" % k)
+            nc.scalar.activation(both[:], x_pool[k][:].indirect(offsets[:]), COPY)
+            for b in range(B):
+                x_g[k, b] = both[:, b * N : (b + 1) * N]
 
         def x_turned(pair, tags):
             x_slot = sb([P, N * PACK], BF16, "x_slot%d" % pair)
             for b in range(B):
                 turned = bank([P, 2, 2, P], tags[b])
                 for i in range(2):
-                    words = x_g[2 * pair + i][:].bitcast(F32)
+                    words = x_g[2 * pair + i, b].bitcast(F32)
                     for v in range(2):
-                        nc.tensor.transpose(turned[:, i, v, :], words[:, b * HALF + v : (b + 1) * HALF : 2], ident[:])
+                        nc.tensor.transpose(turned[:, i, v, :], words[:, v::2], ident[:])
                 nc.scalar.copy(
                     x_slot[:].bitcast(F32)[:, b * N : (b + 1) * N].rearrange("p (i d v) -> p i d v", i=2, v=2),
                     turned[:].rearrange("p i v d -> p i d v"),
                 )
             return x_slot
 
-        def x_operand(pair, x_slot, after=None):
-            mx = sb([P, N], U32, "x%d_codes" % pair, after), sb([P, N], U8, "x%d_scales" % pair)
+        def x_operand(pair, x_slot, after=None, skip=0):
+            mx = sb([P, N], U32, "x%d_codes" % pair, after, skip), sb([P, N], U8, "x%d_scales" % pair)
             quantize(mx, slice(0, N), x_slot[:], E4M3)
             return mx
 
@@ -278,25 +281,31 @@ def tile_attend_gex_sig_wx_kernel(tc, xT, dyT, hT, ts, wm, offs, out_0, out_1):
             scatter_vector(1, k, dx_block(1, k, "u%d" % (2 + k), staged=staged[:, k, :]))
             store_window(k)
         x_slot = x_turned(0, ("l0", "l1"))
-        dzs = [
-            (sb([P, DV], U32, "dzs%d_codes" % b, "staged_pair", b * DV * WIDTH[U32]), sb([P, DV], U8, "dzs%d_scales" % b))
-            for b in range(B)
-        ]
+        x_gather(2)
+        x_g[LAST, 0] = sb([P, N], BF16, "x_g3_0", "x_pool2", 3 * N * WIDTH[F32])[:]
+        nc.scalar.activation(x_g[LAST, 0], x_pool[LAST][:].indirect(entries(0, N)), COPY)
+        x_g[LAST, 1] = sb([P, N], BF16, "x_g3_1", "staged_pair")[:]
+        nc.vector.tensor_copy(x_g[LAST, 1], x_pool[LAST][:].indirect(entries(N, N)))
+        quarter = N * WIDTH[F32]
+        dzs = [(sb([P, DV], U32, "dzs%d_codes" % b, "x_pool3", b * quarter), sb([P, DV], U8, "dzs%d_scales" % b)) for b in range(B)]
         for b in range(B):
             quantize(dzs[b], slice(0, DV), slots[b], E5M2)
-        x_mx = [x_operand(0, x_slot)]
+        x_mx = [x_operand(0, x_slot, "x_pool3", 2 * quarter)]
 
-        staged = [dx_block(b, LAST, "l%d" % b) for b in range(B)]
-        for half in range(2):
-            nc.scalar.activation(windows[LAST][:].indirect(entries(half * HALF, HALF)), staged[0][:, halves[half]], COPY)
-        scatter_vector(1, LAST, staged[1])
-        store_window(LAST)
+        staged = sb([P, B * N], F32, "staged_last", "x_pool2")
+        for b in range(B):
+            dx_block(b, LAST, "l%d" % b, staged=staged[:, b * N : (b + 1) * N])
 
-        x_gather(2, "staged0_3")
-        scatter_vector(0, 2, dx_block(0, 2, "l2", "x_pool2"))
-        x_gather(3, "dy0")
+        def scatter_scalar(first, count):
+            nc.scalar.activation(windows[LAST][:].indirect(entries(first, count)), staged[:, first : first + count], COPY)
+
+        scatter_scalar(0, PIECE)
+        scatter_vector(0, 2, dx_block(0, 2, "l2", staged=sb([P, N], F32, "staged0_2", "x_pool3", 3 * quarter)[:]))
+        scatter_scalar(PIECE, PIECE)
         x_mx.append(x_operand(1, x_turned(1, ("u0", "u1"))))
         scatter_vector(1, 2, dx_block(1, 2, "u1"))
-        gw_blocks(0, x_mx[0], ("l3", "u2", "u3", "l0"), "x_g3")
+        scatter_scalar(2 * PIECE, B * N - 2 * PIECE)
+        nc.scalar.dma_start(out_1[LAST * P :, :], windows[LAST][:])
+        gw_blocks(0, x_mx[0], ("l3", "u2", "u3", "l0"), "x_pool2")
         gw_blocks(1, x_mx[1], ("l1", "u0", "l3", "u2"), "dy1")
         nc.scalar.dma_start(out_1[2 * P : 3 * P, :], windows[2][:])

@@ -199,7 +199,10 @@ def tile_attend_gex_sig_wx_kernel(tc, xT, dyT, hT, ts, wm, offs, out_0, out_1):
         for b in range(B):
             grad_plane(b, LAST, "slope0_0")
         weigh(1, 0, first_pair, "h3")
-        x_pool = [load(x_rows[k], [P, T], "x_pool%d" % k, ("h0", "h1", None, None)[k]) for k in range(PACK)]
+        x_pool = [load(x_rows[k], [P, T], "x_pool%d" % k, "h%d" % k) for k in range(2)]
+        x_late = sb([P, 2, T], F32, "x_late")
+        for e in range(2):
+            nc.sync.dma_start(x_late[:, e, :], x_rows[2 + e])
 
         wm_bf = [sb([P, D * PACK], BF16, "wm_bf0")]
         feat = [sb([P, HALF * PACK], BF16, "feat0_%d" % half, (None, "dy0")[half]) for half in range(2)]
@@ -281,31 +284,36 @@ def tile_attend_gex_sig_wx_kernel(tc, xT, dyT, hT, ts, wm, offs, out_0, out_1):
             scatter_vector(1, k, dx_block(1, k, "u%d" % (2 + k), staged=staged[:, k, :]))
             store_window(k)
         x_slot = x_turned(0, ("l0", "l1"))
-        x_gather(2)
-        x_g[LAST, 0] = sb([P, N], BF16, "x_g3_0", "x_pool2", 3 * N * WIDTH[F32])[:]
-        nc.scalar.activation(x_g[LAST, 0], x_pool[LAST][:].indirect(entries(0, N)), COPY)
-        x_g[LAST, 1] = sb([P, N], BF16, "x_g3_1", "staged_pair")[:]
-        nc.vector.tensor_copy(x_g[LAST, 1], x_pool[LAST][:].indirect(entries(N, N)))
+        x_pairs = sb([P, T, 2], BF16, "x_pairs", "x_pool0")
+        nc.gpsimd.tensor_copy(x_pairs[:], x_late[:].rearrange("p e c -> p c e"))
+        words = sb([P, B * N], U32, "x_words", "staged_pair")
+        nc.vector.tensor_copy(words[:], x_pairs[:].rearrange("p c e -> p (c e)").bitcast(U32).indirect(offsets[:]))
         quarter = N * WIDTH[F32]
-        dzs = [(sb([P, DV], U32, "dzs%d_codes" % b, "x_pool3", b * quarter), sb([P, DV], U8, "dzs%d_scales" % b)) for b in range(B)]
+        dzs = [(sb([P, DV], U32, "dzs%d_codes" % b, "x_pool0", b * quarter), sb([P, DV], U8, "dzs%d_scales" % b)) for b in range(B)]
         for b in range(B):
             quantize(dzs[b], slice(0, DV), slots[b], E5M2)
-        x_mx = [x_operand(0, x_slot, "x_pool3", 2 * quarter)]
+        x_mx = [x_operand(0, x_slot, "x_pool0", 2 * quarter)]
 
-        staged = sb([P, B * N], F32, "staged_last", "x_pool2")
+        staged = sb([P, B * N], F32, "staged_last", "dy1")
         for b in range(B):
             dx_block(b, LAST, "l%d" % b, staged=staged[:, b * N : (b + 1) * N])
-
-        def scatter_scalar(first, count):
+        for first in range(0, B * N, PIECE):
+            count = min(PIECE, B * N - first)
             nc.scalar.activation(windows[LAST][:].indirect(entries(first, count)), staged[:, first : first + count], COPY)
-
-        scatter_scalar(0, PIECE)
-        scatter_vector(0, 2, dx_block(0, 2, "l2", staged=sb([P, N], F32, "staged0_2", "x_pool3", 3 * quarter)[:]))
-        scatter_scalar(PIECE, PIECE)
-        x_mx.append(x_operand(1, x_turned(1, ("u0", "u1"))))
-        scatter_vector(1, 2, dx_block(1, 2, "u1"))
-        scatter_scalar(2 * PIECE, B * N - 2 * PIECE)
         nc.scalar.dma_start(out_1[LAST * P :, :], windows[LAST][:])
-        gw_blocks(0, x_mx[0], ("l3", "u2", "u3", "l0"), "x_pool2")
+
+        scatter_vector(0, 2, dx_block(0, 2, "l2", staged=sb([P, N], F32, "staged0_2", "x_pool0", 3 * quarter)[:]))
+        x_slot = sb([P, N * PACK], BF16, "x_slot1")
+        for b in range(B):
+            turned = bank([P, PACK, P], "u%d" % b)
+            for t in range(PACK):
+                nc.tensor.transpose(turned[:, t, :], words[:].bitcast(F32)[:, b * N + t : (b + 1) * N : PACK], ident[:])
+            nc.scalar.copy(
+                x_slot[:, b * HALF * PACK : (b + 1) * HALF * PACK].rearrange("p (e d t) -> p e d t", e=2, t=PACK),
+                turned[:].rearrange("p t d -> p (t d)").bitcast(BF16).rearrange("p (t d e) -> p e d t", t=PACK, e=2),
+            )
+        x_mx.append(x_operand(1, x_slot))
+        scatter_vector(1, 2, dx_block(1, 2, "u1"))
+        gw_blocks(0, x_mx[0], ("l3", "u2", "u3", "l0"), "x_words")
         gw_blocks(1, x_mx[1], ("l1", "u0", "l3", "u2"), "dy1")
         nc.scalar.dma_start(out_1[2 * P : 3 * P, :], windows[2][:])

@@ -59,7 +59,6 @@ def tile_attend_gex_sig_wx_kernel(tc, xT, dyT, hT, ts, wm, offs, out_0, out_1):
             return psum.tile(shape, F32, name=name, tag=name, offset=BANKS.index(tag) * BANK_BYTES)
 
         offsets = lists.tile([P, B * N // GROUP], U16, name="offsets")
-        nc.sync.dma_start(offsets[:], offs)
 
         def entries(first, count):
             return offsets[:, first // GROUP : (first + count) // GROUP]
@@ -86,6 +85,8 @@ def tile_attend_gex_sig_wx_kernel(tc, xT, dyT, hT, ts, wm, offs, out_0, out_1):
         h_pool, dy_pool = [], []
         for j in range(PACK):
             h_pool.append(load(h_rows[j], [P, T], "h%d" % j))
+            if j == 0:
+                nc.sync.dma_start(offsets[:], offs)
             dy_pool.append(load(dy_rows[j], [P, T], "dy%d" % j))
         wm_raw = [load(wm[b].rearrange("(m j) d -> m j d", j=PACK), [P, PACK, D], "wm_raw%d" % b) for b in range(B)]
 
@@ -94,8 +95,7 @@ def tile_attend_gex_sig_wx_kernel(tc, xT, dyT, hT, ts, wm, offs, out_0, out_1):
             nc.gpsimd.memset(windows[k][:], 0.0)
 
         ts_g = sb([P, B * N], F32, "ts_g")
-        nc.vector.tensor_copy(ts_g[:, :N], ts_pool[:].indirect(entries(0, N)))
-        nc.scalar.activation(ts_g[:, N:], ts_pool[:].indirect(entries(N, N)), COPY)
+        nc.vector.tensor_copy(ts_g[:], ts_pool[:].indirect(offsets[:]))
         minus_ts = []
         for b in range(B):
             turned = bank([P, PACK, P], "l%d" % b)
@@ -225,15 +225,18 @@ def tile_attend_gex_sig_wx_kernel(tc, xT, dyT, hT, ts, wm, offs, out_0, out_1):
         quantize(wm_mx[1], slice(0, D), wm_bf[1][:], E4M3)
         quantize(dzf[1], slice(0, N), feat1[:], E5M2)
 
-        weave = sb([P, B, DV * PACK], BF16, "dz_slots", "dy2")
-        slots = [weave[:, b, :] for b in range(B)]
-        for b in range(B):
-            for u in range(2):
-                nc.gpsimd.tensor_scalar(
-                    slots[b][:, u * HALF * PACK : (u + 1) * HALF * PACK].rearrange("p (c t) -> p c t", t=PACK),
-                    dz_part(b, u, 0, PACK).rearrange("p (t c) -> p c t", t=PACK),
-                    1.0, 0.0, MULT, ADD,
-                )
+        def weave(slots, b, u):
+            nc.gpsimd.tensor_scalar(
+                slots.rearrange("p (c t) -> p c t", t=PACK),
+                dz_part(b, u, 0, PACK).rearrange("p (t c) -> p c t", t=PACK),
+                1.0, 0.0, MULT, ADD,
+            )
+
+        early = sb([P, HALF * PACK], BF16, "dz_slots_early", "wm_raw1", N * WIDTH[F32])
+        weave(early[:], 0, 0)
+        later = sb([P, 3, HALF * PACK], BF16, "dz_slots", "dy2")
+        for i, (b, u) in enumerate(((0, 1), (1, 0), (1, 1))):
+            weave(later[:, i, :], b, u)
 
         x_g = {}
 
@@ -286,13 +289,14 @@ def tile_attend_gex_sig_wx_kernel(tc, xT, dyT, hT, ts, wm, offs, out_0, out_1):
         x_slot = x_turned(0, ("l0", "l1"))
         x_pairs = sb([P, T, 2], BF16, "x_pairs", "x_pool0")
         nc.gpsimd.tensor_copy(x_pairs[:], x_late[:].rearrange("p e c -> p c e"))
-        words = sb([P, B * N], U32, "x_words", "staged_pair")
+        words = sb([P, B * N], U32, "x_words", "staged_pair", 2 * N * WIDTH[F32])
         nc.vector.tensor_copy(words[:], x_pairs[:].rearrange("p c e -> p (c e)").bitcast(U32).indirect(offsets[:]))
         quarter = N * WIDTH[F32]
-        dzs = [(sb([P, DV], U32, "dzs%d_codes" % b, "x_pool0", b * quarter), sb([P, DV], U8, "dzs%d_scales" % b)) for b in range(B)]
-        for b in range(B):
-            quantize(dzs[b], slice(0, DV), slots[b], E5M2)
-        x_mx = [x_operand(0, x_slot, "x_pool0", 2 * quarter)]
+        dzs = [(sb([P, DV], U32, "dzs%d_codes" % b, "x_late", b * quarter), sb([P, DV], U8, "dzs%d_scales" % b)) for b in range(B)]
+        quantize(dzs[0], halves[0], early[:], E5M2)
+        quantize(dzs[0], halves[1], later[:, 0, :], E5M2)
+        quantize(dzs[1], slice(0, DV), later[:, 1:, :].rearrange("p u c -> p (u c)"), E5M2)
+        x_mx = [x_operand(0, x_slot, "x_late", 2 * quarter)]
 
         staged = sb([P, B * N], F32, "staged_last", "dy1")
         for b in range(B):
@@ -314,6 +318,6 @@ def tile_attend_gex_sig_wx_kernel(tc, xT, dyT, hT, ts, wm, offs, out_0, out_1):
             )
         x_mx.append(x_operand(1, x_slot))
         scatter_vector(1, 2, dx_block(1, 2, "u1"))
-        gw_blocks(0, x_mx[0], ("l3", "u2", "u3", "l0"), "x_words")
+        gw_blocks(0, x_mx[0], ("l3", "u2", "u3", "l0"), "staged_pair")
         gw_blocks(1, x_mx[1], ("l1", "u0", "l3", "u2"), "dy1")
         nc.scalar.dma_start(out_1[2 * P : 3 * P, :], windows[2][:])

@@ -128,9 +128,9 @@ def tile_attend_gex_sig_wx_kernel(tc, xT, dyT, hT, ts, wm, offs, out_0, out_1):
             )
 
         halves = [slice(0, HALF), slice(HALF, N)]
-        dzf = [mx_tiles(N, "dzf%d" % b) for b in range(B)]
+        dzf = [mx_tiles(N, "dzf0")]
         wm_mx = [mx_tiles(D, "wm%d" % b) for b in range(B)]
-        fwd, back, dz_t = {}, {}, {}
+        grads, fwd, back, dz_t = {}, {}, {}, {}
 
         def reuse(name, j, first):
             return (name % j, name % first if j != first else None)
@@ -142,10 +142,16 @@ def tile_attend_gex_sig_wx_kernel(tc, xT, dyT, hT, ts, wm, offs, out_0, out_1):
             nc.vector.scalar_tensor_tensor(slope[:], h_g[:], minus_one[:], h_g[:], ADD, MULT)
             grad = sb([P, N], F32, *reuse("grad%d_%%d" % b, j, j % 2))
             nc.vector.tensor_tensor(grad[:], dy_pool[j][:].indirect(entries(b * N, N)), slope[:], MULT)
-            for t in range(PACK):
-                if j % 2 == 0 and t % 2 == 0:
-                    fwd[b, t // 2] = bank([P, 2, 2, P], "%s%d" % ("lu"[j // 2], 2 * b + t // 2))
-                nc.tensor.transpose(fwd[b, t // 2][:, t % 2, j % 2, :], grad[:, t::PACK], ident[:])
+            grads[b, j] = grad
+            if b == 0 or j < 2:
+                for half in range(2):
+                    turn(b, j, half, "%s%d" % ("lu"[j // 2], 2 * b + half))
+
+        def turn(b, j, half, tag):
+            if j % 2 == 0:
+                fwd[b, half] = bank([P, 2, 2, P], tag)
+            for i in range(2):
+                nc.tensor.transpose(fwd[b, half][:, i, j % 2, :], grads[b, j][:, 2 * half + i :: PACK], ident[:])
 
         def dz_part(b, u, t, count=1):
             return dz_t[b, u][:, t * 2 * P : (t + count) * 2 * P]
@@ -174,7 +180,8 @@ def tile_attend_gex_sig_wx_kernel(tc, xT, dyT, hT, ts, wm, offs, out_0, out_1):
 
         def dx_block(b, k, tag, after=None, copy=nc.scalar.copy, staged=None):
             acc = bank([P, N], tag)
-            product(acc[:], wm_mx[b], k, dzf[b], slice(0, N))
+            for cols in halves if (b, k) == (0, 0) else [slice(0, N)]:
+                product(acc[:, cols], wm_mx[b], k, dzf[b], cols)
             if staged is None:
                 staged = sb([P, N], F32, "staged%d_%d" % (b, k), after)[:]
             copy(
@@ -201,14 +208,16 @@ def tile_attend_gex_sig_wx_kernel(tc, xT, dyT, hT, ts, wm, offs, out_0, out_1):
         weigh(1, 0, first_pair, "h3")
         x_pool = [load(x_rows[k], [P, T], "x_pool%d" % k, "h%d" % k) for k in range(2)]
         x_late = sb([P, 2, T], F32, "x_late")
-        for e in range(2):
-            nc.sync.dma_start(x_late[:, e, :], x_rows[2 + e])
+        nc.sync.dma_start(x_late[:], xT[2 * P :, :].rearrange("(m e) c -> m e c", e=2))
 
         wm_bf = [sb([P, D * PACK], BF16, "wm_bf0")]
         feat = [sb([P, HALF * PACK], BF16, "feat0_%d" % half, (None, "dy0")[half]) for half in range(2)]
         weigh(0, 1, fwd, None)
         for half in range(2):
             features(0, half, feat[half][:])
+        for half, tag in enumerate(("u1", "l0")):
+            for j in (2, 3):
+                turn(1, j, half, tag)
         interleave(wm_bf[0][:], wm_raw[0][:])
         quantize(dzf[0], halves[0], feat[0][:], E5M2)
         quantize(wm_mx[0], slice(0, D), wm_bf[0][:], E4M3)
@@ -221,7 +230,7 @@ def tile_attend_gex_sig_wx_kernel(tc, xT, dyT, hT, ts, wm, offs, out_0, out_1):
         for half in range(2):
             features(1, half, feat1[:, half * HALF * PACK : (half + 1) * HALF * PACK])
         scatter_vector(0, 0, staged)
-        dzf[1] = (sb([P, N], U32, "dzf1_late", "staged0_0"), dzf[1][1])
+        dzf.append((sb([P, N], U32, "dzf1_codes", "staged0_0"), sb([P, N], U8, "dzf1_scales")))
         quantize(wm_mx[1], slice(0, D), wm_bf[1][:], E4M3)
         quantize(dzf[1], slice(0, N), feat1[:], E5M2)
 
@@ -279,12 +288,12 @@ def tile_attend_gex_sig_wx_kernel(tc, xT, dyT, hT, ts, wm, offs, out_0, out_1):
                     nc.sync.dma_start(out_0[b, k * P : (k + 1) * P, :], gw[:, 2 * b + i, :])
 
         by_vector = nc.vector.tensor_copy
-        scatter_vector(0, 1, dx_block(0, 1, "u1", "wm_raw1"))
+        scatter_vector(0, 1, dx_block(0, 1, "u2", "wm_raw1"))
         x_gather(0)
         x_gather(1)
         staged = sb([P, 2, N], F32, "staged_pair", "x_pool1")
         for k in range(2):
-            scatter_vector(1, k, dx_block(1, k, "u%d" % (2 + k), staged=staged[:, k, :]))
+            scatter_vector(1, k, dx_block(1, k, ("u3", "u0")[k], staged=staged[:, k, :]))
             store_window(k)
         x_slot = x_turned(0, ("l0", "l1"))
         x_pairs = sb([P, T, 2], BF16, "x_pairs", "x_pool0")
@@ -313,8 +322,8 @@ def tile_attend_gex_sig_wx_kernel(tc, xT, dyT, hT, ts, wm, offs, out_0, out_1):
             for t in range(PACK):
                 nc.tensor.transpose(turned[:, t, :], words[:].bitcast(F32)[:, b * N + t : (b + 1) * N : PACK], ident[:])
             nc.scalar.copy(
-                x_slot[:, b * HALF * PACK : (b + 1) * HALF * PACK].rearrange("p (e d t) -> p e d t", e=2, t=PACK),
-                turned[:].rearrange("p t d -> p (t d)").bitcast(BF16).rearrange("p (t d e) -> p e d t", t=PACK, e=2),
+                x_slot[:, b * HALF * PACK : (b + 1) * HALF * PACK].rearrange("p (d e t) -> p d e t", e=2, t=PACK),
+                turned[:].rearrange("p t d -> p (t d)").bitcast(BF16).rearrange("p (t d e) -> p d e t", t=PACK, e=2),
             )
         x_mx.append(x_operand(1, x_slot))
         scatter_vector(1, 2, dx_block(1, 2, "u1"))

@@ -88,7 +88,10 @@ def tile_attend_gex_sig_wx_kernel(tc, xT, dyT, hT, ts, wm, offs, out_0, out_1):
             if j == 0:
                 nc.sync.dma_start(offsets[:], offs)
             dy_pool.append(load(dy_rows[j], [P, T], "dy%d" % j))
-        wm_raw = [load(wm[b].rearrange("(m j) d -> m j d", j=PACK), [P, PACK, D], "wm_raw%d" % b) for b in range(B)]
+        wm_rows = [wm[b].rearrange("(m j) d -> m j d", j=PACK) for b in range(B)]
+        wm_raw = [load(wm_rows[0], [P, PACK, D], "wm_raw0")]
+        x_pool = [load(x_rows[0], [P, T], "x_pool0")]
+        wm_raw.append(load(wm_rows[1], [P, PACK, D], "wm_raw1"))
 
         windows = [sb([P, T], F32, "window%d" % k) for k in range(PACK)]
         for k in range(PACK):
@@ -206,12 +209,21 @@ def tile_attend_gex_sig_wx_kernel(tc, xT, dyT, hT, ts, wm, offs, out_0, out_1):
         for b in range(B):
             grad_plane(b, LAST, "slope0_0")
         weigh(1, 0, first_pair, "h3")
-        x_pool = [load(x_rows[k], [P, T], "x_pool%d" % k, "h%d" % k) for k in range(2)]
+        x_pool.append(load(x_rows[1], [P, T], "x_pool1", "h1"))
         x_late = sb([P, 2, T], F32, "x_late")
         nc.sync.dma_start(x_late[:], xT[2 * P :, :].rearrange("(m e) c -> m e c", e=2))
 
+        x_g = {}
+
+        def x_gather(k):
+            both = sb([P, B * N], BF16, "x_g%d" % k)
+            nc.scalar.activation(both[:], x_pool[k][:].indirect(offsets[:]), COPY)
+            for b in range(B):
+                x_g[k, b] = both[:, b * N : (b + 1) * N]
+
         wm_bf = [sb([P, D * PACK], BF16, "wm_bf0")]
-        feat = [sb([P, HALF * PACK], BF16, "feat0_%d" % half, (None, "dy0")[half]) for half in range(2)]
+        block = N * WIDTH[F32]
+        feat = [sb([P, HALF * PACK], BF16, "feat0_0"), sb([P, HALF * PACK], BF16, "feat0_1", "dy0", block)]
         weigh(0, 1, fwd, None)
         for half in range(2):
             features(0, half, feat[half][:])
@@ -222,8 +234,19 @@ def tile_attend_gex_sig_wx_kernel(tc, xT, dyT, hT, ts, wm, offs, out_0, out_1):
         quantize(dzf[0], halves[0], feat[0][:], E5M2)
         quantize(wm_mx[0], slice(0, D), wm_bf[0][:], E4M3)
         quantize(dzf[0], halves[1], feat[1][:], E5M2)
-        weigh(1, 1, fwd, "feat0_0")
-        wm_bf.append(sb([P, D * PACK], BF16, "wm_bf1", "dy0"))
+        x_gather(0)
+        weigh(1, 1, fwd, "x_pool0")
+
+        def weave(slots, b, u):
+            nc.gpsimd.tensor_scalar(
+                slots.rearrange("p (c t) -> p c t", t=PACK),
+                dz_part(b, u, 0, PACK).rearrange("p (t c) -> p c t", t=PACK),
+                1.0, 0.0, MULT, ADD,
+            )
+
+        early = sb([P, HALF * PACK], BF16, "dz_slots_early", "dy0", ALIGN)
+        weave(early[:], 0, 0)
+        wm_bf.append(sb([P, D * PACK], BF16, "wm_bf1", "dy0", 2 * block - ALIGN))
         nc.gpsimd.tensor_copy(wm_bf[1][:].rearrange("p (c j) -> p c j", j=PACK), wm_raw[1][:].rearrange("p j c -> p c j"))
         staged = dx_block(0, 0, "u0", None, nc.vector.tensor_copy)
         feat1 = sb([P, N * PACK], BF16, "feat1", "dy2")
@@ -234,26 +257,9 @@ def tile_attend_gex_sig_wx_kernel(tc, xT, dyT, hT, ts, wm, offs, out_0, out_1):
         quantize(wm_mx[1], slice(0, D), wm_bf[1][:], E4M3)
         quantize(dzf[1], slice(0, N), feat1[:], E5M2)
 
-        def weave(slots, b, u):
-            nc.gpsimd.tensor_scalar(
-                slots.rearrange("p (c t) -> p c t", t=PACK),
-                dz_part(b, u, 0, PACK).rearrange("p (t c) -> p c t", t=PACK),
-                1.0, 0.0, MULT, ADD,
-            )
-
-        early = sb([P, HALF * PACK], BF16, "dz_slots_early", "wm_raw1", N * WIDTH[F32])
-        weave(early[:], 0, 0)
         later = sb([P, 3, HALF * PACK], BF16, "dz_slots", "dy2")
         for i, (b, u) in enumerate(((0, 1), (1, 0), (1, 1))):
             weave(later[:, i, :], b, u)
-
-        x_g = {}
-
-        def x_gather(k):
-            both = sb([P, B * N], BF16, "x_g%d" % k)
-            nc.scalar.activation(both[:], x_pool[k][:].indirect(offsets[:]), COPY)
-            for b in range(B):
-                x_g[k, b] = both[:, b * N : (b + 1) * N]
 
         def x_turned(pair, tags):
             x_slot = sb([P, N * PACK], BF16, "x_slot%d" % pair)
@@ -289,7 +295,6 @@ def tile_attend_gex_sig_wx_kernel(tc, xT, dyT, hT, ts, wm, offs, out_0, out_1):
 
         by_vector = nc.vector.tensor_copy
         scatter_vector(0, 1, dx_block(0, 1, "u2", "wm_raw1"))
-        x_gather(0)
         x_gather(1)
         staged = sb([P, 2, N], F32, "staged_pair", "x_pool1")
         for k in range(2):

@@ -20,15 +20,15 @@ COPY = mybir.ActivationFunctionType.Copy
 
 P = 128
 PACK = 4
+LAST = PACK - 1
 HALF = N // 2
 GROUP = 16
 ALIGN = 64
 WIDTH = {F32: 4, BF16: 2, U32: 4, U8: 1}
+BLOCK = N * WIDTH[F32]
 BANKS = ["l0", "l1", "l2", "l3", "u0", "u1", "u2", "u3"]
-BANK_BYTES = 2048
 PIECE = 384
 TS_ROW = P - 1
-LAST = PACK - 1
 
 
 def tile_attend_gex_sig_wx_kernel(tc, xT, dyT, hT, ts, wm, offs, out_0, out_1):
@@ -37,7 +37,6 @@ def tile_attend_gex_sig_wx_kernel(tc, xT, dyT, hT, ts, wm, offs, out_0, out_1):
         lists = ctx.enter_context(tc.tile_pool(name="lists", bufs=1))
         keep = ctx.enter_context(tc.tile_pool(name="keep", bufs=1))
         psum = ctx.enter_context(tc.psum_pool(name="psum", bufs=1))
-
 
         place = {}
         free = [0]
@@ -51,12 +50,12 @@ def tile_attend_gex_sig_wx_kernel(tc, xT, dyT, hT, ts, wm, offs, out_0, out_1):
                 place[name] = place[after] + skip
             return keep.tile(shape, dtype, name=name, tag=name, align_bytes=ALIGN, offset=place[name])
 
-        banks = []
+        tenants = []
 
         def bank(shape, tag):
-            banks.append(tag)
-            name = "bank%d_%s" % (len(banks), tag)
-            return psum.tile(shape, F32, name=name, tag=name, offset=BANKS.index(tag) * BANK_BYTES)
+            tenants.append(tag)
+            name = "bank%d_%s" % (len(tenants), tag)
+            return psum.tile(shape, F32, name=name, tag=name, offset=BANKS.index(tag) * BLOCK)
 
         offsets = lists.tile([P, B * N // GROUP], U16, name="offsets")
 
@@ -81,7 +80,7 @@ def tile_attend_gex_sig_wx_kernel(tc, xT, dyT, hT, ts, wm, offs, out_0, out_1):
 
         h_rows = hT.rearrange("(m j) c -> j m c", j=PACK)
         dy_rows = dyT.rearrange("(m j) c -> j m c", j=PACK)
-        x_rows = xT.rearrange("(k m) c -> k m c", m=P)
+        x_rows = xT.rearrange("(k d) c -> k d c", d=P)
         h_pool, dy_pool = [], []
         for j in range(PACK):
             h_pool.append(load(h_rows[j], [P, T], "h%d" % j))
@@ -101,11 +100,11 @@ def tile_attend_gex_sig_wx_kernel(tc, xT, dyT, hT, ts, wm, offs, out_0, out_1):
         nc.vector.tensor_copy(ts_g[:], ts_pool[:].indirect(offsets[:]))
         minus_ts = []
         for b in range(B):
-            turned = bank([P, PACK, P], "l%d" % b)
+            ts_bank = bank([P, PACK, P], "l%d" % b)
             for t in range(PACK):
-                nc.tensor.transpose(turned[:, t, :], ts_g[:, b * N + t : (b + 1) * N : PACK], ident[:])
+                nc.tensor.transpose(ts_bank[:, t, :], ts_g[:, b * N + t : (b + 1) * N : PACK], ident[:])
             minus_ts.append(sb([P, PACK], F32, "minus_ts%d" % b))
-            nc.vector.tensor_scalar_mul(minus_ts[b][:], turned[:, :, TS_ROW], -1.0)
+            nc.vector.tensor_scalar_mul(minus_ts[b][:], ts_bank[:, :, TS_ROW], -1.0)
 
         def mx_tiles(width, name):
             return sb([P, width], U32, name + "_codes"), sb([P, width], U8, name + "_scales")
@@ -113,21 +112,15 @@ def tile_attend_gex_sig_wx_kernel(tc, xT, dyT, hT, ts, wm, offs, out_0, out_1):
         def quantize(mx, cols, src, fmt):
             nc.vector.quantize_mx(out=mx[0][:, cols].bitcast(fmt), scales=mx[1][:, cols], in_=src)
 
-        def product(acc, left, e, right, cols):
+        def product(acc, left, part, right, cols):
             nc.tensor.matmul_mx(
                 out=acc,
-                lhsT=left[0][:, e * P : (e + 1) * P].bitcast(E4M3),
-                lhsT_scale=left[1][:, e * P : (e + 1) * P],
+                lhsT=left[0][:, part * P : (part + 1) * P].bitcast(E4M3),
+                lhsT_scale=left[1][:, part * P : (part + 1) * P],
                 rhs=right[0][:, cols].bitcast(E5M2),
                 rhs_scale=right[1][:, cols],
                 start=True,
                 stop=True,
-            )
-
-        def interleave(dst, planes, copy=nc.vector.tensor_copy):
-            copy(
-                dst.rearrange("p (a c j) -> p a j c", c=PACK, j=PACK),
-                planes.rearrange("p j (a c) -> p a j c", c=PACK),
             )
 
         halves = [slice(0, HALF), slice(HALF, N)]
@@ -143,9 +136,8 @@ def tile_attend_gex_sig_wx_kernel(tc, xT, dyT, hT, ts, wm, offs, out_0, out_1):
             nc.scalar.activation(h_g[:], h_pool[j][:].indirect(entries(b * N, N)), COPY)
             slope = sb([P, N], F32, "slope%d_%d" % (b, j), slope_after)
             nc.vector.scalar_tensor_tensor(slope[:], h_g[:], minus_one[:], h_g[:], ADD, MULT)
-            grad = sb([P, N], F32, *reuse("grad%d_%%d" % b, j, j % 2))
-            nc.vector.tensor_tensor(grad[:], dy_pool[j][:].indirect(entries(b * N, N)), slope[:], MULT)
-            grads[b, j] = grad
+            grads[b, j] = sb([P, N], F32, *reuse("grad%d_%%d" % b, j, j % 2))
+            nc.vector.tensor_tensor(grads[b, j][:], dy_pool[j][:].indirect(entries(b * N, N)), slope[:], MULT)
             if b == 0 or j < 2:
                 for half in range(2):
                     turn(b, j, half, "%s%d" % ("lu"[j // 2], 2 * b + half))
@@ -181,107 +173,44 @@ def tile_attend_gex_sig_wx_kernel(tc, xT, dyT, hT, ts, wm, offs, out_0, out_1):
                 back[b, half][:].rearrange("p i u s -> p s i u"),
             )
 
-        def dx_block(b, k, tag, after=None, copy=nc.scalar.copy, staged=None):
-            acc = bank([P, N], tag)
-            for cols in halves if (b, k) == (0, 0) else [slice(0, N)]:
-                product(acc[:, cols], wm_mx[b], k, dzf[b], cols)
-            if staged is None:
-                staged = sb([P, N], F32, "staged%d_%d" % (b, k), after)[:]
-            copy(
-                staged.rearrange("p (s h i) -> p s h i", h=2, i=2),
-                acc[:].rearrange("p (h s i) -> p s h i", h=2, i=2),
-            )
-            return staged
-
-        def store_window(k):
-            nc.sync.dma_start(out_1[k * P : (k + 1) * P, :], windows[k][:])
-
-        def scatter_vector(b, k, staged):
-            nc.vector.tensor_copy(windows[k][:].indirect(entries(b * N, N)), staged)
-
-        for j in range(2):
-            for b in range(B):
-                grad_plane(b, j, "slope%d_0" % b if j else None)
-        first_pair = dict(fwd)
-        for b in range(B):
-            grad_plane(b, 2, "slope%d_0" % b)
-        weigh(0, 0, first_pair, "h2")
-        for b in range(B):
-            grad_plane(b, LAST, "slope0_0")
-        weigh(1, 0, first_pair, "h3")
-        x_pool.append(load(x_rows[1], [P, T], "x_pool1", "h1"))
-        x_late = sb([P, 2, T], F32, "x_late")
-        nc.sync.dma_start(x_late[:], xT[2 * P :, :].rearrange("(m e) c -> m e c", e=2))
-
-        x_g = {}
-
-        def x_gather(k):
-            both = sb([P, B * N], BF16, "x_g%d" % k)
-            nc.scalar.activation(both[:], x_pool[k][:].indirect(offsets[:]), COPY)
-            for b in range(B):
-                x_g[k, b] = both[:, b * N : (b + 1) * N]
-
-        wm_bf = [sb([P, D * PACK], BF16, "wm_bf0")]
-        block = N * WIDTH[F32]
-        feat = [sb([P, HALF * PACK], BF16, "feat0_0"), sb([P, HALF * PACK], BF16, "feat0_1", "dy0", block)]
-        weigh(0, 1, fwd, None)
-        for half in range(2):
-            features(0, half, feat[half][:])
-        for half, tag in enumerate(("u1", "l0")):
-            for j in (2, 3):
-                turn(1, j, half, tag)
-        interleave(wm_bf[0][:], wm_raw[0][:])
-        quantize(dzf[0], halves[0], feat[0][:], E5M2)
-        quantize(wm_mx[0], slice(0, D), wm_bf[0][:], E4M3)
-        quantize(dzf[0], halves[1], feat[1][:], E5M2)
-        x_gather(0)
-        weigh(1, 1, fwd, "x_pool0")
-
         def weave(slots, b, u):
             nc.gpsimd.tensor_scalar(
                 slots.rearrange("p (c t) -> p c t", t=PACK),
                 dz_part(b, u, 0, PACK).rearrange("p (t c) -> p c t", t=PACK),
-                1.0, 0.0, MULT, ADD,
+                1.0,
+                0.0,
+                MULT,
+                ADD,
             )
 
-        early = sb([P, HALF * PACK], BF16, "dz_slots_early", "dy0", ALIGN)
-        weave(early[:], 0, 0)
-        wm_bf.append(sb([P, D * PACK], BF16, "wm_bf1", "dy0", 2 * block - ALIGN))
-        nc.gpsimd.tensor_copy(wm_bf[1][:].rearrange("p (c j) -> p c j", j=PACK), wm_raw[1][:].rearrange("p j c -> p c j"))
-        staged = dx_block(0, 0, "u0", None, nc.vector.tensor_copy)
-        feat1 = sb([P, N * PACK], BF16, "feat1", "dy2")
-        for half in range(2):
-            features(1, half, feat1[:, half * HALF * PACK : (half + 1) * HALF * PACK])
-        scatter_vector(0, 0, staged)
-        dzf.append((sb([P, N], U32, "dzf1_codes", "staged0_0"), sb([P, N], U8, "dzf1_scales")))
-        quantize(wm_mx[1], slice(0, D), wm_bf[1][:], E4M3)
-        quantize(dzf[1], slice(0, N), feat1[:], E5M2)
+        def dx_block(b, k, tag, staged, copy=nc.scalar.copy, parts=(slice(0, N),)):
+            acc = bank([P, N], tag)
+            for cols in parts:
+                product(acc[:, cols], wm_mx[b], k, dzf[b], cols)
+            copy(
+                staged.rearrange("p (s h i) -> p s h i", h=2, i=2),
+                acc[:].rearrange("p (h s i) -> p s h i", h=2, i=2),
+            )
 
-        later = sb([P, 3, HALF * PACK], BF16, "dz_slots", "dy2")
-        for i, (b, u) in enumerate(((0, 1), (1, 0), (1, 1))):
-            weave(later[:, i, :], b, u)
+        def scatter_vector(b, k, staged):
+            nc.vector.tensor_copy(windows[k][:].indirect(entries(b * N, N)), staged)
 
-        def x_turned(pair, tags):
-            x_slot = sb([P, N * PACK], BF16, "x_slot%d" % pair)
-            for b in range(B):
-                turned = bank([P, 2, 2, P], tags[b])
-                for i in range(2):
-                    words = x_g[2 * pair + i, b].bitcast(F32)
-                    for v in range(2):
-                        nc.tensor.transpose(turned[:, i, v, :], words[:, v::2], ident[:])
-                nc.scalar.copy(
-                    x_slot[:].bitcast(F32)[:, b * N : (b + 1) * N].rearrange("p (i d v) -> p i d v", i=2, v=2),
-                    turned[:].rearrange("p i v d -> p i d v"),
-                )
-            return x_slot
+        def store_window(queue, k):
+            queue.dma_start(out_1[k * P : (k + 1) * P, :], windows[k][:])
 
-        def x_operand(pair, x_slot, after=None, skip=0):
-            mx = sb([P, N], U32, "x%d_codes" % pair, after, skip), sb([P, N], U8, "x%d_scales" % pair)
+        x_g = {}
+
+        def x_gather(k):
+            x_g[k] = sb([P, B * N], BF16, "x_g%d" % k)
+            nc.scalar.activation(x_g[k][:], x_pool[k][:].indirect(offsets[:]), COPY)
+
+        def x_operand(name, x_slot, after=None, skip=0):
+            mx = sb([P, N], U32, name + "_codes"), sb([P, N], U8, name + "_scales", after, skip)
             quantize(mx, slice(0, N), x_slot[:], E4M3)
             return mx
 
-        def gw_blocks(pair, x_mx, tags, after):
-            gw = sb([P, PACK, DV], F32, "gw%d" % pair, after)
+        def gw_blocks(first, x_mx, tags, after):
+            gw = sb([P, PACK, DV], F32, "gw%d" % first, after)
             for b in range(B):
                 for i in range(2):
                     acc = bank([P, DV], tags[2 * b + i])
@@ -290,48 +219,125 @@ def tile_attend_gex_sig_wx_kernel(tc, xT, dyT, hT, ts, wm, offs, out_0, out_1):
                         gw[:, 2 * b + i, :].rearrange("p (m u e) -> p m u e", u=2, e=2),
                         acc[:].rearrange("p (u m e) -> p m u e", u=2, e=2),
                     )
-                    k = 2 * pair + i
+                    k = first + i
                     nc.sync.dma_start(out_0[b, k * P : (k + 1) * P, :], gw[:, 2 * b + i, :])
 
-        by_vector = nc.vector.tensor_copy
-        scatter_vector(0, 1, dx_block(0, 1, "u2", "wm_raw1"))
-        x_gather(1)
-        staged = sb([P, 2, N], F32, "staged_pair", "x_pool1")
-        for k in range(2):
-            scatter_vector(1, k, dx_block(1, k, ("u3", "u0")[k], staged=staged[:, k, :]))
-            store_window(k)
-        x_slot = x_turned(0, ("l0", "l1"))
-        x_pairs = sb([P, T, 2], BF16, "x_pairs", "x_pool0")
-        nc.gpsimd.tensor_copy(x_pairs[:], x_late[:].rearrange("p e c -> p c e"))
-        words = sb([P, B * N], U32, "x_words", "staged_pair", 2 * N * WIDTH[F32])
-        nc.vector.tensor_copy(words[:], x_pairs[:].rearrange("p c e -> p (c e)").bitcast(U32).indirect(offsets[:]))
-        quarter = N * WIDTH[F32]
-        dzs = [(sb([P, DV], U32, "dzs%d_codes" % b, "x_late", b * quarter), sb([P, DV], U8, "dzs%d_scales" % b)) for b in range(B)]
-        quantize(dzs[0], halves[0], early[:], E5M2)
-        quantize(dzs[0], halves[1], later[:, 0, :], E5M2)
-        quantize(dzs[1], slice(0, DV), later[:, 1:, :].rearrange("p u c -> p (u c)"), E5M2)
-        x_mx = [x_operand(0, x_slot, "x_late", 2 * quarter)]
-
-        staged = sb([P, B * N], F32, "staged_last", "dy1")
+        for j in range(2):
+            for b in range(B):
+                grad_plane(b, j, "slope%d_0" % b if j else None)
+        low_planes = dict(fwd)
         for b in range(B):
-            dx_block(b, LAST, "l%d" % b, staged=staged[:, b * N : (b + 1) * N])
+            grad_plane(b, 2, "slope%d_0" % b)
+        weigh(0, 0, low_planes, "h2")
+        for b in range(B):
+            grad_plane(b, LAST, "slope0_0")
+        weigh(1, 0, low_planes, "h3")
+        x_pool.append(load(x_rows[1], [P, T], "x_pool1", "h1"))
+        x_late = sb([P, 2, T], F32, "x_late")
+        nc.sync.dma_start(x_late[:], xT[2 * P :, :].rearrange("(d e) c -> d e c", e=2))
+
+        wm_bf0 = sb([P, D * PACK], BF16, "wm_bf0")
+        feat0 = [sb([P, HALF * PACK], BF16, "feat0_0"), sb([P, HALF * PACK], BF16, "feat0_1", "dy0", BLOCK)]
+        weigh(0, 1, fwd, None)
+        for half in range(2):
+            features(0, half, feat0[half][:])
+        for half, tag in enumerate(("u1", "l0")):
+            for j in (2, 3):
+                turn(1, j, half, tag)
+        nc.vector.tensor_copy(
+            wm_bf0[:].rearrange("p (a c j) -> p a j c", c=PACK, j=PACK),
+            wm_raw[0][:].rearrange("p j (a c) -> p a j c", c=PACK),
+        )
+        quantize(dzf[0], halves[0], feat0[0][:], E5M2)
+        quantize(wm_mx[0], slice(0, D), wm_bf0[:], E4M3)
+        quantize(dzf[0], halves[1], feat0[1][:], E5M2)
+        x_gather(0)
+        weigh(1, 1, fwd, "x_pool0")
+
+        wm_bf1 = sb([P, D * PACK], BF16, "wm_bf1", "dy0", 2 * BLOCK - ALIGN)
+        nc.gpsimd.tensor_copy(wm_bf1[:].rearrange("p (d j) -> p d j", j=PACK), wm_raw[1][:].rearrange("p j d -> p d j"))
+
+        staged0_0 = sb([P, N], F32, "staged0_0")
+        dx_block(0, 0, "u0", staged0_0[:], nc.vector.tensor_copy, halves)
+        feat1 = sb([P, N * PACK], BF16, "feat1", "dy2")
+        for half in range(2):
+            features(1, half, feat1[:, half * HALF * PACK : (half + 1) * HALF * PACK])
+        scatter_vector(0, 0, staged0_0[:])
+        dzf.append((sb([P, N], U32, "dzf1_codes", "staged0_0"), sb([P, N], U8, "dzf1_scales")))
+        quantize(wm_mx[1], slice(0, D), wm_bf1[:], E4M3)
+        quantize(dzf[1], slice(0, N), feat1[:], E5M2)
+
+        slots_first = sb([P, HALF * PACK], BF16, "slots_first", "feat1")
+        weave(slots_first[:], 0, 0)
+        x_pairs = sb([P, T, 2], BF16, "x_pairs", "h0")
+        nc.gpsimd.tensor_copy(x_pairs[:], x_late[:].rearrange("p e c -> p c e"))
+        slots_rest = sb([P, 3, HALF * PACK], BF16, "slots_rest", "x_late")
+        for i, (b, u) in enumerate(((0, 1), (1, 0), (1, 1))):
+            weave(slots_rest[:, i, :], b, u)
+
+        staged0_1 = sb([P, N], F32, "staged0_1", "wm_raw1")
+        dx_block(0, 1, "u2", staged0_1[:])
+        scatter_vector(0, 1, staged0_1[:])
+        x_gather(1)
+        staged1_low = sb([P, 2, N], F32, "staged1_low", "x_pool1")
+        for k, tag in enumerate(("u3", "u0")):
+            dx_block(1, k, tag, staged1_low[:, k, :])
+            scatter_vector(1, k, staged1_low[:, k, :])
+            store_window(nc.sync, k)
+
+        x_slot_low = sb([P, N * PACK], BF16, "x_slot_low")
+        for b in range(B):
+            slot_pairs = bank([P, 2, 2, P], "l%d" % b)
+            for k in range(2):
+                for v in range(2):
+                    nc.tensor.transpose(
+                        slot_pairs[:, k, v, :], x_g[k][:, b * N : (b + 1) * N].bitcast(F32)[:, v::2], ident[:]
+                    )
+            nc.scalar.copy(
+                x_slot_low[:].bitcast(F32)[:, b * N : (b + 1) * N].rearrange("p (k d v) -> p k d v", k=2, v=2),
+                slot_pairs[:].rearrange("p k v d -> p k d v"),
+            )
+
+        pairs_g = sb([P, B * N], U32, "pairs_g", "x_pool1", 2 * BLOCK)
+        nc.vector.tensor_copy(pairs_g[:], x_pairs[:].rearrange("p c e -> p (c e)").bitcast(U32).indirect(offsets[:]))
+        dzs = [
+            (sb([P, DV], U32, "dzs%d_codes" % b), sb([P, DV], U8, "dzs%d_scales" % b, "dz_t1_1", ALIGN + b * DV))
+            for b in range(B)
+        ]
+        quantize(dzs[0], halves[0], slots_first[:], E5M2)
+        quantize(dzs[0], halves[1], slots_rest[:, 0, :], E5M2)
+        quantize(dzs[1], slice(0, DV), slots_rest[:, 1:, :].rearrange("p u c -> p (u c)"), E5M2)
+        x_low = x_operand("x_low", x_slot_low, "dz_t1_1", ALIGN + 2 * DV)
+
+        staged_last = sb([P, B * N], F32, "staged_last", "dy1")
+        for b in range(B):
+            dx_block(b, LAST, "l%d" % b, staged_last[:, b * N : (b + 1) * N])
         for first in range(0, B * N, PIECE):
             count = min(PIECE, B * N - first)
-            nc.scalar.activation(windows[LAST][:].indirect(entries(first, count)), staged[:, first : first + count], COPY)
-        nc.scalar.dma_start(out_1[LAST * P :, :], windows[LAST][:])
-
-        scatter_vector(0, 2, dx_block(0, 2, "l2", staged=sb([P, N], F32, "staged0_2", "x_pool0", 3 * quarter)[:]))
-        x_slot = sb([P, N * PACK], BF16, "x_slot1")
-        for b in range(B):
-            turned = bank([P, PACK, P], "u%d" % b)
-            for t in range(PACK):
-                nc.tensor.transpose(turned[:, t, :], words[:].bitcast(F32)[:, b * N + t : (b + 1) * N : PACK], ident[:])
-            nc.scalar.copy(
-                x_slot[:, b * HALF * PACK : (b + 1) * HALF * PACK].rearrange("p (d e t) -> p d e t", e=2, t=PACK),
-                turned[:].rearrange("p t d -> p (t d)").bitcast(BF16).rearrange("p (t d e) -> p d e t", t=PACK, e=2),
+            nc.scalar.activation(
+                windows[LAST][:].indirect(entries(first, count)), staged_last[:, first : first + count], COPY
             )
-        x_mx.append(x_operand(1, x_slot))
-        scatter_vector(1, 2, dx_block(1, 2, "u1"))
-        gw_blocks(0, x_mx[0], ("l3", "u2", "u3", "l0"), "staged_pair")
-        gw_blocks(1, x_mx[1], ("l1", "u0", "l3", "u2"), "dy1")
-        nc.scalar.dma_start(out_1[2 * P : 3 * P, :], windows[2][:])
+        store_window(nc.scalar, LAST)
+
+        staged0_2 = sb([P, N], F32, "staged0_2", "dz_t1_1", BLOCK - ALIGN)
+        dx_block(0, 2, "l2", staged0_2[:])
+        scatter_vector(0, 2, staged0_2[:])
+        x_slot_high = sb([P, N * PACK], BF16, "x_slot_high", "dz_t1_1", ALIGN - 2 * BLOCK)
+        for b in range(B):
+            feature_pairs = bank([P, PACK, P], "u%d" % b)
+            for t in range(PACK):
+                nc.tensor.transpose(
+                    feature_pairs[:, t, :], pairs_g[:].bitcast(F32)[:, b * N + t : (b + 1) * N : PACK], ident[:]
+                )
+            nc.scalar.copy(
+                x_slot_high[:, b * HALF * PACK : (b + 1) * HALF * PACK].rearrange("p (d e t) -> p d e t", e=2, t=PACK),
+                feature_pairs[:].rearrange("p t d -> p (t d)").bitcast(BF16).rearrange("p (t d e) -> p d e t", t=PACK, e=2),
+            )
+        x_high = x_operand("x_high", x_slot_high)
+        staged1_2 = sb([P, N], F32, "staged1_2")
+        dx_block(1, 2, "u1", staged1_2[:])
+        scatter_vector(1, 2, staged1_2[:])
+
+        gw_blocks(0, x_low, ("l3", "u2", "u3", "l0"), "x_pool1")
+        gw_blocks(2, x_high, ("l1", "u0", "l3", "u2"), "dy1")
+        store_window(nc.scalar, 2)

import math
from contextlib import ExitStack

import concourse.mybir as mybir
from concourse.masks import make_identity

B, N, T, D, DV = 2, 512, 2048, 512, 512
FLOPS = 2 * 2 * B * N * D * DV

F32 = mybir.dt.float32
BF16 = mybir.dt.bfloat16
U32 = mybir.dt.uint32
U16 = mybir.dt.uint16
U8 = mybir.dt.uint8
E4M3 = mybir.dt.float8_e4m3fn_x4
E5M2 = mybir.dt.float8_e5m2_x4
MULT = mybir.AluOpType.mult
ADD = mybir.AluOpType.add
COPY = mybir.ActivationFunctionType.Copy

P = 128
PACK = 4
LAST = PACK - 1
HALF = N // 2
GROUP = 16
ALIGN = 64
WIDTH = {F32: 4, BF16: 2, U32: 4, U8: 1}
BLOCK = N * WIDTH[F32]
BANKS = ["l0", "l1", "l2", "l3", "u0", "u1", "u2", "u3"]
PIECE = 384
TS_ROW = P - 1


def tile_attend_gex_sig_wx_kernel(tc, xT, dyT, hT, ts, wm, offs, out_0, out_1):
    nc = tc.nc
    with ExitStack() as ctx:
        lists = ctx.enter_context(tc.tile_pool(name="lists", bufs=1))
        keep = ctx.enter_context(tc.tile_pool(name="keep", bufs=1))
        psum = ctx.enter_context(tc.psum_pool(name="psum", bufs=1))

        place = {}
        free = [0]

        def sb(shape, dtype, name, after=None, skip=0):
            if after is None:
                place[name] = free[0]
                size = math.prod(shape[1:]) * WIDTH[dtype]
                free[0] = free[0] + -(-size // ALIGN) * ALIGN
            else:
                place[name] = place[after] + skip
            return keep.tile(shape, dtype, name=name, tag=name, align_bytes=ALIGN, offset=place[name])

        tenants = []

        def bank(shape, tag):
            tenants.append(tag)
            name = "bank%d_%s" % (len(tenants), tag)
            return psum.tile(shape, F32, name=name, tag=name, offset=BANKS.index(tag) * BLOCK)

        offsets = lists.tile([P, B * N // GROUP], U16, name="offsets")

        def entries(first, count):
            return offsets[:, first // GROUP : (first + count) // GROUP]

        ts_pool = sb([P, T], F32, "ts_pool")
        nc.scalar.dma_start(ts_pool[TS_ROW:, :], ts[TS_ROW:, :])
        nc.vector.memset(ts_pool[:TS_ROW, :].bitcast(U32), 0)

        ident = sb([P, P], F32, "ident")
        make_identity(nc, ident[:])
        one = sb([P, 1], F32, "one")
        nc.vector.memset(one[:], 1.0)
        minus_one = sb([P, 1], F32, "minus_one")
        nc.scalar.activation(minus_one[:], one[:], COPY, scale=-1.0)

        def load(rows, shape, name, after=None):
            raw = sb(shape, F32, name, after)
            nc.sync.dma_start(raw[:], rows)
            return raw

        h_rows = hT.rearrange("(m j) c -> j m c", j=PACK)
        dy_rows = dyT.rearrange("(m j) c -> j m c", j=PACK)
        x_rows = xT.rearrange("(k d) c -> k d c", d=P)
        h_pool, dy_pool = [], []
        for j in range(PACK):
            h_pool.append(load(h_rows[j], [P, T], "h%d" % j))
            if j == 0:
                nc.sync.dma_start(offsets[:], offs)
            dy_pool.append(load(dy_rows[j], [P, T], "dy%d" % j))
        wm_rows = [wm[b].rearrange("(m j) d -> m j d", j=PACK) for b in range(B)]
        wm_raw = [load(wm_rows[0], [P, PACK, D], "wm_raw0")]
        x_pool = [load(x_rows[0], [P, T], "x_pool0")]
        wm_raw.append(load(wm_rows[1], [P, PACK, D], "wm_raw1"))

        windows = [sb([P, T], F32, "window%d" % k) for k in range(PACK)]
        for k in range(PACK):
            nc.gpsimd.memset(windows[k][:], 0.0)

        ts_g = sb([P, B * N], F32, "ts_g")
        nc.vector.tensor_copy(ts_g[:], ts_pool[:].indirect(offsets[:]))
        minus_ts = []
        for b in range(B):
            ts_bank = bank([P, PACK, P], "l%d" % b)
            for t in range(PACK):
                nc.tensor.transpose(ts_bank[:, t, :], ts_g[:, b * N + t : (b + 1) * N : PACK], ident[:])
            minus_ts.append(sb([P, PACK], F32, "minus_ts%d" % b))
            nc.vector.tensor_scalar_mul(minus_ts[b][:], ts_bank[:, :, TS_ROW], -1.0)

        def mx_tiles(width, name):
            return sb([P, width], U32, name + "_codes"), sb([P, width], U8, name + "_scales")

        def quantize(mx, cols, src, fmt):
            nc.vector.quantize_mx(out=mx[0][:, cols].bitcast(fmt), scales=mx[1][:, cols], in_=src)

        def product(acc, left, part, right, cols):
            nc.tensor.matmul_mx(
                out=acc,
                lhsT=left[0][:, part * P : (part + 1) * P].bitcast(E4M3),
                lhsT_scale=left[1][:, part * P : (part + 1) * P],
                rhs=right[0][:, cols].bitcast(E5M2),
                rhs_scale=right[1][:, cols],
                start=True,
                stop=True,
            )

        halves = [slice(0, HALF), slice(HALF, N)]
        dzf = [mx_tiles(N, "dzf0")]
        wm_mx = [mx_tiles(D, "wm%d" % b) for b in range(B)]
        grads, fwd, back, dz_t = {}, {}, {}, {}

        def reuse(name, j, first):
            return (name % j, name % first if j != first else None)

        def grad_plane(b, j, slope_after):
            h_g = sb([P, N], F32, *reuse("h_g%d_%%d" % b, j, 0))
            nc.scalar.activation(h_g[:], h_pool[j][:].indirect(entries(b * N, N)), COPY)
            slope = sb([P, N], F32, "slope%d_%d" % (b, j), slope_after)
            nc.vector.scalar_tensor_tensor(slope[:], h_g[:], minus_one[:], h_g[:], ADD, MULT)
            grads[b, j] = sb([P, N], F32, *reuse("grad%d_%%d" % b, j, j % 2))
            nc.vector.tensor_tensor(grads[b, j][:], dy_pool[j][:].indirect(entries(b * N, N)), slope[:], MULT)
            if b == 0 or j < 2:
                for half in range(2):
                    turn(b, j, half, "%s%d" % ("lu"[j // 2], 2 * b + half))

        def turn(b, j, half, tag):
            if j % 2 == 0:
                fwd[b, half] = bank([P, 2, 2, P], tag)
            for i in range(2):
                nc.tensor.transpose(fwd[b, half][:, i, j % 2, :], grads[b, j][:, 2 * half + i :: PACK], ident[:])

        def dz_part(b, u, t, count=1):
            return dz_t[b, u][:, t * 2 * P : (t + count) * 2 * P]

        def weigh(b, u, turned, after):
            dz_t[b, u] = sb([P, PACK * 2 * P], BF16, "dz_t%d_%d" % (b, u), after)
            for half in range(2):
                for i in range(2):
                    t = 2 * half + i
                    nc.scalar.activation(
                        dz_part(b, u, t).rearrange("p (m e) -> p m e", e=2),
                        turned[b, half][:, i].rearrange("p e m -> p m e"),
                        COPY,
                        scale=minus_ts[b][:, t : t + 1],
                    )
                if u == 0:
                    back[b, half] = bank([P, 2, 2, P], "l%d" % (2 * b + half))
                for i in range(2):
                    nc.tensor.transpose(back[b, half][:, i, u, :], dz_part(b, u, 2 * half + i).bitcast(F32), ident[:])

        def features(b, half, feat):
            nc.scalar.copy(
                feat.bitcast(F32).rearrange("p (s i u) -> p s i u", i=2, u=2),
                back[b, half][:].rearrange("p i u s -> p s i u"),
            )

        def weave(slots, b, u):
            nc.gpsimd.tensor_scalar(
                slots.rearrange("p (c t) -> p c t", t=PACK),
                dz_part(b, u, 0, PACK).rearrange("p (t c) -> p c t", t=PACK),
                1.0,
                0.0,
                MULT,
                ADD,
            )

        def dx_block(b, k, tag, staged, copy=nc.scalar.copy, parts=(slice(0, N),)):
            acc = bank([P, N], tag)
            for cols in parts:
                product(acc[:, cols], wm_mx[b], k, dzf[b], cols)
            copy(
                staged.rearrange("p (s h i) -> p s h i", h=2, i=2),
                acc[:].rearrange("p (h s i) -> p s h i", h=2, i=2),
            )

        def scatter_vector(b, k, staged):
            nc.vector.tensor_copy(windows[k][:].indirect(entries(b * N, N)), staged)

        def store_window(queue, k):
            queue.dma_start(out_1[k * P : (k + 1) * P, :], windows[k][:])

        x_g = {}

        def x_gather(k):
            x_g[k] = sb([P, B * N], BF16, "x_g%d" % k)
            nc.scalar.activation(x_g[k][:], x_pool[k][:].indirect(offsets[:]), COPY)

        def x_operand(name, x_slot, after=None, skip=0):
            mx = sb([P, N], U32, name + "_codes"), sb([P, N], U8, name + "_scales", after, skip)
            quantize(mx, slice(0, N), x_slot[:], E4M3)
            return mx

        def gw_blocks(first, x_mx, tags, after):
            gw = sb([P, PACK, DV], F32, "gw%d" % first, after)
            for b in range(B):
                for i in range(2):
                    acc = bank([P, DV], tags[2 * b + i])
                    product(acc[:], x_mx, 2 * b + i, dzs[b], slice(0, DV))
                    nc.scalar.copy(
                        gw[:, 2 * b + i, :].rearrange("p (m u e) -> p m u e", u=2, e=2),
                        acc[:].rearrange("p (u m e) -> p m u e", u=2, e=2),
                    )
                    k = first + i
                    nc.sync.dma_start(out_0[b, k * P : (k + 1) * P, :], gw[:, 2 * b + i, :])

        for j in range(2):
            for b in range(B):
                grad_plane(b, j, "slope%d_0" % b if j else None)
        low_planes = dict(fwd)
        for b in range(B):
            grad_plane(b, 2, "slope%d_0" % b)
        weigh(0, 0, low_planes, "h2")
        for b in range(B):
            grad_plane(b, LAST, "slope0_0")
        weigh(1, 0, low_planes, "h3")
        x_pool.append(load(x_rows[1], [P, T], "x_pool1", "h1"))
        x_late = sb([P, 2, T], F32, "x_late")
        nc.sync.dma_start(x_late[:], xT[2 * P :, :].rearrange("(d e) c -> d e c", e=2))

        wm_bf0 = sb([P, D * PACK], BF16, "wm_bf0")
        feat0 = [sb([P, HALF * PACK], BF16, "feat0_0"), sb([P, HALF * PACK], BF16, "feat0_1", "dy0", BLOCK)]
        weigh(0, 1, fwd, None)
        for half in range(2):
            features(0, half, feat0[half][:])
        for half, tag in enumerate(("u1", "l0")):
            for j in (2, 3):
                turn(1, j, half, tag)
        nc.vector.tensor_copy(
            wm_bf0[:].rearrange("p (a c j) -> p a j c", c=PACK, j=PACK),
            wm_raw[0][:].rearrange("p j (a c) -> p a j c", c=PACK),
        )
        quantize(dzf[0], halves[0], feat0[0][:], E5M2)
        quantize(wm_mx[0], slice(0, D), wm_bf0[:], E4M3)
        quantize(dzf[0], halves[1], feat0[1][:], E5M2)
        x_gather(0)
        weigh(1, 1, fwd, "x_pool0")

        wm_bf1 = sb([P, D * PACK], BF16, "wm_bf1", "dy0", 2 * BLOCK - ALIGN)
        nc.gpsimd.tensor_copy(wm_bf1[:].rearrange("p (d j) -> p d j", j=PACK), wm_raw[1][:].rearrange("p j d -> p d j"))

        staged0_0 = sb([P, N], F32, "staged0_0")
        dx_block(0, 0, "u0", staged0_0[:], nc.vector.tensor_copy, halves)
        feat1 = sb([P, N * PACK], BF16, "feat1", "dy2")
        for half in range(2):
            features(1, half, feat1[:, half * HALF * PACK : (half + 1) * HALF * PACK])
        scatter_vector(0, 0, staged0_0[:])
        dzf.append((sb([P, N], U32, "dzf1_codes", "staged0_0"), sb([P, N], U8, "dzf1_scales")))
        quantize(wm_mx[1], slice(0, D), wm_bf1[:], E4M3)
        quantize(dzf[1], slice(0, N), feat1[:], E5M2)

        slots_first = sb([P, HALF * PACK], BF16, "slots_first", "feat1")
        weave(slots_first[:], 0, 0)
        x_pairs = sb([P, T, 2], BF16, "x_pairs", "h0")
        nc.gpsimd.tensor_copy(x_pairs[:], x_late[:].rearrange("p e c -> p c e"))
        slots_rest = sb([P, 3, HALF * PACK], BF16, "slots_rest", "x_late")
        for i, (b, u) in enumerate(((0, 1), (1, 0), (1, 1))):
            weave(slots_rest[:, i, :], b, u)

        staged0_1 = sb([P, N], F32, "staged0_1", "wm_raw1")
        dx_block(0, 1, "u2", staged0_1[:])
        scatter_vector(0, 1, staged0_1[:])
        x_gather(1)
        staged1_low = sb([P, 2, N], F32, "staged1_low", "x_pool1")
        for k, tag in enumerate(("u3", "u0")):
            dx_block(1, k, tag, staged1_low[:, k, :])
            scatter_vector(1, k, staged1_low[:, k, :])
            store_window(nc.sync, k)

        x_slot_low = sb([P, N * PACK], BF16, "x_slot_low")
        for b in range(B):
            slot_pairs = bank([P, 2, 2, P], "l%d" % b)
            for k in range(2):
                for v in range(2):
                    nc.tensor.transpose(
                        slot_pairs[:, k, v, :], x_g[k][:, b * N : (b + 1) * N].bitcast(F32)[:, v::2], ident[:]
                    )
            nc.scalar.copy(
                x_slot_low[:].bitcast(F32)[:, b * N : (b + 1) * N].rearrange("p (k d v) -> p k d v", k=2, v=2),
                slot_pairs[:].rearrange("p k v d -> p k d v"),
            )

        pairs_g = sb([P, B * N], U32, "pairs_g", "x_pool1", 2 * BLOCK)
        nc.vector.tensor_copy(pairs_g[:], x_pairs[:].rearrange("p c e -> p (c e)").bitcast(U32).indirect(offsets[:]))
        dzs = [
            (sb([P, DV], U32, "dzs%d_codes" % b), sb([P, DV], U8, "dzs%d_scales" % b, "dz_t1_1", ALIGN + b * DV))
            for b in range(B)
        ]
        quantize(dzs[0], halves[0], slots_first[:], E5M2)
        quantize(dzs[0], halves[1], slots_rest[:, 0, :], E5M2)
        quantize(dzs[1], slice(0, DV), slots_rest[:, 1:, :].rearrange("p u c -> p (u c)"), E5M2)
        x_low = x_operand("x_low", x_slot_low, "dz_t1_1", ALIGN + 2 * DV)

        staged_last = sb([P, B * N], F32, "staged_last", "dy1")
        for b in range(B):
            dx_block(b, LAST, "l%d" % b, staged_last[:, b * N : (b + 1) * N])
        for first in range(0, B * N, PIECE):
            count = min(PIECE, B * N - first)
            nc.scalar.activation(
                windows[LAST][:].indirect(entries(first, count)), staged_last[:, first : first + count], COPY
            )
        store_window(nc.scalar, LAST)

        staged0_2 = sb([P, N], F32, "staged0_2", "dz_t1_1", BLOCK - ALIGN)
        dx_block(0, 2, "l2", staged0_2[:])
        scatter_vector(0, 2, staged0_2[:])
        x_slot_high = sb([P, N * PACK], BF16, "x_slot_high", "dz_t1_1", ALIGN - 2 * BLOCK)
        for b in range(B):
            feature_pairs = bank([P, PACK, P], "u%d" % b)
            for t in range(PACK):
                nc.tensor.transpose(
                    feature_pairs[:, t, :], pairs_g[:].bitcast(F32)[:, b * N + t : (b + 1) * N : PACK], ident[:]
                )
            nc.scalar.copy(
                x_slot_high[:, b * HALF * PACK : (b + 1) * HALF * PACK].rearrange("p (d e t) -> p d e t", e=2, t=PACK),
                feature_pairs[:].rearrange("p t d -> p (t d)").bitcast(BF16).rearrange("p (t d e) -> p d e t", t=PACK, e=2),
            )
        x_high = x_operand("x_high", x_slot_high)
        staged1_2 = sb([P, N], F32, "staged1_2")
        dx_block(1, 2, "u1", staged1_2[:])
        scatter_vector(1, 2, staged1_2[:])

        gw_blocks(0, x_low, ("l3", "u2", "u3", "l0"), "x_pool1")
        gw_blocks(2, x_high, ("l1", "u0", "l3", "u2"), "dy1")
        store_window(nc.scalar, 2)
